import numpy as np, ml_dtypes
CORES = [40,41,42,43,44,45,46,47]
N = 8
BF = ml_dtypes.bfloat16
def gentries(a):
    return np.ascontiguousarray(a.reshape(8, 16, -1).transpose(0, 2, 1)).reshape(8, -1)
def gtable(e):
    e = np.asarray(e); return np.ascontiguousarray(e.reshape(8, -1, 16).transpose(0, 2, 1)).reshape(128, -1).astype(np.int32)
W, P, R, S, E, LM = 2048, 192, 3, 3, 1, 14
def pack(nb, x, v, z, th):
    return {"nb": np.ascontiguousarray(nb.reshape(N, 128, W)).astype(np.int32), "xd": np.ascontiguousarray(x.reshape(N, 128, W)).astype(np.float32).astype(BF),
            "pv": np.stack([gtable(a) for a in v]), "pz": np.ascontiguousarray(z.reshape(N, 128, P)).astype(np.float32).astype(BF), "th": np.repeat(th, 16, axis=1).astype(np.int32)}
def blur(rng, pat, sel, m):
    b = np.stack([pat[g][sel[:, g]] for g in range(8)], axis=1).transpose(0, 1, 3, 2)
    b = np.clip(b + rng.integers(-1, 2, b.shape) * (rng.random(b.shape) < 0.25), 0, 15)
    return np.where(np.arange(16)[:, None] < m[:, :, None, :], b, rng.integers(0, 16, b.shape))
def alike(rng, s, want):
    o = np.argsort(s, kind="stable"); n = np.bincount(s, minlength=8); b = np.add.accumulate(n) - n
    return o[np.minimum(b[want] + (rng.random(want.shape) * n[want]).astype(np.int64), len(s) - 1)]
def parts(rng):
    pat = rng.integers(0, 16, (8, 8, 16))
    s = np.where(rng.random((N, 8, W)) < 0.7, rng.integers(0, 8, (1, 8, W)), rng.integers(0, 8, (N, 8, W)))
    x = blur(rng, pat, s, rng.integers(0, 17, (N, 8, W)))
    sp = rng.integers(0, 8, (N, 8, P)); z = blur(rng, pat, sp, rng.integers(0, 17, (N, 8, P)))
    nb = rng.integers(0, W, (N, 8, 16, W)); v = rng.integers(0, W, (N, 8, P))
    for q in range(N):
        for g in range(8):
            w = alike(rng, s[q, g], np.broadcast_to(s[q, g], (16, W)))
            nb[q, g] = np.where(rng.random((16, W)) < 0.5, w, nb[q, g])
            v[q, g] = np.where(rng.random(P) < 0.6, alike(rng, s[q, g], sp[q, g]), v[q, g])
    th = np.stack([rng.integers(40, 91, (N, 8)), rng.integers(25, 76, (N, 8))], axis=-1)
    return nb, x, v, z, th
def setup_inputs(rng):
    return pack(*parts(rng))
def uneven(rng, shape, n):
    a = np.minimum((n * rng.random(shape) ** 3).astype(np.int64), n - 1)
    return np.where(rng.random(shape[:-1] + (1,)) < 0.5, a, n - 1 - a)
def setup_inputs_spread(rng):
    def digits(n):
        top = 1 << rng.integers(0, 5, (N, 8, 1, n)); a = np.minimum((rng.random((N, 8, 16, n)) * top).astype(np.int64), 15)
        return np.where(rng.random((N, 8, 1, n)) < 0.5, a, 15 - a)
    return pack(uneven(rng, (N, 8, 16, W), W), digits(W), uneven(rng, (N, 8, P), W), digits(P), rng.integers(0, 242, (N, 8, 2)))
def setup_inputs_ends(rng):
    def digits(n):
        return np.where(rng.random((N, 8, 1, n)) < 0.5, 15 * rng.integers(0, 2, (N, 8, 1, n)), 15 * rng.integers(0, 2, (N, 8, 16, n)))
    x = digits(W); x[..., 0] = 0; x[..., W - 1] = 15; x[:, 1:6:2, :, 0] = 15; x[:, 1:6:2, :, W - 1] = 0
    z = digits(P); z[..., 0] = 0; z[..., 1] = 15; z[..., P - 2] = 15; z[..., P - 1] = 0
    nb = np.where(rng.random((N, 8, 16, W)) < 0.25, rng.integers(0, W, (N, 8, 16, W)), (W - 1) * rng.integers(0, 2, (N, 8, 16, W)))
    nb[:, 7, :, W - 1] = W - 1
    v = np.where(rng.random((N, 8, P)) < 0.25, rng.integers(0, W, (N, 8, P)), (W - 1) * rng.integers(0, 2, (N, 8, P)))
    v[..., 0] = 0; v[..., 1] = W - 1; v[..., P - 2] = W - 1; v[..., P - 1] = W - 1
    pairs = np.array([[0, 0], [0, 241], [241, 0], [241, 241]])
    th = pairs[np.argsort(rng.random((N, 8)), axis=1) & 3]; th[N - 1] = pairs[np.array([0, 3, 2, 1, 0, 2, 3, 1])]; th[:, 2] = np.array([120, 121])
    return pack(nb, x, v, z, th)
def setup_inputs_corners(rng):
    M = P // 4; nb = np.zeros((N, 8, 16, W), np.int64); x = np.zeros((N, 8, 16, W), np.int64); v = np.zeros((N, 8, P), np.int64); z = np.zeros((N, 8, 16, P), np.int64)
    th = np.zeros((N, 8, 2), np.int64); th[..., 0] = 40; th[..., 1] = 24
    rows = np.arange(16)[:, None]
    for q in range(N):
        for g in range(8):
            zz = rng.integers(4, 12, 16)[:, None]; o = rng.permutation(W); place = o[:P]; cont = o[P:P + 16 * M].reshape(M, 16); good = o[P + 16 * M::2]; miss = o[P + 16 * M + 1::2]
            lw = rng.choice(np.array([0, 1, 2, 7, LM - 1, LM, LM + 1, 15, 16]), P); lv = np.minimum(lw, LM)[:M]; case = rng.permutation(np.arange(M) & 7)
            d = np.zeros(W, np.int64); d[good] = rng.choice(np.array([0, 1, 23]), len(good)); d[miss] = rng.choice(np.array([24, 24, 25, 39, 40]), len(miss))
            d[cont] = rng.choice(np.array([40, 40, 41, 54, 55, 56]), (M, 16)); j = np.flatnonzero(case == 0); d[cont[j, lv[j]]] = 39
            sign = 1 - 2 * rng.integers(0, 2, (16, W)); diff = (d >> 4) + (np.argsort(rng.random((16, W)), axis=0) < (d & 15))
            diff[:, place] = np.where(rows < lw, rng.integers(0, 2, (16, P)), np.where(rows == lw, 2, rng.integers(0, 5, (16, P))))
            x[q, g] = zz + sign * diff
            w = rng.random((16, W)); b = np.where(w < 0.15, np.arange(W), np.where(w < 0.25, 0, np.where(w < 0.35, W - 1, rng.integers(0, W, (16, W)))))
            b[:, place[:M]] = cont.T
            for e in range(E + 1): b[(lv + e)[:, None], cont] = rng.choice(miss, (M, 16))
            last = (lv + 15) & 15
            for c, e, k in ((1, 0, last), (2, 0, lv), (3, 1, last), (4, E, lv), (6, 0, last), (7, 0, 0 * lv + 15), (7, 0, 0 * lv)):
                j = np.flatnonzero(case == c); b[lv[j] + e, cont[j, k[j]]] = rng.choice(good, len(j))
            j = np.flatnonzero(case == 6); b[(lv[j] + 1)[:, None], cont[j]] = rng.choice(good, (len(j), 16))
            nb[q, g] = b
            pl = place.copy(); n = P - M; pl[M:] = np.where(rng.random(n) < 0.25, rng.choice(place[:M], n), pl[M:]); pl[P - 1] = W - 1; pl[P - 2] = 0
            t = np.repeat(zz, P, axis=1); t[:, M:] = np.where(rng.random(n) < 0.5, np.clip(zz + rng.integers(-3, 4, (16, n)), 0, 15), rng.integers(0, 16, (16, n)))
            r = rng.permutation(P); v[q, g] = pl[r]; z[q, g] = t[:, r]
    th[1, :, 0] = 0; th[N - 1, :4] = np.array([[0, 0], [0, 241], [241, 0], [241, 241]])
    return pack(nb, x, v, z, th)
def setup_inputs_crowd(rng):
    nb, x, v, z, th = parts(rng)
    v[:, 0] = rng.integers(0, W, (N, 1)); v[:, 1] = rng.integers(0, W - 1, (N, 1))
    for q in range(N): v[q, 1, rng.integers(0, P)] = W - 1
    v[:, 2] = rng.choice(np.array([0, 3, W // 2, W - 1]), (N, P)); v[:, 3] = np.repeat(v[:, 3, :P // 2], 2, axis=1)
    nb[:, 4, :15] = rng.integers(0, W, (N, 1, 1)); nb[:, 5] = nb[:, 5, :1]
    v[:, 6] = rng.integers(0, W, (N, 1)); z[:, 6] = z[:, 6, :, :1]; v[:, 7] = W - 1
    th[0, :, 0] = 0; th[1, :, 0] = 0; th[1, 7, 0] = 1
    x[1, 7, 15] = np.minimum(x[1, 7, 15], 14); z[1, 7, 15] = 15; j = rng.integers(0, P); u = rng.integers(0, W - 1)
    nb[1, 7, :, v[1, 7, j]] = u; z[1, 7, :, j] = x[1, 7, :, u]
    th[2, :7, 0] = 241; th[2, 7, 0] = 0
    return pack(nb, x, v, z, th)
def setup_inputs_calm(rng):
    M = P - P // 8; rows = np.arange(16)[:, None]
    nb = rng.integers(0, W, (N, 8, 16, W)); x = rng.integers(0, 16, (N, 8, 16, W))
    n = np.argsort(rng.random((8, W)), axis=1)[:, :(R + 1) * M].reshape(8, R + 1, M)
    th = np.zeros((N, 8, 2), np.int64); th[..., 0] = rng.integers(16, 33, (N, 8))
    z0 = np.clip(rng.integers(0, 16, (8, 16, M)) + rng.integers(-1, 2, (N, 8, 16, M)), 0, 15); z = z0
    at = np.where(rows < rng.integers(0, 17, (N, 8, 1, M)), np.clip(z + rng.integers(-1, 2, z.shape), 0, 15), rng.integers(0, 16, z.shape))
    o = rng.permutation(N); want = np.zeros((R - 1, N), np.int64)
    for t in range(R - 1): want[t, o] = (np.arange(N) + t) & 3
    want[0, o[0]] = 8 * P; want[0, o[1]] = 8 * P - 1
    weight = 1 + (np.arange(M) < P - M).astype(np.int64); a = np.zeros(N, np.int64)
    for t in range(R):
        if t > 0: z = np.roll(z, S, axis=0)
        near = (np.abs(at - z) <= 1).astype(np.int64)
        l = np.minimum(np.add.reduce(np.multiply.accumulate(near, axis=2), axis=2), LM)
        for q in range(N):
            for g in range(8):
                x[q, g][:, n[g, t]] = at[q, g]; nb[q, g][l[q, g], n[g, t]] = n[g, t + 1]
                if t < R - 1: nb[q, g][15, n[g, t]] = n[g, t + 1]
        fail = rng.random((N, 8, M)) < 0.4; over = np.where(rng.random((N, 8, M)) < 0.5, 0, rng.integers(0, 8, (N, 8, M)))
        if t < R - 1:
            over = 0 * over
            for q in range(N):
                k = int(want[t, q]); j = rng.permutation(8 * (2 * M - P))[:min(k, 8 * P - k)]
                fail[q] = k > 3; fail[q, j & 7, P - M + (j >> 3)] = k < 4
        h = th[..., 0][:, :, None] + (a & 15)[:, None, None]
        under = np.where(rng.random((N, 8, M)) < 0.5, 0, rng.integers(0, 16, (N, 8, M)))
        need = np.where(fail, h + over, h - 1 - under)[:, :, None, :]
        m = rng.integers(0, 10, (N, 8, 1, M)); base = need // (16 - m)
        place = np.argsort(np.argsort(rng.random(z.shape) + 2 * (rows < m), axis=2), axis=2)
        diff = np.where(rows >= m, base + (place < need - base * (16 - m)), 0)
        come = z + np.where(z < 8, diff, -diff)
        a = np.add.reduce((fail * weight).reshape(N, -1), axis=1)
        z = np.where(fail[:, :, None, :], np.abs(z - at), z); at = come
    v = np.zeros((N, 8, P), np.int64); zp = np.zeros((N, 8, 16, P), np.int64); who = np.concatenate([np.arange(M), np.arange(P - M)])
    for q in range(N):
        for g in range(8):
            x[q, g][:, n[g, R]] = at[q, g]
            r = who[rng.permutation(P)]; v[q, g] = n[g, 0][r]; zp[q, g] = z0[q, g][:, r]
    return pack(nb, x, v, zp, th)
def check_inputs(d):
    bad = []
    for k, hi in (("nb", W - 1), ("xd", 15), ("pv", W - 1), ("pz", 15), ("th", 241)):
        a = np.asarray(d[k]).astype(np.float64)
        if not (np.min(a) >= 0 and np.max(a) <= hi): bad.append("range of " + k)
        if np.any(a != np.floor(a)): bad.append("whole numbers of " + k)
    t = np.asarray(d["th"]).reshape(N, 8, 16, 2)
    if np.any(t != t[:, :, :1]): bad.append("rows of a group alike in th")
    return bad
def dist(x, z, u):
    s = np.zeros(u.shape, np.int64)
    for p in range(16):
        s = s + np.abs(np.take_along_axis(x[:, :, p], u.reshape(N, 8, -1), 2).reshape(u.shape) - z[:, :, p][:, :, None, :])
    return s
def reference(nb, xd, pv, pz, th):
    c = nb.astype(np.int64).reshape(N, 8, 16, W); x = xd.astype(np.float32).astype(np.int64).reshape(N, 8, 16, W)
    v = np.stack([gentries(a) for a in pv]).astype(np.int64); z = pz.astype(np.float32).astype(np.int64).reshape(N, 8, 16, P)
    h = th.astype(np.int64).reshape(N, 8, 16, 2)[:, :, 0]; a = np.zeros(N, np.int64)
    for t in range(R):
        if t > 0: v = np.roll(v, S, axis=0); z = np.roll(z, S, axis=0)
        xv = np.take_along_axis(x, v[:, :, None, :], 3); con = np.take_along_axis(c, v[:, :, None, :], 3)
        near = (np.abs(xv - z) <= 1).astype(np.int64)
        l = np.minimum(np.add.reduce(np.multiply.accumulate(near, axis=2), axis=2), LM)
        tl = np.take_along_axis(con, l[:, :, None, :], 2)
        ok = dist(x, z, tl)[:, :, 0] < h[:, :, 0, None] + (a & 15)[:, None, None]
        new = np.where(ok, tl[:, :, 0], con[:, :, 15]); todo = ~ok; fixed = np.zeros(ok.shape, bool)
        order = (l[:, :, None, :] + np.arange(16)[:, None]) & 15
        for e in range(E + 1):
            cand = np.take_along_axis(c.reshape(N, 8, 16 * W), ((l + e)[:, :, None, :] * W + con).reshape(N, 8, -1), 2).reshape(N, 8, 16, P)
            hit = np.take_along_axis(dist(x, z, cand) < h[:, :, 1, None, None], order, 2); cand = np.take_along_axis(cand, order, 2)
            got = todo & np.any(hit, axis=2)
            new = np.where(got, np.take_along_axis(cand, np.argmax(hit, axis=2)[:, :, None, :], 2)[:, :, 0], new)
            fixed = fixed | got; todo = todo & ~got
        a = np.add.reduce((~ok).astype(np.int64).reshape(N, -1), axis=1)
        for q in range(N):
            for g in range(8):
                i = np.flatnonzero(fixed[q, g]); u, k = np.unique(v[q, g, i], return_index=True); i = i[k]
                c[q, g][l[q, g][i], u] = new[q, g][i]
                if t < R - 1:
                    u, i = np.unique(v[q, g], return_index=True)
                    x[q, g][:, u] = (xv[q, g][:, i] + z[q, g][:, i]) >> 1
        z = np.where(todo[:, :, None, :], np.abs(z - xv), z); v = new
    return {"ynb": c.reshape(N, 128, W).astype(np.float32), "yv": np.stack([gtable(b) for b in v]).astype(np.float32), "yz": z.reshape(N, 128, P).astype(np.float32).astype(BF)}

@@ -1,0 +1,586 @@
+import math
+from concourse.mybir import AluOpType as OP, ActivationFunctionType as AF
+
+W, P, R, STEP = 2048, 192, 3, 3
+n, NC = 64, 3
+NB = n // 16
+SP = 2 * n
+WX = SP + W
+SEG = n + 32
+H16 = ["Id", "nId", "Id128", "Id256", "Id64s", "One", "One4096", "Nr", "Tri", "Linv", "M", "OH4", "nOH4",
+       "kA", "kB", "kC", "Zc", "L64", "Ln16", "K0", "Id4096"]
+B16 = ["L", "nOne", "Id2m1"]
+F16, BF, F32 = "float16", "bfloat16", "float32"
+SCRATCH = {
+    "nbi": ("sbuf", [128, W], "int32"), "nbf": ("sbuf", [128, WX], F32),
+    "xdb": ("sbuf", [128, W], BF), "xw": ("sbuf", [128, WX], F32),
+    "pvi": ("sbuf", [128, 12], "int32"), "pzb": ("sbuf", [128, P], BF), "thi": ("sbuf", [128, 2], "int32"),
+    "pvx": ("sbuf", [128, P], F16),
+    "h16": ("sbuf", [128, len(H16), 16], F16), "hbig": ("sbuf", [128, len(H16), 128], F16),
+    "b16": ("sbuf", [128, len(B16), 16], BF), "bbig": ("sbuf", [128, len(B16), 128], BF),
+    "dw": ("sbuf", [128, 144], F32), "t1": ("sbuf", [128, 144], F16), "td": ("sbuf", [128, 144], F16),
+    "col": ("sbuf", [128, 32], F32), "coli": ("sbuf", [128, 8], "int32"), "blk": ("sbuf", [128, 8], F32),
+    "tmp": ("sbuf", [128, 10, 16], F32), "tmpi": ("sbuf", [128, 2, 16], "int32"),
+    "io4": ("sbuf", [128, NB, SEG], BF), "io5": ("sbuf", [128, NB, SEG], F32), "io6": ("sbuf", [128, NB, SEG], F16),
+    "io7": ("sbuf", [128, NB, SEG], F16), "ddc": ("sbuf", [128, NB * SEG], F16), "keepd": ("sbuf", [128, NB * SEG], F32),
+    "db": ("sbuf", [128, n], F16), "keep": ("sbuf", [128, n], F32), "o32": ("sbuf", [128, 128], F32),
+    "land": ("sbuf", [128, R, NC, 2 * n], F16), "send": ("sbuf", [128, R - 1, NC, 2 * n], F16),
+    "zrep": ("sbuf", [128, NC, 16 * n], F16), "zq": ("sbuf", [128, NC, 4 * n], F16),
+    "vsc": ("sbuf", [128, NC, n], F32), "vl": ("sbuf", [128, NC * NB], F32), "vu": ("sbuf", [128, NC * NB], "uint16"),
+    "xv": ("sbuf", [128, NC, n], F16), "conu": ("sbuf", [128, NC, n], "uint16"),
+    "cf": ("sbuf", [128, NC, 3 * n], F16), "aa": ("sbuf", [128, NC, n], F16), "bad": ("sbuf", [128, NC, n], F16),
+    "ul": ("sbuf", [128, NC, n], F16), "nd": ("sbuf", [128, NC, n], BF), "ndw": ("sbuf", [128, NC, n], F32),
+    "gg": ("sbuf", [128, NC, 16 * n], F16), "gm": ("sbuf", [128, NC, 16 * n], F16),
+    "cu": ("sbuf", [128, NC, 2 * n], "uint16"), "mx": ("sbuf", [128, NC, 2, 16 * n], F16),
+    "yy": ("sbuf", [128, NC, n], F16), "pre": ("sbuf", [128, NC, n], F32), "tsc": ("sbuf", [128, NC, n], F32),
+    "tu": ("sbuf", [128, NC * NB], "uint16"), "xt": ("sbuf", [128, NC, n], F16), "at": ("sbuf", [128, NC, n], F16),
+    "sh": ("sbuf", [128, NC, n], F16), "acc": ("sbuf", [128, NC], F32), "ai": ("sbuf", [128, 2], "int32"),
+    "ne": ("sbuf", [128, NC, NB, n], F16), "dsc": ("sbuf", [128, NC, NB * SEG], F32),
+    "du": ("sbuf", [128, NC * NB], "uint16"), "nu": ("sbuf", [128, NC * NB], "uint16"),
+    "fr": ("sbuf", [128, NC, 2 * n], F16), "dl": ("sbuf", [128, NC, 2 * n], F16), "ad": ("sbuf", [128, NC, 2 * n], F16), "mm": ("sbuf", [128, NC, 2 * n], F16),
+    "ye": ("sbuf", [128, NC, 3 * n], BF), "sel": ("sbuf", [128, NC, 3 * n], F16), "val": ("sbuf", [128, NC, 3 * n], F16),
+    "tt": ("sbuf", [128, NC, n], F32), "zt": ("sbuf", [128, NC, n], F16),
+    "oz": ("sbuf", [128, P], BF), "ov": ("sbuf", [128, 12], F32),
+}
+for _b in range(8):
+    SCRATCH["ps%d" % _b] = ("psum", [128, 512], F32)
+NDMA = 16
+SEMAPHORES = (["eV", "eS", "eP", "eG", "sent"] + ["d%d" % k for k in range(NDMA)]
+              + ["arr%d" % k for k in range((R - 1) * NC)])
+
+VALS, NES, HELP, ROUNDS = (1, 2), (0,), 3, 1300
+MXS = 2
+HOP, GA, SC = 110, 1.56, 3.8
+
+
+def build(g, T, topo, core, dst):
+    ops = []
+    V, S, PE = g.vector, g.scalar, g.tensor
+
+    def add(eng, cost, fn, rd, wr, bank=None, kind="c", sem=None):
+        ops.append({"eng": eng, "cost": cost, "fn": fn, "rd": rd, "wr": wr, "bank": bank, "kind": kind, "sem": sem})
+
+    def vop(cols, fn, rd, wr, bank=None):
+        add("V", 40 + max(64, cols), fn, rd, wr, bank)
+
+    def sop(cols, fn, rd, wr, bank=None):
+        add("S", 60 + max(64, cols), fn, rd, wr, bank)
+
+    def gop(cols, fn, rd, wr):
+        add("G", 200 + 2 * cols, fn, rd, wr)
+
+    def pe(mms, rd, wr, bank):
+        def fn():
+            last = None
+            for o, l, r, st, sp, _n in mms:
+                last = PE.matmul(o, l, r, st, sp)
+            return last
+        add("P", 30 + sum(max(64, m[5]) for m in mms) // 2, fn, rd, wr, bank)
+
+    def grp(out, terms, cols):
+        return [(out, l, r, j == 0, j == len(terms) - 1, cols) for j, (l, r) in enumerate(terms)]
+
+    nd_ = [0]
+
+    def dma(q, out, in_, rd, wr, cost):
+        s = "d%d" % nd_[0]
+        nd_[0] += 1
+        Q = {"Y": g.sync, "S": g.scalar}[q]
+        add(q, cost, lambda: Q.dma_start(out, in_), rd, wr, kind="d", sem=s)
+
+    def ts(out, in0, s1, s2, o0, o1, rd, wr, cols=64, bank=None):
+        if o1 is None:
+            vop(cols, lambda: V.tensor_scalar(out, in0, s1, None, o0), rd, wr, bank)
+        else:
+            vop(cols, lambda: V.tensor_scalar(out, in0, s1, s2, o0, o1), rd, wr, bank)
+
+    def tt(out, a, b, o, rd, wr, cols=64, bank=None):
+        vop(cols, lambda: V.tensor_tensor(out, a, b, o), rd, wr, bank)
+
+    def cp(out, a, rd, wr, cols=64, bank=None):
+        vop(cols, lambda: V.tensor_copy(out, a), rd, wr, bank)
+
+    def ms(out, c, wr, cols=64):
+        vop(cols, lambda: V.memset(out, c), [], wr)
+
+    def act(out, a, f, rd, wr, cols=64, bank=None, **kw):
+        sop(cols, lambda: S.activation(out, a, f, **kw), rd, wr, bank)
+
+    def iota(out, pat, base, cm, wr, cols, flt=True):
+        if flt:
+            gop(cols, lambda: g.iota(out, pat, base, cm, allow_small_or_imprecise_dtypes=True), [], wr)
+        else:
+            gop(cols, lambda: g.iota(out, pat, base, cm), [], wr)
+
+    ps = [T["ps%d" % b] for b in range(8)]
+    hs = lambda m: T.h16[:, H16.index(m), :]
+    bs = lambda m: T.b16[:, B16.index(m), :]
+    Hm = lambda m: T.hbig[:, H16.index(m), :]
+    Bm = lambda m: T.bbig[:, B16.index(m), :]
+    CN = ["p16", "p0", "p15", "odd", "t1c", "tdw", "zc", "zoff", "dabs", "ndb", "lnb", "xwb", "ub", "zb", "zo", "l15",
+          "s64", "p08", "p192", "p33", "th0", "th1", "mb", "hb0", "hb1", "hb2", "hH", "m4096", "k0", "l64", "ln16"]
+    C = lambda m: T.col[:, CN.index(m):CN.index(m) + 1]
+
+    dma("Y", T.xdb[:, 0:W], T.xd[:], [], ["xdb"], 4200)
+    dma("S", T.pvi[:], T.pv[:], [], ["pvi"], 2600)
+    dma("S", T.pzb[:], T.pz[:], [], ["pzb"], 2700)
+    dma("S", T.thi[:], T.th[:], [], ["thi"], 2700)
+    for q in range(4):
+        dma("Y", T.nbi[:, 512 * q:512 * q + 512], T.nb[:, 512 * q:512 * q + 512], [], ["nbi%d" % q], 5500 + 1300 * q)
+    for q in range(4):
+        cp(T.nbf[:, SP + 512 * q:SP + 512 * q + 512], T.nbi[:, 512 * q:512 * q + 512], ["nbi%d" % q], ["nbf%d" % q], 512)
+    NBF = ["nbf%d" % q for q in range(5)]
+    XW = ["xw%d" % q for q in range(5)]
+    ms(T.nbf[:, 0:SP], 0.0, ["nbf4"], SP)
+    ms(T.xw[:, 0:SP], 0.0, ["xw4"], SP)
+
+    iota(T.coli[:, 0:1], [[0, 1]], 0, 1, ["ci0"], 1, False)
+    iota(T.dw[:], [[1, 144]], 0, -1, ["dw"], 144)
+    iota(T.tmp[:, 0, :], [[1, 16]], 0, 0, ["m0"], 16)
+    iota(T.tmp[:, 1, :], [[0, 2], [1, 8]], 0, 0, ["m1"], 16)
+    iota(T.tmp[:, 2, :], [[-16, 2], [1, 8]], 18, 0, ["m2"], 16)
+    iota(T.tmpi[:, 0, :], [[1, 2], [0, 8]], 0, 1, ["mi0"], 16, False)
+    iota(T.io4[:, :, 0:n], [[-16, NB], [1, n]], 0, 0, ["io4a"], NB * n)
+    iota(T.io4[:, :, n:SEG], [[0, NB], [0, 2], [1, 16]], 0, 0, ["io4b"], NB * 32)
+    iota(T.io5[:, :, 0:n], [[32, NB], [0, n]], 0, 0, ["io5a"], NB * n)
+    iota(T.io5[:, :, n:n + 16], [[32, NB], [0, 16]], 3072, 0, ["io5b"], NB * 16)
+    ts(T.coli[:, 1:2], T.coli[:, 0:1], 15, None, OP.bitwise_and, None, ["ci0"], ["ci1"])
+    ts(T.coli[:, 2:3], T.coli[:, 0:1], 1, None, OP.bitwise_and, None, ["ci0"], ["ci2"])
+    cp(C("p16"), T.coli[:, 1:2], ["ci1"], ["p16"])
+    cp(C("odd"), T.coli[:, 2:3], ["ci2"], ["odd"])
+    ts(C("p0"), C("p16"), 0.0, None, OP.is_equal, None, ["p16"], ["p0"])
+    ts(C("p15"), C("p16"), 15.0, None, OP.is_equal, None, ["p16"], ["p15"])
+    for name, src, a, b in (("t1c", "odd", 8, 16), ("tdw", "p15", -1 / 256, 2 / 256), ("zc", "p15", -255 / 256, -1 / 256), ("zoff", "p15", -2047, 0),
+                            ("dabs", "p15", -2040, 0), ("ndb", "p15", 1027, 191.75), ("lnb", "p15", -47872, -192),
+                            ("xwb", "p15", -1792, 0), ("ub", "p15", -1, 1), ("zb", "p15", -2047, -48), ("zo", "p15", 2047, 0),
+                            ("l15", "p15", 257, -1), ("s64", "p15", -64, 64), ("p08", "p0", 8, 0), ("p192", "p0", 192, 0),
+                            ("p33", "p0", 33, 0), ("m4096", "p0", 0, -4096),
+                            ("k0", "p0", -504, 0), ("hH", "p16", 2, 0), ("l64", "p15", 64, 0), ("ln16", "p15", -16, 0)):
+        act(C(name), C(src), AF.Identity, [src], [name], scale=float(a), bias=float(b))
+    ts(T.dw[:], T.dw[:], C("p16"), None, OP.add, None, ["dw", "p16"], ["dw"], 144)
+    ts(T.td[:], T.dw[:], 16.0, C("tdw"), OP.is_equal, OP.mult, ["dw", "tdw"], ["td"], 144)
+    ts(T.t1[:], T.dw[:], C("t1c"), None, OP.is_equal, None, ["dw", "t1c"], ["t1"], 144)
+    ts(T.blk[:], T.dw[:, 0:128:16], 0.0, None, OP.is_equal, None, ["dw"], ["blk"])
+    D16 = T.tmp[:, 0, :]
+    ts(D16, D16, C("p16"), None, OP.subtract, None, ["m0", "p16"], ["m0"])
+    ts(T.tmp[:, 1, :], T.tmp[:, 1, :], C("p16"), None, OP.subtract, None, ["m1", "p16"], ["m1"])
+    for name in ("Id", "Linv"):
+        ts(hs(name), D16, 0.0, None, OP.is_equal, None, ["m0"], ["h" + name])
+    ms(hs("One"), 1.0, ["hOne"])
+    for name, src, s in (("nId", "Id", -1.0), ("Id128", "Id", 128.0), ("Id256", "Id", 256.0),
+                         ("Id4096", "Id", 4096.0), ("Id64s", "Id", "s64"), ("One4096", "One", 4096.0), ("Nr", "One", -3072.0),
+                         ("K0", "One", "k0"), ("Zc", "One", "zc"),
+                         ("L64", "One", "l64"), ("Ln16", "One", "ln16")):
+        if s in CN:
+            act(hs(name), hs(src), AF.Identity, ["h" + src, s], ["h" + name], scale=C(s))
+        else:
+            act(hs(name), hs(src), AF.Identity, ["h" + src], ["h" + name], scale=s)
+    ms(T.h16[:, H16.index("Linv"), 15:16], 1.0 / 256, ["hLinv"])
+    ts(hs("Tri"), D16, 0.0, None, OP.is_gt, None, ["m0"], ["hTri"])
+    ts(T.tmp[:, 3, :], D16, 0.0, 4096.0, OP.is_equal, OP.mult, ["m0"], ["m3"])
+    ts(T.tmp[:, 4, :], D16, -1.0, 4096.0, OP.is_equal, OP.mult, ["m0"], ["m4"])
+    tt(hs("OH4"), T.tmp[:, 3, :], T.tmp[:, 4, :], OP.subtract, ["m3", "m4"], ["hOH4"])
+    tt(hs("nOH4"), T.tmp[:, 4, :], T.tmp[:, 3, :], OP.subtract, ["m3", "m4"], ["hnOH4"])
+    io, im = H16.index("OH4"), H16.index("M")
+    tt(T.h16[:, im, 1:16], T.h16[:, io, 1:16], T.h16[:, io, 0:15], OP.add, ["hOH4"], ["hM"])
+    cp(T.h16[:, im, 0:1], T.h16[:, io, 0:1], ["hOH4", "hM"], ["hM"])
+    ts(T.tmpi[:, 1, :], T.tmpi[:, 0, :], 1, None, OP.bitwise_and, None, ["mi0"], ["mi1"])
+    ts(T.tmp[:, 5, :], T.tmpi[:, 1, :], 32.0, -17.0, OP.mult, OP.add, ["mi1"], ["m5"])
+    ts(T.tmp[:, 2, :], T.tmp[:, 2, :], C("p0"), None, OP.mult, None, ["m2", "p0"], ["m2"])
+    tt(T.tmp[:, 5, :], T.tmp[:, 5, :], T.tmp[:, 2, :], OP.add, ["m5", "m2"], ["m5"])
+    ts(T.tmp[:, 6, :], T.tmp[:, 1, :], -1.0, 16.0, OP.is_equal, OP.mult, ["m1"], ["m6"])
+    ts(T.tmp[:, 7, :], T.tmp[:, 1, :], -9.0, 16.0, OP.is_equal, OP.mult, ["m1"], ["m7"])
+    tt(hs("kA"), T.tmp[:, 5, :], T.tmp[:, 6, :], OP.add, ["m5", "m6"], ["hkA"])
+    ts(T.tmp[:, 7, :], T.tmp[:, 7, :], C("p08"), None, OP.add, None, ["m7", "p08"], ["m7"])
+    tt(hs("kB"), T.tmp[:, 5, :], T.tmp[:, 7, :], OP.add, ["m5", "m7"], ["hkB"])
+    ts(hs("kC"), hs("OH4"), -1.0 / 32, C("p192"), OP.mult, OP.add, ["hOH4", "p192"], ["hkC"])
+    cp(T.h16[:, H16.index("kC"), 15:16], C("p33"), ["p33", "hkC"], ["hkC"])
+    ts(bs("L"), D16, 0.0, None, OP.is_equal, None, ["m0"], ["bL"])
+    cp(T.b16[:, B16.index("L"), 15:16], C("l15"), ["l15", "bL"], ["bL"])
+    ms(bs("nOne"), -1.0, ["bnOne"])
+    ts(bs("Id2m1"), hs("Id"), 2.0, -1.0, OP.mult, OP.add, ["hId"], ["bId2m1"])
+    for gq in range(8):
+        sl = slice(16 * gq, 16 * gq + 16)
+        act(T.bbig[:, :, sl], T.b16[:], AF.Identity, ["blk"] + ["b" + m for m in B16], ["bbig%d" % gq], scale=T.blk[:, gq:gq + 1])
+        ts(T.hbig[:, :, sl], T.h16[:], T.blk[:, gq:gq + 1], None, OP.mult, None, ["blk"] + ["h" + m for m in H16],
+           ["hbig%d" % gq], len(H16) * 8)
+    HB = ["hbig%d" % q for q in range(8)]
+    BB = ["bbig%d" % q for q in range(8)]
+    ts(T.io6[:, :, 0:n], T.io4[:, :, 0:n], C("p16"), 8192.0, OP.is_ge, OP.mult, ["io4a", "p16"], ["io6a"], NB * n // 2)
+    ts(T.io6[:, :, n:SEG], T.io4[:, :, n:SEG], C("p16"), 8192.0, OP.not_equal, OP.mult, ["io4b", "p16"], ["io6b"])
+    act(T.io7[:, :, 0:n + 16], T.io5[:, :, 0:n + 16], AF.Identity, ["io5a", "io5b", "hH"], ["io7a"], NB * (n + 16), bias=C("hH"))
+    ms(T.io7[:, :, n + 16:SEG], float(SP), ["io7b"])
+    for b in range(NB):
+        tt(T.ddc[:, SEG * b:SEG * b + SEG], T.io7[:, b, :], T.io6[:, b, :], OP.add, ["io7a", "io7b", "io6a", "io6b", "ddc"], ["ddc"], SEG)
+        act(T.db[:, 16 * b:16 * b + 16], T.io6[:, 0, n:n + 16], AF.Identity, ["io6b"], ["db%d" % b], scale=-1.0)
+    DB = ["db%d" % b for b in range(NB)]
+    ms(T.keepd[:], 0.0, ["keepd"], NB * SEG)
+    ms(T.keepd[:, 0:NB * SEG:SEG], 65536.0, ["keepd"])
+    ms(T.keep[:], 1.0, ["keep"])
+    ms(T.keep[:, 0:n:16], 0.0, ["keep"])
+    ms(T.o32[:], 1.0 / 32, ["o32"], 128)
+    cp(T.col[:, CN.index("th0"):CN.index("th0") + 2], T.thi[:], ["thi"], ["th"])
+    ts(C("mb"), C("th1"), -1.0, 1.0, OP.mult, OP.add, ["th"], ["mb"])
+    ts(C("hb0"), C("th0"), -1.0, 0.5, OP.mult, OP.add, ["th"], ["hb0"])
+
+    for q in range(4):
+        sl = slice(512 * q, 512 * q + 512)
+        pe(grp(ps[q][:, 0:512], [(Bm("L"), T.xdb[:, sl])], 512), BB + ["xdb"], ["P%d" % q], q)
+        act(T.xw[:, SP + 512 * q:SP + 512 * q + 512], ps[q][:, 0:512], AF.Identity, ["P%d" % q, "xwb"], ["xw%d" % q], 512, q, bias=C("xwb"))
+
+    cp(T.vl[:], T.pvi[:], ["pvi"], ["vl%d" % c for c in range(NC)])
+    cp(T.vu[:], T.pvi[:], ["pvi"], ["vu%d" % c for c in range(NC)])
+    for c in reversed(range(NC)):
+        ts(T.land[:, 0, c, 0:n], T.pzb[:, n * c:n * c + n], C("zoff"), None, OP.add, None, ["pzb", "zoff"], ["z0_%d" % c])
+        for b in range(NB):
+            k = NB * c + b
+            act(T.pvx[:, 16 * k:16 * k + 16], hs("Id"), AF.Identity, ["hId", "vl%d" % c], ["pvx%d" % k], scale=T.vl[:, k:k + 1])
+        pe(grp(ps[5][:, 384:448], [(Hm("One"), T.pvx[:, n * c:n * c + n])], n), HB + ["pvx%d" % (NB * c + b) for b in range(NB)],
+           ["Pnv"], 5)
+        act(T.land[:, 0, c, n:2 * n], ps[5][:, 384:448], AF.Copy, ["Pnv"], ["v0_%d" % c], n, 5)
+
+    rid, pid, _se = topo.addr(dst)
+    eng = topo.engines(core, dst)[:4]
+    mask = sum(1 << e for e in eng)
+    win_n, win_x = T.nbf[:, SP:WX], T.xw[:, SP:WX]
+
+    for t in range(R):
+        last = t == R - 1
+
+        def chunk(c, t=t, last=last):
+            s = str(c)
+            z, vb = T.land[:, t, c, 0:n], T.land[:, t, c, n:2 * n]
+            zn, vn = "z%d_%d" % (t, c), "v%d_%d" % (t, c)
+            lc = slice(NB * c, NB * c + NB)
+            if t > 0:
+                add("X", 3000, None, ["sent%d_%d" % (t - 1, c)], [zn, vn], kind="r", sem="arr%d" % ((t - 1) * NC + c))
+                pe(grp(ps[5][:, 0:64], [(Hm("Id"), T.db[:]), (Hm("Id"), vb)], n), HB + DB + [vn], ["Pvs"], 5)
+                vop(n, lambda c=c: V.tensor_tensor_scan(T.vsc[:, c, :], T.keep[:], ps[5][:, 0:64], 0.0, OP.mult, OP.max),
+                    ["Pvs", "keep"], ["vsc" + s], 5)
+                cp(T.vu[:, lc], T.vsc[:, c, 15:n:16], ["vsc" + s], ["vu" + s])
+                vcol = lambda b, c=c: T.vsc[:, c, 16 * b + 15:16 * b + 16]
+                vname = "vsc" + s
+            else:
+                vcol = lambda b, c=c: T.vl[:, NB * c + b:NB * c + b + 1]
+                vname = "vl" + s
+            def zcopy(o, a, pat, cols, rd, wr):
+                gop(cols, lambda: g.affine_select(o, a, pat, OP.is_ge, 0.0, 0, 0), rd, wr)
+            for j in range(4):
+                zcopy(T.zq[:, c, j:4 * n:4], z, [[0, n]], n, [zn], ["zq%d" % j + s])
+            for j in range(4):
+                zcopy(T.zrep[:, c, j:16 * n:4], T.zq[:, c, :], [[0, 4 * n]], 4 * n, ["zq%d" % i + s for i in range(4)], ["zr%d" % j + s])
+            ZR = ["zr%d" % j + s for j in range(4)]
+            gn = int(GA * n) + 20
+            vl_ = T.vu[:, lc]
+            cp(T.conu[:, c, :], win_n.indirect(vl_), NBF + ["vu" + s], ["conu" + s], gn)
+            act(T.xv[:, c, :], win_x.indirect(vl_), AF.Copy, XW + ["vu" + s], ["xv" + s], gn)
+            con = T.cf[:, c, 2 * n:3 * n]
+            act(con, win_n.indirect(vl_), AF.Copy, NBF + ["vu" + s], ["con" + s], gn)
+            xv, u = T.xv[:, c, :], T.ul[:, c, :]
+            pe(grp(ps[5][:, 64:128], [(Hm("Linv"), xv), (Hm("nId"), z)], n), HB + ["xv" + s, zn], ["Pd"], 5)
+            act(T.aa[:, c, :], ps[5][:, 64:128], AF.Abs, ["Pd", "dabs"], ["aa" + s], n, 5, bias=C("dabs"))
+            act(T.bad[:, c, :], T.aa[:, c, :], AF.Relu, ["aa" + s], ["bad" + s], n, bias=-1.0)
+            pe(grp(ps[5][:, 192:256], [(Hm("Tri"), T.bad[:, c, :])], n), HB + ["bad" + s], ["Pc"], 5)
+            act(u, ps[5][:, 192:256], AF.Relu, ["Pc", "ub"], ["u" + s], n, 5, bias=C("ub"), scale=-1.0)
+            yield
+            pe(grp(ps[2][:, 128:192], [(Hm("Id"), con), (Hm("OH4"), u)], n)
+               + grp(ps[2][:, 192:256], [(Hm("Id"), con), (Hm("nOH4"), u)], n), HB + ["con" + s, "u" + s], ["Py"], 2)
+            act(T.yy[:, c, :], ps[2][:, 128:192], AF.Relu, ["Py", "m4096"], ["yy" + s], n, 2, bias=C("m4096"))
+            act(T.pre[:, c, :], ps[2][:, 192:256], AF.Relu, ["Py"], ["pre" + s], n, 2)
+            pe(grp(ps[2][:, 256:320], [(Hm("Id"), T.db[:]), (Hm("One"), T.yy[:, c, :])], n), HB + DB + ["yy" + s], ["Pt"], 2)
+            vop(n, lambda c=c: V.tensor_tensor_scan(T.tsc[:, c, :], T.keep[:], ps[2][:, 256:320], 0.0, OP.mult, OP.max),
+                ["Pt", "keep"], ["tsc" + s], 2)
+            cp(T.tu[:, lc], T.tsc[:, c, 15:n:16], ["tsc" + s], ["tu" + s])
+            act(T.xt[:, c, :], win_x.indirect(T.tu[:, lc]), AF.Copy, XW + ["tu" + s], ["xt" + s], gn)
+            pe(grp(ps[2][:, 320:384], [(Hm("Linv"), T.xt[:, c, :]), (Hm("nId"), z)], n), HB + ["xt" + s, zn], ["PdT"], 2)
+            act(T.at[:, c, :], ps[2][:, 320:384], AF.Abs, ["PdT", "dabs"], ["at" + s], n, 2, bias=C("dabs"))
+            pe(grp(ps[2][:, 384:448], [(Hm("One"), T.at[:, c, :])], n), HB + ["at" + s], ["PDT"], 2)
+            hb = "hb%d" % t
+            if last:
+                act(T.sh[:, c, :], ps[2][:, 384:448], AF.Sign, ["PDT", hb], ["sh" + s], n, 2, bias=C(hb))
+            else:
+                act(T.sh[:, c, :], ps[2][:, 384:448], AF.Sign, ["PDT", hb], ["sh" + s, "acc" + s], n + 30, 2, bias=C(hb),
+                    accum_out=T.acc[:, c:c + 1])
+            for b in range(NB):
+                if c in NES:
+                    act(T.ne[:, c, b, :], vb, AF.Abs, [vn, vname], ["ne%d" % b + s], n, bias=vcol(b), scale=-1.0)
+                else:
+                    ts(T.ne[:, c, b, :], vb, vcol(b), None, OP.not_equal, None, [vn, vname], ["ne%d" % b + s])
+
+            def dpre(stop=False):
+                mm = [(ps[7][:, 0:NB * SEG], Hm("Id"), T.ddc[:], True, False, NB * SEG)]
+                for b in range(NB):
+                    mm.append((ps[7][:, SEG * b:SEG * b + n], Hm("Id4096"), T.ne[:, c, b, :], False, False, n))
+                    mm.append((ps[7][:, SEG * b + n + 16:SEG * b + SEG], Hm("Id"), T.land[:, t, c, n + 16 * b:n + 16 * b + 16],
+                               False, stop and b == NB - 1, 16))
+                pe(mm, HB + [vn, "ddc"] + ["ne%d" % b + s for b in range(NB)], ["P7"], 7)
+
+            def dscan(lst, name, c=c, s=s, lc=lc):
+                vop(NB * SEG, lambda: V.tensor_tensor_scan(T.dsc[:, c, :], T.keepd[:], ps[7][:, 0:NB * SEG], 0.0, OP.add, OP.min),
+                    ["P7", "keepd"], ["dsc" + s], 7)
+                cp(lst[:, lc], T.dsc[:, c, SEG - 1:NB * SEG:SEG], ["dsc" + s], [name + s])
+            if not last:
+                dpre(True)
+                dscan(T.du, "du")
+                pe(grp(ps[5][:, 128:192], [(Hm("Linv"), xv), (Hm("Id"), z)], n), HB + ["xv" + s, zn], ["Pn"], 5)
+                act(T.nd[:, c, :], ps[5][:, 128:192], AF.Identity, ["Pn", "ndb"], ["nd" + s], n, 5, bias=C("ndb"), scale=0.5)
+                pe(grp(ps[5][:, 256:320], [(Bm("L"), T.nd[:, c, :])], n), BB + ["nd" + s], ["PL"], 5)
+                act(T.ndw[:, c, :], ps[5][:, 256:320], AF.Identity, ["PL", "lnb"], ["ndw" + s], n, 5, bias=C("lnb"))
+            yield
+            first = c == NC - 1
+            h = n // 2
+            if first and HELP & 1:
+                cp(T.gg[:, c, 0:16 * h], win_n.indirect(T.conu[:, c, 0:h]), NBF + ["conu" + s], ["gga" + s], int(GA * 16 * h))
+            else:
+                act(T.gg[:, c, 0:16 * h], win_n.indirect(T.conu[:, c, 0:h]), AF.Copy, NBF + ["conu" + s], ["gga" + s], int(GA * 16 * h))
+            act(T.gg[:, c, 16 * h:16 * n], win_n.indirect(T.conu[:, c, h:n]), AF.Copy, NBF + ["conu" + s], ["ggb" + s], int(GA * 16 * h))
+            rb = 3 + (t * NC + c) % 2
+            Rp, PR = ps[rb], "P%d" % rb
+            for h in range(2):
+                hn = "%d" % h + s
+                parts = [(0, 0, 4), (1, 4, 8)] if first and h == 0 and HELP & 2 else [(h, 0, 8)]
+                for bk, k0, k1 in parts:
+                    mm = []
+                    for k in range(k0, k1):
+                        mm += grp(ps[bk][:, n * k:n * k + n], [(Hm("Id"), T.gg[:, c, 8 * h + k:16 * n:16]), (Hm("M"), u)], n)
+                    pe(mm, HB + ["gga" + s, "ggb" + s, "u" + s], ["P%d" % bk], bk)
+                    gm = T.gm[:, c, 8 * n * h + n * k0:8 * n * h + n * k1]
+                    if k1 == 8 and k0:
+                        ts(gm, ps[bk][:, n * k0:n * k1], -4096.0, 0.0, OP.add, OP.max, ["P%d" % bk], ["gn" + hn], (k1 - k0) * n, bk)
+                    else:
+                        act(gm, ps[bk][:, n * k0:n * k1], AF.Relu, ["P%d" % bk], ["gm" + hn], (k1 - k0) * n, bk, bias=-4096.0)
+                Cp = ps[2][:, n * h:n * h + n]
+                pe(grp(Cp, [(T.t1[:, 16 - k:144 - k], T.gm[:, c, 8 * n * h + n * k:8 * n * h + n * k + n]) for k in range(8)], n),
+                   ["t1", "gm" + hn, "gn" + hn], ["PC%d" % h], 2)
+                cp(T.cu[:, c, n * h:n * h + n], Cp, ["PC%d" % h], ["cu" + hn], n, 2)
+                act(T.cf[:, c, n * h:n * h + n], Cp, AF.Copy, ["PC%d" % h], ["cf" + hn], n, 2)
+                w = n // MXS
+                for j in range(MXS):
+                    tt(T.mx[:, c, h, 16 * w * j:16 * w * j + 16 * w], win_x.indirect(T.cu[:, c, n * h + w * j:n * h + w * j + w]),
+                       T.zrep[:, c, 16 * w * j:16 * w * j + 16 * w], OP.max, XW + ZR + ["cu" + hn], ["mx%d" % j + hn], int(GA * 16 * w))
+                pe(grp(Rp[:, n * h:n * h + n], [(Hm("Zc"), z), (Hm("K0"), u)]
+                       + [(T.td[:, 16 - k:144 - k], T.mx[:, c, h, k:16 * n:16]) for k in range(16)], n),
+                   HB + ["td", zn, "u" + s] + ["mx%d" % j + hn for j in range(MXS)], [PR + "r%d" % h], rb)
+            yield
+            RR = [PR + "r0", PR + "r1"]
+            act(T.dl[:, c, :], Rp[:, 0:2 * n], AF.Identity, RR, ["dl" + s], 2 * n, rb, bias=-0.4375)
+            tt(T.fr[:, c, :], Rp[:, 0:2 * n], T.dl[:, c, :], OP.subtract, RR + ["dl" + s], ["fr" + s], 2 * n, rb)
+            act(T.ad[:, c, :], T.dl[:, c, :], AF.Abs, ["dl" + s], ["ad" + s], 2 * n, bias=-1536.0)
+            if c == 0 or last:
+                dpre()
+            pe(grp(Rp[:, 2 * n:4 * n], [(Hm("Id256"), T.fr[:, c, :]), (Hm("Id"), T.ad[:, c, :])], 2 * n), HB + ["fr" + s, "ad" + s],
+               [PR + "m"], rb)
+            act(T.mm[:, c, :], Rp[:, 2 * n:4 * n], AF.Relu, [PR + "m", "mb"], ["mm" + s], 2 * n, rb, bias=C("mb"))
+            pe(grp(ps[6][:, 0:n], [(Hm("kA"), u), (Hm("Id128"), T.mm[:, c, 0:n])], n)
+               + grp(ps[6][:, n:2 * n], [(Hm("kB"), u), (Hm("Id128"), T.mm[:, c, n:2 * n])], n)
+               + grp(ps[6][:, 2 * n:3 * n], [(Hm("kC"), u), (Hm("Id64s"), T.sh[:, c, :])], n),
+               HB + ["u" + s, "mm" + s, "sh" + s], ["Px"], 6)
+            act(T.ye[:, c, :], ps[6][:, 0:3 * n], AF.Exp, ["Px"], ["ye" + s], 3 * n, 6, scale=-math.log(4.0))
+            mm = []
+            for a in range(3):
+                mm += grp(ps[6][:, 192 + n * a:192 + n * a + n],
+                          [(Bm("Id2m1" if a == b else "nOne"), T.ye[:, c, n * b:n * b + n]) for b in range(3)], n)
+            pe(mm, BB + ["ye" + s], ["Ps"], 6)
+            ts(T.sel[:, c, :], ps[6][:, 192:384], 0.0, None, OP.is_gt, None, ["Ps"], ["sel" + s], 3 * n, 6)
+            cfn = ["sel" + s, "cf0" + s, "cf1" + s, "con" + s]
+            if c in VALS:
+                pe(grp(ps[6][:, 0:3 * n], [(Hm("Id"), T.cf[:, c, :]), (Hm("Id4096"), T.sel[:, c, :])], 3 * n), HB + cfn, ["Px"], 6)
+                act(T.val[:, c, :], ps[6][:, 0:3 * n], AF.Relu, ["Px"], ["val" + s], 3 * n, 6, bias=-4096.0)
+            else:
+                tt(T.val[:, c, :], T.sel[:, c, :], T.cf[:, c, :], OP.mult, cfn, ["val" + s], 4 * n)
+            selc = T.sel[:, c, 2 * n:3 * n]
+            if not (c == 0 or last):
+                dpre()
+            mm = []
+            for b in range(NB):
+                mm.append((ps[7][:, SEG * b:SEG * b + n], Hm("One4096"), selc, False, False, n))
+                mm.append((ps[7][:, SEG * b + n:SEG * b + n + 16], Hm("Nr"), T.sel[:, c, 2 * n + 16 * b:2 * n + 16 * b + 16],
+                           False, b == NB - 1, 16))
+            pe(mm, HB + ["sel" + s, "P7"], ["P7"], 7)
+            dscan(T.nu, "nu")
+            vals = [(Hm("One"), T.val[:, c, n * a:n * a + n]) for a in range(3)]
+            pe(grp(ps[2][:, 448:512], vals + [(Hm("OH4"), u)], n), HB + ["val" + s, "u" + s], ["Ptt"], 2)
+            act(T.tt[:, c, :], ps[2][:, 448:512], AF.Relu, ["Ptt", "m4096"], ["tt" + s], n, 2, bias=C("m4096"))
+            pe(grp(ps[6][:, 384:448], [(Hm("Id"), T.aa[:, c, :]), (Hm("nId"), z), (Hm("L64"), selc)], n),
+               HB + ["aa" + s, zn, "sel" + s], ["Pz1"], 6)
+            act(T.zt[:, c, :], ps[6][:, 384:448], AF.Relu, ["Pz1", "zb"], ["zt" + s], n, 6, bias=C("zb"))
+            pe(grp(ps[6][:, 448:512], [(Hm("Id"), T.zt[:, c, :]), (Hm("Id"), z), (Hm("Ln16"), selc)], n),
+               HB + ["zt" + s, zn, "sel" + s], ["Pz2"], 6)
+            if not last:
+                act(T.send[:, t, c, 0:n], ps[6][:, 448:512], AF.Copy, ["Pz2"], ["sz%d_%d" % (t, c)], n, 6)
+                pe(grp(ps[5][:, 384:448], vals, n), HB + ["val" + s], ["Pnv"], 5)
+                act(T.send[:, t, c, n:2 * n], ps[5][:, 384:448], AF.Copy, ["Pnv"], ["sv%d_%d" % (t, c)], n, 5)
+                add("G", 700, lambda t=t, c=c: g.remote_dma(T.land[:, t + 1, c, :], T.send[:, t, c, :], T.sem["arr%d" % (t * NC + c)],
+                                                           T.sem["sent"], pid, rid, mask),
+                    ["sz%d_%d" % (t, c), "sv%d_%d" % (t, c)], ["sent%d_%d" % (t, c)], kind="s")
+            else:
+                act(T.oz[:, n * c:n * c + n], ps[6][:, 448:512], AF.Identity, ["Pz2", "zo"], ["oz" + s], n, 6, bias=C("zo"))
+                pe(grp(ps[5][:, 0:64], [(Hm("Id"), T.db[:])] + vals, n), HB + DB + ["val" + s], ["Pvs"], 5)
+                vop(n, lambda c=c: V.tensor_tensor_scan(T.tsc[:, c, :], T.keep[:], ps[5][:, 0:64], 0.0, OP.mult, OP.max),
+                    ["Pvs", "keep"], ["tsc" + s], 5)
+                cp(T.ov[:, lc], T.tsc[:, c, 15:n:16], ["tsc" + s], ["ov" + s])
+        gens = [chunk(c) for c in range(NC)]
+        for c in (2, 1, 0, 2, 1, 0, 2, 1, 2, 0, 1, 0):
+            next(gens[c], None)
+        for c in reversed(range(NC)):
+            s = str(c)
+            lc = slice(NB * c, NB * c + NB)
+            tt(T.nbf[:, 0:WX].indirect(T.nu[:, lc]), T.tt[:, c, :], T.pre[:, c, :], OP.add, ["nu" + s, "tt" + s, "pre" + s], NBF,
+               int(SC * n))
+            if not last:
+                cp(T.xw[:, 0:WX].indirect(T.du[:, lc]), T.ndw[:, c, :], ["du" + s, "ndw" + s], XW, int(SC * n))
+        if not last:
+            pe(grp(ps[5][:, 448:449], [(T.o32[:], T.acc[:, c:c + 1]) for c in range(NC)], 256),
+               ["o32"] + ["acc%d" % c for c in range(NC)], ["Pa"], 5)
+            ts(T.ai[:, 0:1], ps[5][:, 448:449], 768.0, None, OP.add, None, ["Pa"], ["ai0"], 64, 5)
+            ts(T.ai[:, 1:2], T.ai[:, 0:1], 15, None, OP.bitwise_and, None, ["ai0"], ["ai1"])
+            ts(C("hb%d" % (t + 1)), T.ai[:, 1:2], -1.0, C("hb0"), OP.mult, OP.add, ["ai1", "hb0"], ["hb%d" % (t + 1)])
+    dma("Y", T.ynb[0:64, :], T.nbf[0:64, SP:WX], NBF, ["o0"], 6000)
+    dma("S", T.ynb[64:128, :], T.nbf[64:128, SP:WX], NBF, ["o1"], 6000)
+    dma("Y", T.yz[:], T.oz[:], ["oz%d" % c for c in range(NC)], ["o2"], 3000)
+    dma("Y", T.yv[:], T.ov[:], ["ov%d" % c for c in range(NC)], ["o3"], 3000)
+    return ops, len(eng)
+
+
+def key(o):
+    return o["wr"][0] + "<" + (o["rd"][-1] if o["rd"] else "")
+
+
+def plan(ops):
+    N = len(ops)
+    deps = [set() for _ in range(N)]
+    wr, rd = {}, {}
+    for i, o in enumerate(ops):
+        for a in o["rd"]:
+            if a in wr:
+                deps[i].add(wr[a])
+        for a in o["wr"]:
+            if a in wr:
+                deps[i].add(wr[a])
+            deps[i].update(rd.get(a, ()))
+        for a in o["rd"]:
+            rd.setdefault(a, []).append(i)
+        for a in o["wr"]:
+            wr[a] = i
+            rd[a] = []
+        deps[i].discard(i)
+    succ = [[] for _ in range(N)]
+    for i in range(N):
+        for d in deps[i]:
+            succ[d].append(i)
+    prio = [0] * N
+    for i in reversed(range(N)):
+        prio[i] = ops[i]["cost"] + max([prio[j] + HOP for j in succ[i]], default=0)
+    prio = [p + BONUS.get(key(o), 0) for p, o in zip(prio, ops)]
+    left = [len(d) for d in deps]
+    ready = [i for i in range(N) if not left[i]]
+    end, free, bank, order = [0] * N, {}, {}, []
+    while ready:
+        def start(i):
+            o = ops[i]
+            s = max([end[d] + HOP for d in deps[i]], default=0)
+            if o["kind"] != "r":
+                s = max(s, free.get(o["eng"], 0))
+            b = bank.get(o["bank"])
+            if b is not None:
+                s = max(s, end[b] + (HOP if ops[b]["eng"] != o["eng"] else 0))
+            return s
+        st = {i: start(i) for i in ready}
+        t0 = min(st.values())
+        e0 = ops[min(ready, key=lambda i: (st[i], -prio[i]))]["eng"]
+        i = max([j for j in ready if ops[j]["eng"] == e0 and st[j] <= t0 + SLACK], key=lambda j: (prio[j], -j))
+        o = ops[i]
+        end[i] = st[i] + o["cost"]
+        if o["kind"] != "r":
+            free[o["eng"]] = st[i] + 60 if o["kind"] == "d" else end[i]
+        if o["bank"] is not None:
+            b = bank.get(o["bank"])
+            if b is not None and ops[b]["eng"] != o["eng"]:
+                deps[i].add(b)
+            bank[o["bank"]] = i
+        order.append(i)
+        ready.remove(i)
+        for j in succ[i]:
+            left[j] -= 1
+            if not left[j]:
+                ready.append(j)
+    return order, deps, end
+
+
+SLACK = 60
+BONUS = {}
+TUNED = []
+
+
+def tune(ops, rounds):
+    keys = sorted({key(o) for o in ops})
+    steps = (-3000, -1500, -600, -200, 200, 600, 1500, 3000)
+    best, x = max(plan(ops)[2]), 12345
+    for _ in range(rounds):
+        old = dict(BONUS)
+        x = (x * 1103515245 + 12345) % 2147483648
+        for _j in range(1 + (x >> 16) % 3):
+            x = (x * 1103515245 + 12345) % 2147483648
+            k = keys[(x >> 8) % len(keys)]
+            x = (x * 1103515245 + 12345) % 2147483648
+            BONUS[k] = BONUS.get(k, 0) + steps[(x >> 16) % 8]
+        e = max(plan(ops)[2])
+        if e <= best:
+            best = e
+        else:
+            BONUS.clear()
+            BONUS.update(old)
+    return best
+
+
+def rank_program(g, core, T, topo):
+    rank = T.rank_of(core)
+    if rank is None:
+        return
+    dst = T.cores[(rank + STEP) % len(T.cores)]
+    ops, ne = build(g, T, topo, core, dst)
+    if not TUNED:
+        TUNED.append(tune(ops, ROUNDS))
+    order, deps, _end = plan(ops)
+    Q = {"V": g.vector, "S": g.scalar, "P": g.tensor, "G": g, "Y": g.sync}
+    need = set()
+    for i in order:
+        for d in deps[i]:
+            if not (ops[d]["eng"] == "P" and ops[i]["eng"] == "P") and ops[i]["kind"] != "r":
+                need.add(d)
+    count, tick, know, clock = {}, {}, {q: {} for q in Q}, {}
+    for i in order:
+        o = ops[i]
+        if o["kind"] == "r":
+            tick[i], clock[i] = (o["sem"], ne), {}
+            count[o["sem"]] = ne
+            continue
+        q, kn = o["eng"], know[o["eng"]]
+        want = {}
+        for d in deps[i]:
+            if d in tick and not (ops[d]["eng"] == "P" and q == "P"):
+                sem, v = tick[d]
+                if v > want.get(sem, (0, 0))[0]:
+                    want[sem] = (v, d)
+        for sem, (v, d) in sorted(want.items(), key=lambda kv: -order.index(kv[1][1])):
+            if kn.get(sem, 0) < v:
+                Q[q].wait_ge(T.sem[sem], v)
+                kn[sem] = v
+                for s2, v2 in clock[d].items():
+                    kn[s2] = max(kn.get(s2, 0), v2)
+        ins = o["fn"]()
+        clock[i] = dict(kn)
+        if o["kind"] == "d":
+            ins.then_inc(T.sem[o["sem"]], 16)
+            tick[i] = (o["sem"], 16)
+            count[o["sem"]] = 16
+        elif o["kind"] == "s":
+            count["sent"] = count.get("sent", 0) + ne
+        elif i in need:
+            sem = "e" + q
+            count[sem] = count.get(sem, 0) + 1
+            ins.then_inc(T.sem[sem], 1)
+            tick[i] = (sem, count[sem])
+    for sem, v in count.items():
+        if max(know[q].get(sem, 0) for q in Q) < v or sem == "sent":
+            g.sync.wait_ge(T.sem[sem], v)

@@ -1,46 +1,45 @@
-import math
 from concourse.mybir import AluOpType as OP, ActivationFunctionType as AF
 
 W, P, R, STEP = 2048, 192, 3, 3
-n, NC = 64, 3
-NB = n // 16
-SP = 2 * n
-WX = SP + W
-SEG = n + 32
-H16 = ["Id", "nId", "Id128", "Id256", "Id64s", "One", "One4096", "Nr", "Tri", "Linv", "M", "OH4", "nOH4",
-       "kA", "kB", "kC", "Zc", "L64", "Ln16", "K0", "Id4096"]
-B16 = ["L", "nOne", "Id2m1"]
-F16, BF, F32 = "float16", "bfloat16", "float32"
+CH = [(128, 64), (64, 64), (0, 64)]
+NC = len(CH)
+NM = max(n for _c, n in CH)
+SP = 16
+WX = W + 2 * SP
+H16 = ["Id", "One", "L", "nId", "Linv", "Tri", "M", "OHm", "nOH", "I8192",
+       "Zc", "n256", "WA", "WB", "G", "nOne", "na1", "n8192", "A3", "B3", "eId", "K15"]
+HE = 10
+F16, BF, F32, U16 = "float16", "bfloat16", "float32", "uint16"
+CN = ["p16", "odd", "p8", "p15", "bdb", "t1c", "tdw", "zc", "zoff", "dabs", "ndb", "lnb", "xwb", "ohb", "lin", "l15", "b3", "hi",
+      "th0", "th1", "hB", "hb0", "hb1", "hb2", "pm"]
+
+
+def _s(cols, dt):
+    return ("sbuf", [128, cols], dt)
+
+
 SCRATCH = {
-    "nbi": ("sbuf", [128, W], "int32"), "nbf": ("sbuf", [128, WX], F32),
-    "xdb": ("sbuf", [128, W], BF), "xw": ("sbuf", [128, WX], F32),
-    "pvi": ("sbuf", [128, 12], "int32"), "pzb": ("sbuf", [128, P], BF), "thi": ("sbuf", [128, 2], "int32"),
-    "pvx": ("sbuf", [128, P], F16),
+    "nbi": _s(W, "int32"), "nbf": _s(WX, F32), "xdb": _s(W, BF), "xw": _s(WX, F32),
+    "pvi": _s(12, "int32"), "pvf": _s(16, F32), "pzb": _s(P, BF), "thi": _s(2, "int32"),
     "h16": ("sbuf", [128, len(H16), 16], F16), "hbig": ("sbuf", [128, len(H16), 128], F16),
-    "b16": ("sbuf", [128, len(B16), 16], BF), "bbig": ("sbuf", [128, len(B16), 128], BF),
-    "dw": ("sbuf", [128, 144], F32), "t1": ("sbuf", [128, 144], F16), "td": ("sbuf", [128, 144], F16),
-    "col": ("sbuf", [128, 32], F32), "coli": ("sbuf", [128, 8], "int32"), "blk": ("sbuf", [128, 8], F32),
-    "tmp": ("sbuf", [128, 10, 16], F32), "tmpi": ("sbuf", [128, 2, 16], "int32"),
-    "io4": ("sbuf", [128, NB, SEG], BF), "io5": ("sbuf", [128, NB, SEG], F32), "io6": ("sbuf", [128, NB, SEG], F16),
-    "io7": ("sbuf", [128, NB, SEG], F16), "ddc": ("sbuf", [128, NB * SEG], F16), "keepd": ("sbuf", [128, NB * SEG], F32),
-    "db": ("sbuf", [128, n], F16), "keep": ("sbuf", [128, n], F32), "o32": ("sbuf", [128, 128], F32),
-    "land": ("sbuf", [128, R, NC, 2 * n], F16), "send": ("sbuf", [128, R - 1, NC, 2 * n], F16),
-    "zrep": ("sbuf", [128, NC, 16 * n], F16), "zq": ("sbuf", [128, NC, 4 * n], F16),
-    "vsc": ("sbuf", [128, NC, n], F32), "vl": ("sbuf", [128, NC * NB], F32), "vu": ("sbuf", [128, NC * NB], "uint16"),
-    "xv": ("sbuf", [128, NC, n], F16), "conu": ("sbuf", [128, NC, n], "uint16"),
-    "cf": ("sbuf", [128, NC, 3 * n], F16), "aa": ("sbuf", [128, NC, n], F16), "bad": ("sbuf", [128, NC, n], F16),
-    "ul": ("sbuf", [128, NC, n], F16), "nd": ("sbuf", [128, NC, n], BF), "ndw": ("sbuf", [128, NC, n], F32),
-    "gg": ("sbuf", [128, NC, 16 * n], F16), "gm": ("sbuf", [128, NC, 16 * n], F16),
-    "cu": ("sbuf", [128, NC, 2 * n], "uint16"), "mx": ("sbuf", [128, NC, 2, 16 * n], F16),
-    "yy": ("sbuf", [128, NC, n], F16), "pre": ("sbuf", [128, NC, n], F32), "tsc": ("sbuf", [128, NC, n], F32),
-    "tu": ("sbuf", [128, NC * NB], "uint16"), "xt": ("sbuf", [128, NC, n], F16), "at": ("sbuf", [128, NC, n], F16),
-    "sh": ("sbuf", [128, NC, n], F16), "acc": ("sbuf", [128, NC], F32), "ai": ("sbuf", [128, 2], "int32"),
-    "ne": ("sbuf", [128, NC, NB, n], F16), "dsc": ("sbuf", [128, NC, NB * SEG], F32),
-    "du": ("sbuf", [128, NC * NB], "uint16"), "nu": ("sbuf", [128, NC * NB], "uint16"),
-    "fr": ("sbuf", [128, NC, 2 * n], F16), "dl": ("sbuf", [128, NC, 2 * n], F16), "ad": ("sbuf", [128, NC, 2 * n], F16), "mm": ("sbuf", [128, NC, 2 * n], F16),
-    "ye": ("sbuf", [128, NC, 3 * n], BF), "sel": ("sbuf", [128, NC, 3 * n], F16), "val": ("sbuf", [128, NC, 3 * n], F16),
-    "tt": ("sbuf", [128, NC, n], F32), "zt": ("sbuf", [128, NC, n], F16),
-    "oz": ("sbuf", [128, P], BF), "ov": ("sbuf", [128, 12], F32),
+    "Lb": _s(128, BF), "One32": _s(128, F32), "Id32": _s(128, F32), "o32": _s(128, F32), "K32": _s(128, F32),
+    "ts1": _s(144, F16),
+    "dw": _s(144, F32), "t1": _s(144, F16), "td": _s(144, F16),
+    "col": _s(32, F32), "coli": _s(8, "int32"), "blk": _s(8, F32),
+    "tmp": ("sbuf", [128, 8, 16], F32), "wt": ("sbuf", [128, 3, 2, 16], F32), "li": _s(24, "int32"),
+    "cb": _s(12, U16), "crev": _s(12, U16),
+    "jj": _s(NM, F32), "j2": _s(NM, F32), "j3": _s(NM, F32), "db": _s(NM, F16), "dbr": _s(NM, F16), "anti": _s(NM, F32),
+    "cd": _s(NM, F16), "keep": _s(P, F32), "r32": _s(2 * P, F32),
+    "land": ("sbuf", [128, R, 2 * P], F32), "send": ("sbuf", [128, R, 2 * P], F32),
+    "zrep": _s(16 * P, F16), "zq": _s(4 * P, F16),
+    "vsc": _s(P, F16), "vu": _s(12, U16), "eq": _s(P, F16), "xv": _s(P, F16), "conu": _s(P, U16), "con": _s(P, F16),
+    "aa": _s(P, F16), "bad": _s(P, F16), "oh": _s(P, F16), "nd": _s(P, BF), "ndw": _s(P, F32), "yp": _s(2 * P, F32),
+    "gg": _s(16 * P, F16), "gm": _s(16 * P, F16), "cu": _s(2 * P, U16), "mx": _s(32 * P, F16),
+    "tsc": _s(P, F32), "tu": _s(12, U16), "xt": _s(P, F16), "at": _s(P, F16), "sh": _s(P, F16),
+    "acc": _s(4, F32), "ai": _s(2, "int32"), "dsc": _s(P, F32), "nsc": _s(P, F32), "du": _s(24, U16), "nu": _s(24, U16),
+    "dl": _s(2 * P, F16), "ad": _s(2 * P, F16), "hh": _s(2 * P, F16), "ww": _s(2 * P, F16),
+    "sel": _s(4 * P, F16), "val": _s(4 * P, F16),
+    "oz": _s(P, BF), "ov": _s(12, F32),
 }
 for _b in range(8):
     SCRATCH["ps%d" % _b] = ("psum", [128, 512], F32)
@@ -48,8 +47,13 @@ NDMA = 16
 SEMAPHORES = (["eV", "eS", "eP", "eG", "sent"] + ["d%d" % k for k in range(NDMA)]
               + ["arr%d" % k for k in range((R - 1) * NC)])
 
-VALS, NES, HELP, ROUNDS = (1, 2), (0,), 3, 1300
+ROUNDS = 4000
 MXS = 2
+G1V = {0: (1,), 1: (0,)}
+RLV = {0: (1,)}
+G2S = {2: ((0, 1),)}
+SIDE = [[0], [1, 2]]
+DIG = [[0, 1, 2]]
 HOP, GA, SC = 110, 1.56, 3.8
 
 
@@ -60,8 +64,8 @@ def build(g, T, topo, core, dst):
     def add(eng, cost, fn, rd, wr, bank=None, kind="c", sem=None):
         ops.append({"eng": eng, "cost": cost, "fn": fn, "rd": rd, "wr": wr, "bank": bank, "kind": kind, "sem": sem})
 
-    def vop(cols, fn, rd, wr, bank=None):
-        add("V", 40 + max(64, cols), fn, rd, wr, bank)
+    def vop(cols, fn, rd, wr, bank=None, kind="c"):
+        add("V", 40 + max(64, cols), fn, rd, wr, bank, kind)
 
     def sop(cols, fn, rd, wr, bank=None):
         add("S", 60 + max(64, cols), fn, rd, wr, bank)
@@ -77,8 +81,10 @@ def build(g, T, topo, core, dst):
             return last
         add("P", 30 + sum(max(64, m[5]) for m in mms) // 2, fn, rd, wr, bank)
 
-    def grp(out, terms, cols):
-        return [(out, l, r, j == 0, j == len(terms) - 1, cols) for j, (l, r) in enumerate(terms)]
+    def grp(out, terms, cols, start=True, stop=None):
+        stop = start if stop is None else stop
+        return [(out, x[0], x[1], start and j == 0, stop and j == len(terms) - 1, cols * (x[2] if len(x) > 2 else 1))
+                for j, x in enumerate(terms)]
 
     nd_ = [0]
 
@@ -94,14 +100,17 @@ def build(g, T, topo, core, dst):
         else:
             vop(cols, lambda: V.tensor_scalar(out, in0, s1, s2, o0, o1), rd, wr, bank)
 
-    def tt(out, a, b, o, rd, wr, cols=64, bank=None):
-        vop(cols, lambda: V.tensor_tensor(out, a, b, o), rd, wr, bank)
+    def tt(out, a, b, o, rd, wr, cols=64, bank=None, kind="c"):
+        vop(cols, lambda: V.tensor_tensor(out, a, b, o), rd, wr, bank, kind)
 
-    def cp(out, a, rd, wr, cols=64, bank=None):
-        vop(cols, lambda: V.tensor_copy(out, a), rd, wr, bank)
+    def cp(out, a, rd, wr, cols=64, bank=None, kind="c"):
+        vop(cols, lambda: V.tensor_copy(out, a), rd, wr, bank, kind)
 
-    def ms(out, c, wr, cols=64):
-        vop(cols, lambda: V.memset(out, c), [], wr)
+    def ms(out, c, wr, cols=64, rd=()):
+        vop(cols, lambda: V.memset(out, c), list(rd), wr)
+
+    def scan(out, src, n, rd, wr, bank):
+        vop(n, lambda: V.tensor_tensor_scan(out, T.keep[:, 0:n], src, 0.0, OP.min, OP.max), rd + ["keep"], wr, bank)
 
     def act(out, a, f, rd, wr, cols=64, bank=None, **kw):
         sop(cols, lambda: S.activation(out, a, f, **kw), rd, wr, bank)
@@ -114,329 +123,353 @@ def build(g, T, topo, core, dst):
 
     ps = [T["ps%d" % b] for b in range(8)]
     hs = lambda m: T.h16[:, H16.index(m), :]
-    bs = lambda m: T.b16[:, B16.index(m), :]
     Hm = lambda m: T.hbig[:, H16.index(m), :]
-    Bm = lambda m: T.bbig[:, B16.index(m), :]
-    CN = ["p16", "p0", "p15", "odd", "t1c", "tdw", "zc", "zoff", "dabs", "ndb", "lnb", "xwb", "ub", "zb", "zo", "l15",
-          "s64", "p08", "p192", "p33", "th0", "th1", "mb", "hb0", "hb1", "hb2", "hH", "m4096", "k0", "l64", "ln16"]
     C = lambda m: T.col[:, CN.index(m):CN.index(m) + 1]
+    tm = lambda k: T.tmp[:, k, :]
 
-    dma("Y", T.xdb[:, 0:W], T.xd[:], [], ["xdb"], 4200)
+    dma("Y", T.xdb[:], T.xd[:], [], ["xdb"], 4200)
     dma("S", T.pvi[:], T.pv[:], [], ["pvi"], 2600)
     dma("S", T.pzb[:], T.pz[:], [], ["pzb"], 2700)
     dma("S", T.thi[:], T.th[:], [], ["thi"], 2700)
     for q in range(4):
-        dma("Y", T.nbi[:, 512 * q:512 * q + 512], T.nb[:, 512 * q:512 * q + 512], [], ["nbi%d" % q], 5500 + 1300 * q)
-    for q in range(4):
-        cp(T.nbf[:, SP + 512 * q:SP + 512 * q + 512], T.nbi[:, 512 * q:512 * q + 512], ["nbi%d" % q], ["nbf%d" % q], 512)
-    NBF = ["nbf%d" % q for q in range(5)]
-    XW = ["xw%d" % q for q in range(5)]
-    ms(T.nbf[:, 0:SP], 0.0, ["nbf4"], SP)
-    ms(T.xw[:, 0:SP], 0.0, ["xw4"], SP)
+        dma("Y", T.nbi[:, 512 * q:512 * q + 512], T.nb[:, 512 * q:512 * q + 512], [], ["nbi%d" % q], 5000 + 900 * q)
+    NBI = ["nbi%d" % q for q in range(4)]
+    NBF = ["nbf%d" % q for q in range(4)]
+    XW = ["xw%d" % q for q in range(4)]
 
     iota(T.coli[:, 0:1], [[0, 1]], 0, 1, ["ci0"], 1, False)
     iota(T.dw[:], [[1, 144]], 0, -1, ["dw"], 144)
-    iota(T.tmp[:, 0, :], [[1, 16]], 0, 0, ["m0"], 16)
-    iota(T.tmp[:, 1, :], [[0, 2], [1, 8]], 0, 0, ["m1"], 16)
-    iota(T.tmp[:, 2, :], [[-16, 2], [1, 8]], 18, 0, ["m2"], 16)
-    iota(T.tmpi[:, 0, :], [[1, 2], [0, 8]], 0, 1, ["mi0"], 16, False)
-    iota(T.io4[:, :, 0:n], [[-16, NB], [1, n]], 0, 0, ["io4a"], NB * n)
-    iota(T.io4[:, :, n:SEG], [[0, NB], [0, 2], [1, 16]], 0, 0, ["io4b"], NB * 32)
-    iota(T.io5[:, :, 0:n], [[32, NB], [0, n]], 0, 0, ["io5a"], NB * n)
-    iota(T.io5[:, :, n:n + 16], [[32, NB], [0, 16]], 3072, 0, ["io5b"], NB * 16)
-    ts(T.coli[:, 1:2], T.coli[:, 0:1], 15, None, OP.bitwise_and, None, ["ci0"], ["ci1"])
-    ts(T.coli[:, 2:3], T.coli[:, 0:1], 1, None, OP.bitwise_and, None, ["ci0"], ["ci2"])
-    cp(C("p16"), T.coli[:, 1:2], ["ci1"], ["p16"])
-    cp(C("odd"), T.coli[:, 2:3], ["ci2"], ["odd"])
-    ts(C("p0"), C("p16"), 0.0, None, OP.is_equal, None, ["p16"], ["p0"])
+    iota(T.jj[:], [[0, NM // 16], [1, 16]], 0, 0, ["jj"], NM)
+    iota(T.wt[:, 0, :, :], [[8, 2], [0, 2], [1, 8]], 0, 0, ["w0"], 32)
+    iota(T.wt[:, 1, :, :], [[0, 2], [1, 2], [0, 8]], 0, 0, ["w1"], 32)
+    iota(T.li[:, 0:12], [[1, 12]], 0, 0, ["li0"], 12, False)
+    iota(T.j3[:, 0:12], [[16, 12]], 15, 0, ["j3"], 12)
+    iota(T.keep[:], [[0, P // 16], [8192, 16]], 0, 0, ["keep"], P)
+    c15 = lambda m, k=15: T.h16[:, H16.index(m), k:k + 1]
+    im = H16.index("nOne")
+    iota(T.h16[:, im:im + 3, :], [[-39, 3], [0, 16]], -1, 0, ["hnOne", "hna1", "hn8192"], 48)
+    iota(hs("n8192"), [[0, 16]], -8192, 0, ["hn8192"], 16)
+    iota(hs("K15"), [[0, 16]], 0, 0, ["hK15"], 16)
+    iota(c15("K15"), [[0, 1]], 2032, 0, ["hK15"], 1)
+    iota(T.o32[:], [[0, 128]], 1, 0, ["o32"], 128)
+    for k, m in enumerate((15, 1, 7)):
+        ts(T.coli[:, k + 1:k + 2], T.coli[:, 0:1], m, None, OP.bitwise_and, None, ["ci0"], ["ci%d" % (k + 1)])
+    cp(T.col[:, 0:3], T.coli[:, 1:4], ["ci1", "ci2", "ci3"], ["p16", "odd", "p8"])
     ts(C("p15"), C("p16"), 15.0, None, OP.is_equal, None, ["p16"], ["p15"])
-    for name, src, a, b in (("t1c", "odd", 8, 16), ("tdw", "p15", -1 / 256, 2 / 256), ("zc", "p15", -255 / 256, -1 / 256), ("zoff", "p15", -2047, 0),
-                            ("dabs", "p15", -2040, 0), ("ndb", "p15", 1027, 191.75), ("lnb", "p15", -47872, -192),
-                            ("xwb", "p15", -1792, 0), ("ub", "p15", -1, 1), ("zb", "p15", -2047, -48), ("zo", "p15", 2047, 0),
-                            ("l15", "p15", 257, -1), ("s64", "p15", -64, 64), ("p08", "p0", 8, 0), ("p192", "p0", 192, 0),
-                            ("p33", "p0", 33, 0), ("m4096", "p0", 0, -4096),
-                            ("k0", "p0", -504, 0), ("hH", "p16", 2, 0), ("l64", "p15", 64, 0), ("ln16", "p15", -16, 0)):
+    ts(C("bdb"), C("p16"), 14.0, 100.0, OP.is_equal, OP.mult, ["p16"], ["bdb"])
+    for name, src, a, b in (("t1c", "odd", 8, 16), ("tdw", "p15", 3, -2), ("zc", "p15", -257, 1), ("zoff", "p15", 2032, 0),
+                            ("dabs", "p15", 2032 + 2033 / 256, 0), ("ndb", "p15", -1016 + 2033 / 512, 191.75),
+                            ("lnb", "p15", -53873, -192), ("xwb", "p15", -2033, 0), ("lin", "p15", 2 / 256, -1 / 256),
+                            ("l15", "p15", 255, 1), ("b3", "p15", 0.5 + 2.0 ** -12, -0.5), ("hi", "p16", 1, W + SP),
+                            ("pm", "p16", -1, 15), ("ohb", "p16", -1, 0.5), ("bdb", "bdb", 1, -1.5)):
         act(C(name), C(src), AF.Identity, [src], [name], scale=float(a), bias=float(b))
     ts(T.dw[:], T.dw[:], C("p16"), None, OP.add, None, ["dw", "p16"], ["dw"], 144)
     ts(T.td[:], T.dw[:], 16.0, C("tdw"), OP.is_equal, OP.mult, ["dw", "tdw"], ["td"], 144)
     ts(T.t1[:], T.dw[:], C("t1c"), None, OP.is_equal, None, ["dw", "t1c"], ["t1"], 144)
     ts(T.blk[:], T.dw[:, 0:128:16], 0.0, None, OP.is_equal, None, ["dw"], ["blk"])
-    D16 = T.tmp[:, 0, :]
-    ts(D16, D16, C("p16"), None, OP.subtract, None, ["m0", "p16"], ["m0"])
-    ts(T.tmp[:, 1, :], T.tmp[:, 1, :], C("p16"), None, OP.subtract, None, ["m1", "p16"], ["m1"])
-    for name in ("Id", "Linv"):
-        ts(hs(name), D16, 0.0, None, OP.is_equal, None, ["m0"], ["h" + name])
-    ms(hs("One"), 1.0, ["hOne"])
-    for name, src, s in (("nId", "Id", -1.0), ("Id128", "Id", 128.0), ("Id256", "Id", 256.0),
-                         ("Id4096", "Id", 4096.0), ("Id64s", "Id", "s64"), ("One4096", "One", 4096.0), ("Nr", "One", -3072.0),
-                         ("K0", "One", "k0"), ("Zc", "One", "zc"),
-                         ("L64", "One", "l64"), ("Ln16", "One", "ln16")):
-        if s in CN:
-            act(hs(name), hs(src), AF.Identity, ["h" + src, s], ["h" + name], scale=C(s))
+    ts(T.j2[:], T.jj[:], C("p16"), None, OP.subtract, None, ["jj", "p16"], ["j2"], NM)
+    D16 = T.j2[:, 0:16]
+    for name in ("Id", "L", "Linv"):
+        ts(hs(name), D16, 0.0, None, OP.is_equal, None, ["j2"], ["h" + name])
+    act(hs("One"), D16, AF.Sigmoid, ["j2"], ["hOne"], 1600, scale=0.0, bias=1000.0)
+    for name, src, a, b in (("nId", "Id", -1.0, 0), ("nOH", "Id", -4096.0, 0), ("I8192", "Id", 8192.0, 0), ("OHm", "Id", 4096.0, -4096.0),
+                            ("n256", "Id", -256.0, 0), ("eId", "Id", 2.0 ** -12, 0), ("B3", "Id", "b3", 0), ("A3", "Id", 1.0, -1.0),
+                            ("Zc", "One", "zc", 0)):
+        if a in CN:
+            act(hs(name), hs(src), AF.Identity, ["h" + src, a], ["h" + name], scale=C(a))
         else:
-            act(hs(name), hs(src), AF.Identity, ["h" + src], ["h" + name], scale=s)
-    ms(T.h16[:, H16.index("Linv"), 15:16], 1.0 / 256, ["hLinv"])
-    ts(hs("Tri"), D16, 0.0, None, OP.is_gt, None, ["m0"], ["hTri"])
-    ts(T.tmp[:, 3, :], D16, 0.0, 4096.0, OP.is_equal, OP.mult, ["m0"], ["m3"])
-    ts(T.tmp[:, 4, :], D16, -1.0, 4096.0, OP.is_equal, OP.mult, ["m0"], ["m4"])
-    tt(hs("OH4"), T.tmp[:, 3, :], T.tmp[:, 4, :], OP.subtract, ["m3", "m4"], ["hOH4"])
-    tt(hs("nOH4"), T.tmp[:, 4, :], T.tmp[:, 3, :], OP.subtract, ["m3", "m4"], ["hnOH4"])
-    io, im = H16.index("OH4"), H16.index("M")
-    tt(T.h16[:, im, 1:16], T.h16[:, io, 1:16], T.h16[:, io, 0:15], OP.add, ["hOH4"], ["hM"])
-    cp(T.h16[:, im, 0:1], T.h16[:, io, 0:1], ["hOH4", "hM"], ["hM"])
-    ts(T.tmpi[:, 1, :], T.tmpi[:, 0, :], 1, None, OP.bitwise_and, None, ["mi0"], ["mi1"])
-    ts(T.tmp[:, 5, :], T.tmpi[:, 1, :], 32.0, -17.0, OP.mult, OP.add, ["mi1"], ["m5"])
-    ts(T.tmp[:, 2, :], T.tmp[:, 2, :], C("p0"), None, OP.mult, None, ["m2", "p0"], ["m2"])
-    tt(T.tmp[:, 5, :], T.tmp[:, 5, :], T.tmp[:, 2, :], OP.add, ["m5", "m2"], ["m5"])
-    ts(T.tmp[:, 6, :], T.tmp[:, 1, :], -1.0, 16.0, OP.is_equal, OP.mult, ["m1"], ["m6"])
-    ts(T.tmp[:, 7, :], T.tmp[:, 1, :], -9.0, 16.0, OP.is_equal, OP.mult, ["m1"], ["m7"])
-    tt(hs("kA"), T.tmp[:, 5, :], T.tmp[:, 6, :], OP.add, ["m5", "m6"], ["hkA"])
-    ts(T.tmp[:, 7, :], T.tmp[:, 7, :], C("p08"), None, OP.add, None, ["m7", "p08"], ["m7"])
-    tt(hs("kB"), T.tmp[:, 5, :], T.tmp[:, 7, :], OP.add, ["m5", "m7"], ["hkB"])
-    ts(hs("kC"), hs("OH4"), -1.0 / 32, C("p192"), OP.mult, OP.add, ["hOH4", "p192"], ["hkC"])
-    cp(T.h16[:, H16.index("kC"), 15:16], C("p33"), ["p33", "hkC"], ["hkC"])
-    ts(bs("L"), D16, 0.0, None, OP.is_equal, None, ["m0"], ["bL"])
-    cp(T.b16[:, B16.index("L"), 15:16], C("l15"), ["l15", "bL"], ["bL"])
-    ms(bs("nOne"), -1.0, ["bnOne"])
-    ts(bs("Id2m1"), hs("Id"), 2.0, -1.0, OP.mult, OP.add, ["hId"], ["bId2m1"])
-    for gq in range(8):
-        sl = slice(16 * gq, 16 * gq + 16)
-        act(T.bbig[:, :, sl], T.b16[:], AF.Identity, ["blk"] + ["b" + m for m in B16], ["bbig%d" % gq], scale=T.blk[:, gq:gq + 1])
-        ts(T.hbig[:, :, sl], T.h16[:], T.blk[:, gq:gq + 1], None, OP.mult, None, ["blk"] + ["h" + m for m in H16],
-           ["hbig%d" % gq], len(H16) * 8)
-    HB = ["hbig%d" % q for q in range(8)]
-    BB = ["bbig%d" % q for q in range(8)]
-    ts(T.io6[:, :, 0:n], T.io4[:, :, 0:n], C("p16"), 8192.0, OP.is_ge, OP.mult, ["io4a", "p16"], ["io6a"], NB * n // 2)
-    ts(T.io6[:, :, n:SEG], T.io4[:, :, n:SEG], C("p16"), 8192.0, OP.not_equal, OP.mult, ["io4b", "p16"], ["io6b"])
-    act(T.io7[:, :, 0:n + 16], T.io5[:, :, 0:n + 16], AF.Identity, ["io5a", "io5b", "hH"], ["io7a"], NB * (n + 16), bias=C("hH"))
-    ms(T.io7[:, :, n + 16:SEG], float(SP), ["io7b"])
-    for b in range(NB):
-        tt(T.ddc[:, SEG * b:SEG * b + SEG], T.io7[:, b, :], T.io6[:, b, :], OP.add, ["io7a", "io7b", "io6a", "io6b", "ddc"], ["ddc"], SEG)
-        act(T.db[:, 16 * b:16 * b + 16], T.io6[:, 0, n:n + 16], AF.Identity, ["io6b"], ["db%d" % b], scale=-1.0)
-    DB = ["db%d" % b for b in range(NB)]
-    ms(T.keepd[:], 0.0, ["keepd"], NB * SEG)
-    ms(T.keepd[:, 0:NB * SEG:SEG], 65536.0, ["keepd"])
-    ms(T.keep[:], 1.0, ["keep"])
-    ms(T.keep[:, 0:n:16], 0.0, ["keep"])
-    ms(T.o32[:], 1.0 / 32, ["o32"], 128)
+            act(hs(name), hs(src), AF.Identity, ["h" + src], ["h" + name], scale=a, bias=float(b))
+    iota(c15("A3"), [[0, 1]], 0, 0, ["hA3"], 1)
+    cp(c15("L"), C("l15"), ["l15"], ["hL"])
+    cp(c15("Linv"), C("lin"), ["lin"], ["hLinv"])
+    ts(hs("Tri"), D16, 0.0, -2.0, OP.is_gt, OP.mult, ["j2"], ["hTri"])
+    act(tm(2), D16, AF.Abs, ["j2"], ["m2"], bias=-0.5)
+    ts(hs("M"), tm(2), 1.0, 4096.0, OP.is_lt, OP.mult, ["m2"], ["hM"])
+    ts(tm(3), T.wt[:, 0, 0, :], C("p8"), -39.0, OP.is_ge, OP.mult, ["w0", "p8"], ["m3"])
+    act(tm(4), hs("Id"), AF.Identity, ["hId"], ["m4"], scale=72.0, bias=-1.0)
+    tt(hs("G"), tm(3), tm(4), OP.add, ["m3", "m4"], ["hG"])
+    ts(T.wt[:, 1, :, :], T.wt[:, 1, :, :], C("odd"), 2.0 ** -4 - 256, OP.not_equal, OP.mult, ["w1", "odd"], ["w1"])
+    act(T.wt[:, 1, :, :], T.wt[:, 1, :, :], AF.Identity, ["w1"], ["w1"], bias=256.0)
+    ts(T.wt[:, 2, :, :], T.wt[:, 0, :, :], C("p16"), 2.0 ** -6 - 1, OP.is_lt, OP.mult, ["w0", "p16"], ["w2"])
+    act(T.wt[:, 2, :, :], T.wt[:, 2, :, :], AF.Identity, ["w2"], ["w2"], bias=1.0)
+    iw = H16.index("WA")
+    tt(T.h16[:, iw:iw + 2, :], T.wt[:, 1, :, :], T.wt[:, 2, :, :], OP.mult, ["w1", "w2"], ["hWA", "hWB"])
+    for part, (m0, m1) in enumerate(((0, HE), (HE, len(H16)))):
+        for gq in range(8):
+            ts(T.hbig[:, m0:m1, 16 * gq:16 * gq + 16], T.h16[:, m0:m1, :], T.blk[:, gq:gq + 1], None, OP.mult, None,
+               ["blk"] + ["h" + m for m in H16[m0:m1]], ["hb%d_%d" % (part, gq)], (m1 - m0) * 8)
+    HA = ["hb0_%d" % q for q in range(8)]
+    HB = HA + ["hb1_%d" % q for q in range(8)]
+    cp(T.Lb[:], Hm("L"), HA, ["Lb"])
+    act(T.One32[:], Hm("One"), AF.Copy, HA, ["One32"], 128)
+    act(T.Id32[:], Hm("Id"), AF.Copy, HA, ["Id32"], 128)
+    if G2S:
+        act(T.K32[:], Hm("One"), AF.Identity, HA, ["K32"], 128, scale=-522225.0)
+        ts(T.ts1[:], T.dw[:], 16.0, None, OP.is_equal, None, ["dw"], ["ts1"], 144)
+    ts(T.db[:], T.j2[:], 0.0, -8192.0, OP.not_equal, OP.mult, ["j2"], ["db"], NM)
+    ts(T.anti[:], T.jj[:], C("pm"), None, OP.is_equal, None, ["jj", "pm"], ["anti"], NM)
+    act(T.dbr[:], T.anti[:], AF.Identity, ["anti"], ["dbr"], NM, scale=8192.0, bias=-8192.0)
+    ts(T.crev[:], T.j3[:, 0:12], C("p16"), None, OP.subtract, None, ["j3", "p16"], ["crev"])
+    cp(T.cb[:], T.li[:, 0:12], ["li0"], ["cb"])
+    ts(T.j3[:], T.j2[:], 1.0, 2560.0, OP.min, OP.mult, ["j2", "crev"], ["j3"], NM)
+    act(T.cd[:], T.j3[:], AF.Identity, ["j3"], ["cd"], NM, bias=SP - 8192.0)
     cp(T.col[:, CN.index("th0"):CN.index("th0") + 2], T.thi[:], ["thi"], ["th"])
-    ts(C("mb"), C("th1"), -1.0, 1.0, OP.mult, OP.add, ["th"], ["mb"])
+    ts(C("hB"), C("th1"), -256.0 * 1537, 256.0, OP.add, OP.mult, ["th"], ["hB"])
     ts(C("hb0"), C("th0"), -1.0, 0.5, OP.mult, OP.add, ["th"], ["hb0"])
 
     for q in range(4):
         sl = slice(512 * q, 512 * q + 512)
-        pe(grp(ps[q][:, 0:512], [(Bm("L"), T.xdb[:, sl])], 512), BB + ["xdb"], ["P%d" % q], q)
+        pe(grp(ps[q][:, 0:512], [(T.Lb[:], T.xdb[:, sl])], 512), ["Lb", "xdb"], ["P%d" % q], q)
         act(T.xw[:, SP + 512 * q:SP + 512 * q + 512], ps[q][:, 0:512], AF.Identity, ["P%d" % q, "xwb"], ["xw%d" % q], 512, q, bias=C("xwb"))
 
-    cp(T.vl[:], T.pvi[:], ["pvi"], ["vl%d" % c for c in range(NC)])
-    cp(T.vu[:], T.pvi[:], ["pvi"], ["vu%d" % c for c in range(NC)])
-    for c in reversed(range(NC)):
-        ts(T.land[:, 0, c, 0:n], T.pzb[:, n * c:n * c + n], C("zoff"), None, OP.add, None, ["pzb", "zoff"], ["z0_%d" % c])
-        for b in range(NB):
-            k = NB * c + b
-            act(T.pvx[:, 16 * k:16 * k + 16], hs("Id"), AF.Identity, ["hId", "vl%d" % c], ["pvx%d" % k], scale=T.vl[:, k:k + 1])
-        pe(grp(ps[5][:, 384:448], [(Hm("One"), T.pvx[:, n * c:n * c + n])], n), HB + ["pvx%d" % (NB * c + b) for b in range(NB)],
-           ["Pnv"], 5)
-        act(T.land[:, 0, c, n:2 * n], ps[5][:, 384:448], AF.Copy, ["Pnv"], ["v0_%d" % c], n, 5)
+    cp(T.pvf[:, 0:12], T.pvi[:], ["pvi"], ["pvf"])
+    for c, (c0, n) in enumerate(CH):
+        lc = slice(c0 // 16, (c0 + n) // 16)
+        gn = int(GA * n) + 20
+        tt(T.land[:, 0, 2 * c0:2 * c0 + n], T.pvf[:, 0:12].indirect(T.cb[:, lc]), T.anti[:, 0:n], OP.mult, ["pvf", "cb", "anti"],
+           ["v0_%d" % c], gn)
+        ts(T.land[:, 0, 2 * c0 + n:2 * c0 + 2 * n], T.pzb[:].indirect(T.crev[:, lc]), C("zoff"), None, OP.add, None,
+           ["pzb", "crev", "zoff"], ["z0_%d" % c], gn)
 
     rid, pid, _se = topo.addr(dst)
-    eng = topo.engines(core, dst)[:4]
-    mask = sum(1 << e for e in eng)
-    win_n, win_x = T.nbf[:, SP:WX], T.xw[:, SP:WX]
+    eng = topo.engines(core, dst)
+    mask = topo.mask(core, dst)
+    win_x, NBG = T.xw[:, SP:SP + W], NBF
+    turn = [0]
 
-    for t in range(R):
+    def chunk(t, c):
         last = t == R - 1
+        c0, n = CH[c]
+        s = str(c)
+        nb = n // 16
+        sl = slice(c0, c0 + n)
+        wide = lambda buf, m, a=0, b=None: buf[:, m * c0 + a * n:m * c0 + (m if b is None else b) * n]
+        r7 = lambda k, w=1: ps[7][:, NM * k:NM * k + w * n]
+        r5 = lambda k, w=1: ps[5][:, NM * k:NM * k + w * n]
+        vt, z32 = T.land[:, t, 2 * c0:2 * c0 + n], T.land[:, t, 2 * c0 + n:2 * c0 + 2 * n]
+        zn, vn = "z%d_%d" % (t, c), "v%d_%d" % (t, c)
+        lc = slice(c0 // 16, (c0 + n) // 16)
+        l2 = slice(c0 // 8, (c0 + n) // 8, 2)
+        gn = int(GA * n) + 20
+        if t > 0:
+            add("X", 3000, None, ["sent%d_%d" % (t - 1, c)], [zn, vn], kind="r", sem="arr%d" % ((t - 1) * NC + c))
 
-        def chunk(c, t=t, last=last):
-            s = str(c)
-            z, vb = T.land[:, t, c, 0:n], T.land[:, t, c, n:2 * n]
-            zn, vn = "z%d_%d" % (t, c), "v%d_%d" % (t, c)
-            lc = slice(NB * c, NB * c + NB)
-            if t > 0:
-                add("X", 3000, None, ["sent%d_%d" % (t - 1, c)], [zn, vn], kind="r", sem="arr%d" % ((t - 1) * NC + c))
-                pe(grp(ps[5][:, 0:64], [(Hm("Id"), T.db[:]), (Hm("Id"), vb)], n), HB + DB + [vn], ["Pvs"], 5)
-                vop(n, lambda c=c: V.tensor_tensor_scan(T.vsc[:, c, :], T.keep[:], ps[5][:, 0:64], 0.0, OP.mult, OP.max),
-                    ["Pvs", "keep"], ["vsc" + s], 5)
-                cp(T.vu[:, lc], T.vsc[:, c, 15:n:16], ["vsc" + s], ["vu" + s])
-                vcol = lambda b, c=c: T.vsc[:, c, 16 * b + 15:16 * b + 16]
-                vname = "vsc" + s
+        def zcopy(o, a, cols, rd, wr):
+            gop(cols, lambda: g.affine_select(o, a, [[0, cols]], OP.is_ge, 0.0, 0, 0), rd, wr)
+        for j in range(4):
+            zcopy(T.zq[:, 4 * c0 + j:4 * (c0 + n):4], z32, n, [zn], ["zq%d" % j + s])
+        for j in range(4):
+            zcopy(T.zrep[:, 16 * c0 + j:16 * (c0 + n):4], wide(T.zq, 4), 4 * n, ["zq%d" % i + s for i in range(4)], ["zr%d" % j + s])
+        ZR = ["zr%d" % j + s for j in range(4)]
+        z, zz = T.zq[:, 4 * c0:4 * (c0 + n):4], "zq0" + s
+        pe(grp(r7(0), [(T.One32[:], vt, 4)], n) + grp(r7(1), [(Hm("Id"), T.db[:, 0:n]), (T.One32[:], vt, 4)], n),
+           HA + ["One32", "db", vn], ["Q0", "Q1"], 7)
+        scan(T.vsc[:, sl], r7(1), n, ["Q1"], ["vsc" + s], 7)
+        cp(T.vu[:, lc], T.vsc[:, c0 + 15:c0 + n:16], ["vsc" + s], ["vu" + s])
+        tt(T.eq[:, sl], r7(0), T.vsc[:, sl], OP.is_equal, ["Q0", "vsc" + s], ["eq" + s], n, 7)
+        vl_ = T.vu[:, lc]
+        xv, oh, con, aa, sh = T.xv[:, sl], T.oh[:, sl], T.con[:, sl], T.aa[:, sl], T.sh[:, sl]
+        act(xv, win_x.indirect(vl_), AF.Copy, XW + ["vu" + s], ["xv" + s], gn)
+        pe(grp(r7(2), [(Hm("Linv"), xv), (Hm("nId"), z)], n), HA + ["xv" + s, zz], ["Q2"], 7)
+        act(aa, r7(2), AF.Abs, ["Q2", "dabs"], ["aa" + s], n, 7, bias=C("dabs"))
+        act(T.bad[:, sl], aa, AF.Sign, ["bdb", "aa" + s], ["bad" + s], n, bias=C("bdb"))
+        pe(grp(r7(3), [(Hm("Tri"), T.bad[:, sl]), (Hm("Id"), T.bad[:, sl])], n), HA + ["bad" + s], ["Q3"], 7)
+        act(oh, r7(3), AF.Relu, ["Q3", "ohb"], ["oh" + s], n, 7, bias=C("ohb"), scale=0.5)
+        yield
+        win_n, NBF = (T.nbf[:, SP:SP + W], NBG) if t else (T.nbi[:], NBI)
+        cp(T.conu[:, sl], win_n.indirect(vl_), NBF + ["vu" + s], ["conu" + s], gn)
+        act(con, win_n.indirect(vl_), AF.Copy, NBF + ["vu" + s], ["con" + s], gn)
+        h2 = n // 2
+        for j in range(2):
+            o = T.gg[:, 16 * (c0 + h2 * j):16 * (c0 + h2 * j + h2)]
+            src = win_n.indirect(T.conu[:, c0 + h2 * j:c0 + h2 * j + h2])
+            if j in G1V.get(c, ()):
+                cp(o, src, NBF + ["conu" + s], ["gg%d" % j + s], int(GA * 16 * h2) + 20)
             else:
-                vcol = lambda b, c=c: T.vl[:, NB * c + b:NB * c + b + 1]
-                vname = "vl" + s
-            def zcopy(o, a, pat, cols, rd, wr):
-                gop(cols, lambda: g.affine_select(o, a, pat, OP.is_ge, 0.0, 0, 0), rd, wr)
-            for j in range(4):
-                zcopy(T.zq[:, c, j:4 * n:4], z, [[0, n]], n, [zn], ["zq%d" % j + s])
-            for j in range(4):
-                zcopy(T.zrep[:, c, j:16 * n:4], T.zq[:, c, :], [[0, 4 * n]], 4 * n, ["zq%d" % i + s for i in range(4)], ["zr%d" % j + s])
-            ZR = ["zr%d" % j + s for j in range(4)]
-            gn = int(GA * n) + 20
-            vl_ = T.vu[:, lc]
-            cp(T.conu[:, c, :], win_n.indirect(vl_), NBF + ["vu" + s], ["conu" + s], gn)
-            act(T.xv[:, c, :], win_x.indirect(vl_), AF.Copy, XW + ["vu" + s], ["xv" + s], gn)
-            con = T.cf[:, c, 2 * n:3 * n]
-            act(con, win_n.indirect(vl_), AF.Copy, NBF + ["vu" + s], ["con" + s], gn)
-            xv, u = T.xv[:, c, :], T.ul[:, c, :]
-            pe(grp(ps[5][:, 64:128], [(Hm("Linv"), xv), (Hm("nId"), z)], n), HB + ["xv" + s, zn], ["Pd"], 5)
-            act(T.aa[:, c, :], ps[5][:, 64:128], AF.Abs, ["Pd", "dabs"], ["aa" + s], n, 5, bias=C("dabs"))
-            act(T.bad[:, c, :], T.aa[:, c, :], AF.Relu, ["aa" + s], ["bad" + s], n, bias=-1.0)
-            pe(grp(ps[5][:, 192:256], [(Hm("Tri"), T.bad[:, c, :])], n), HB + ["bad" + s], ["Pc"], 5)
-            act(u, ps[5][:, 192:256], AF.Relu, ["Pc", "ub"], ["u" + s], n, 5, bias=C("ub"), scale=-1.0)
-            yield
-            pe(grp(ps[2][:, 128:192], [(Hm("Id"), con), (Hm("OH4"), u)], n)
-               + grp(ps[2][:, 192:256], [(Hm("Id"), con), (Hm("nOH4"), u)], n), HB + ["con" + s, "u" + s], ["Py"], 2)
-            act(T.yy[:, c, :], ps[2][:, 128:192], AF.Relu, ["Py", "m4096"], ["yy" + s], n, 2, bias=C("m4096"))
-            act(T.pre[:, c, :], ps[2][:, 192:256], AF.Relu, ["Py"], ["pre" + s], n, 2)
-            pe(grp(ps[2][:, 256:320], [(Hm("Id"), T.db[:]), (Hm("One"), T.yy[:, c, :])], n), HB + DB + ["yy" + s], ["Pt"], 2)
-            vop(n, lambda c=c: V.tensor_tensor_scan(T.tsc[:, c, :], T.keep[:], ps[2][:, 256:320], 0.0, OP.mult, OP.max),
-                ["Pt", "keep"], ["tsc" + s], 2)
-            cp(T.tu[:, lc], T.tsc[:, c, 15:n:16], ["tsc" + s], ["tu" + s])
-            act(T.xt[:, c, :], win_x.indirect(T.tu[:, lc]), AF.Copy, XW + ["tu" + s], ["xt" + s], gn)
-            pe(grp(ps[2][:, 320:384], [(Hm("Linv"), T.xt[:, c, :]), (Hm("nId"), z)], n), HB + ["xt" + s, zn], ["PdT"], 2)
-            act(T.at[:, c, :], ps[2][:, 320:384], AF.Abs, ["PdT", "dabs"], ["at" + s], n, 2, bias=C("dabs"))
-            pe(grp(ps[2][:, 384:448], [(Hm("One"), T.at[:, c, :])], n), HB + ["at" + s], ["PDT"], 2)
-            hb = "hb%d" % t
-            if last:
-                act(T.sh[:, c, :], ps[2][:, 384:448], AF.Sign, ["PDT", hb], ["sh" + s], n, 2, bias=C(hb))
-            else:
-                act(T.sh[:, c, :], ps[2][:, 384:448], AF.Sign, ["PDT", hb], ["sh" + s, "acc" + s], n + 30, 2, bias=C(hb),
-                    accum_out=T.acc[:, c:c + 1])
-            for b in range(NB):
-                if c in NES:
-                    act(T.ne[:, c, b, :], vb, AF.Abs, [vn, vname], ["ne%d" % b + s], n, bias=vcol(b), scale=-1.0)
+                act(o, src, AF.Copy, NBF + ["conu" + s], ["gg%d" % j + s], int(GA * 16 * h2) + 20)
+        cbk = rbk = 2 + c
+        Cp, PC, PR = ps[cbk], "P%d" % cbk, "R%d" % cbk
+        Rp = lambda a, b: Cp[:, (4 + a) * n:(4 + b) * n]
+        kb = 4 if (n > 64 or c in RLV) else 8
+        for h in range(2):
+            hn = "%d" % h + s
+            names = []
+            for k0 in range(8 * h, 8 * h + 8, kb):
+                bk = turn[0] % 2
+                turn[0] += 1
+                mm = []
+                for k in range(kb):
+                    mm += grp(ps[bk][:, n * k:n * k + n], [(Hm("Id"), T.gg[:, 16 * c0 + k0 + k:16 * (c0 + n):16]), (Hm("M"), oh)], n)
+                pe(mm, HA + ["gg0" + s, "gg1" + s, "oh" + s], ["P%d" % bk], bk)
+                gm = wide(T.gm, 16, k0, k0 + kb)
+                names.append("gm%d_" % k0 + s)
+                if k0 // kb in RLV.get(c, ()):
+                    ts(gm, ps[bk][:, 0:n * kb], -4096.0, 0.0, OP.add, OP.max, ["P%d" % bk], [names[-1]], kb * n, bk)
                 else:
-                    ts(T.ne[:, c, b, :], vb, vcol(b), None, OP.not_equal, None, [vn, vname], ["ne%d" % b + s])
-
-            def dpre(stop=False):
-                mm = [(ps[7][:, 0:NB * SEG], Hm("Id"), T.ddc[:], True, False, NB * SEG)]
-                for b in range(NB):
-                    mm.append((ps[7][:, SEG * b:SEG * b + n], Hm("Id4096"), T.ne[:, c, b, :], False, False, n))
-                    mm.append((ps[7][:, SEG * b + n + 16:SEG * b + SEG], Hm("Id"), T.land[:, t, c, n + 16 * b:n + 16 * b + 16],
-                               False, stop and b == NB - 1, 16))
-                pe(mm, HB + [vn, "ddc"] + ["ne%d" % b + s for b in range(NB)], ["P7"], 7)
-
-            def dscan(lst, name, c=c, s=s, lc=lc):
-                vop(NB * SEG, lambda: V.tensor_tensor_scan(T.dsc[:, c, :], T.keepd[:], ps[7][:, 0:NB * SEG], 0.0, OP.add, OP.min),
-                    ["P7", "keepd"], ["dsc" + s], 7)
-                cp(lst[:, lc], T.dsc[:, c, SEG - 1:NB * SEG:SEG], ["dsc" + s], [name + s])
-            if not last:
-                dpre(True)
-                dscan(T.du, "du")
-                pe(grp(ps[5][:, 128:192], [(Hm("Linv"), xv), (Hm("Id"), z)], n), HB + ["xv" + s, zn], ["Pn"], 5)
-                act(T.nd[:, c, :], ps[5][:, 128:192], AF.Identity, ["Pn", "ndb"], ["nd" + s], n, 5, bias=C("ndb"), scale=0.5)
-                pe(grp(ps[5][:, 256:320], [(Bm("L"), T.nd[:, c, :])], n), BB + ["nd" + s], ["PL"], 5)
-                act(T.ndw[:, c, :], ps[5][:, 256:320], AF.Identity, ["PL", "lnb"], ["ndw" + s], n, 5, bias=C("lnb"))
-            yield
-            first = c == NC - 1
-            h = n // 2
-            if first and HELP & 1:
-                cp(T.gg[:, c, 0:16 * h], win_n.indirect(T.conu[:, c, 0:h]), NBF + ["conu" + s], ["gga" + s], int(GA * 16 * h))
-            else:
-                act(T.gg[:, c, 0:16 * h], win_n.indirect(T.conu[:, c, 0:h]), AF.Copy, NBF + ["conu" + s], ["gga" + s], int(GA * 16 * h))
-            act(T.gg[:, c, 16 * h:16 * n], win_n.indirect(T.conu[:, c, h:n]), AF.Copy, NBF + ["conu" + s], ["ggb" + s], int(GA * 16 * h))
-            rb = 3 + (t * NC + c) % 2
-            Rp, PR = ps[rb], "P%d" % rb
-            for h in range(2):
-                hn = "%d" % h + s
-                parts = [(0, 0, 4), (1, 4, 8)] if first and h == 0 and HELP & 2 else [(h, 0, 8)]
-                for bk, k0, k1 in parts:
-                    mm = []
-                    for k in range(k0, k1):
-                        mm += grp(ps[bk][:, n * k:n * k + n], [(Hm("Id"), T.gg[:, c, 8 * h + k:16 * n:16]), (Hm("M"), u)], n)
-                    pe(mm, HB + ["gga" + s, "ggb" + s, "u" + s], ["P%d" % bk], bk)
-                    gm = T.gm[:, c, 8 * n * h + n * k0:8 * n * h + n * k1]
-                    if k1 == 8 and k0:
-                        ts(gm, ps[bk][:, n * k0:n * k1], -4096.0, 0.0, OP.add, OP.max, ["P%d" % bk], ["gn" + hn], (k1 - k0) * n, bk)
-                    else:
-                        act(gm, ps[bk][:, n * k0:n * k1], AF.Relu, ["P%d" % bk], ["gm" + hn], (k1 - k0) * n, bk, bias=-4096.0)
-                Cp = ps[2][:, n * h:n * h + n]
-                pe(grp(Cp, [(T.t1[:, 16 - k:144 - k], T.gm[:, c, 8 * n * h + n * k:8 * n * h + n * k + n]) for k in range(8)], n),
-                   ["t1", "gm" + hn, "gn" + hn], ["PC%d" % h], 2)
-                cp(T.cu[:, c, n * h:n * h + n], Cp, ["PC%d" % h], ["cu" + hn], n, 2)
-                act(T.cf[:, c, n * h:n * h + n], Cp, AF.Copy, ["PC%d" % h], ["cf" + hn], n, 2)
-                w = n // MXS
-                for j in range(MXS):
-                    tt(T.mx[:, c, h, 16 * w * j:16 * w * j + 16 * w], win_x.indirect(T.cu[:, c, n * h + w * j:n * h + w * j + w]),
-                       T.zrep[:, c, 16 * w * j:16 * w * j + 16 * w], OP.max, XW + ZR + ["cu" + hn], ["mx%d" % j + hn], int(GA * 16 * w))
-                pe(grp(Rp[:, n * h:n * h + n], [(Hm("Zc"), z), (Hm("K0"), u)]
-                       + [(T.td[:, 16 - k:144 - k], T.mx[:, c, h, k:16 * n:16]) for k in range(16)], n),
-                   HB + ["td", zn, "u" + s] + ["mx%d" % j + hn for j in range(MXS)], [PR + "r%d" % h], rb)
-            yield
-            RR = [PR + "r0", PR + "r1"]
-            act(T.dl[:, c, :], Rp[:, 0:2 * n], AF.Identity, RR, ["dl" + s], 2 * n, rb, bias=-0.4375)
-            tt(T.fr[:, c, :], Rp[:, 0:2 * n], T.dl[:, c, :], OP.subtract, RR + ["dl" + s], ["fr" + s], 2 * n, rb)
-            act(T.ad[:, c, :], T.dl[:, c, :], AF.Abs, ["dl" + s], ["ad" + s], 2 * n, bias=-1536.0)
-            if c == 0 or last:
-                dpre()
-            pe(grp(Rp[:, 2 * n:4 * n], [(Hm("Id256"), T.fr[:, c, :]), (Hm("Id"), T.ad[:, c, :])], 2 * n), HB + ["fr" + s, "ad" + s],
-               [PR + "m"], rb)
-            act(T.mm[:, c, :], Rp[:, 2 * n:4 * n], AF.Relu, [PR + "m", "mb"], ["mm" + s], 2 * n, rb, bias=C("mb"))
-            pe(grp(ps[6][:, 0:n], [(Hm("kA"), u), (Hm("Id128"), T.mm[:, c, 0:n])], n)
-               + grp(ps[6][:, n:2 * n], [(Hm("kB"), u), (Hm("Id128"), T.mm[:, c, n:2 * n])], n)
-               + grp(ps[6][:, 2 * n:3 * n], [(Hm("kC"), u), (Hm("Id64s"), T.sh[:, c, :])], n),
-               HB + ["u" + s, "mm" + s, "sh" + s], ["Px"], 6)
-            act(T.ye[:, c, :], ps[6][:, 0:3 * n], AF.Exp, ["Px"], ["ye" + s], 3 * n, 6, scale=-math.log(4.0))
-            mm = []
-            for a in range(3):
-                mm += grp(ps[6][:, 192 + n * a:192 + n * a + n],
-                          [(Bm("Id2m1" if a == b else "nOne"), T.ye[:, c, n * b:n * b + n]) for b in range(3)], n)
-            pe(mm, BB + ["ye" + s], ["Ps"], 6)
-            ts(T.sel[:, c, :], ps[6][:, 192:384], 0.0, None, OP.is_gt, None, ["Ps"], ["sel" + s], 3 * n, 6)
-            cfn = ["sel" + s, "cf0" + s, "cf1" + s, "con" + s]
-            if c in VALS:
-                pe(grp(ps[6][:, 0:3 * n], [(Hm("Id"), T.cf[:, c, :]), (Hm("Id4096"), T.sel[:, c, :])], 3 * n), HB + cfn, ["Px"], 6)
-                act(T.val[:, c, :], ps[6][:, 0:3 * n], AF.Relu, ["Px"], ["val" + s], 3 * n, 6, bias=-4096.0)
-            else:
-                tt(T.val[:, c, :], T.sel[:, c, :], T.cf[:, c, :], OP.mult, cfn, ["val" + s], 4 * n)
-            selc = T.sel[:, c, 2 * n:3 * n]
-            if not (c == 0 or last):
-                dpre()
-            mm = []
-            for b in range(NB):
-                mm.append((ps[7][:, SEG * b:SEG * b + n], Hm("One4096"), selc, False, False, n))
-                mm.append((ps[7][:, SEG * b + n:SEG * b + n + 16], Hm("Nr"), T.sel[:, c, 2 * n + 16 * b:2 * n + 16 * b + 16],
-                           False, b == NB - 1, 16))
-            pe(mm, HB + ["sel" + s, "P7"], ["P7"], 7)
-            dscan(T.nu, "nu")
-            vals = [(Hm("One"), T.val[:, c, n * a:n * a + n]) for a in range(3)]
-            pe(grp(ps[2][:, 448:512], vals + [(Hm("OH4"), u)], n), HB + ["val" + s, "u" + s], ["Ptt"], 2)
-            act(T.tt[:, c, :], ps[2][:, 448:512], AF.Relu, ["Ptt", "m4096"], ["tt" + s], n, 2, bias=C("m4096"))
-            pe(grp(ps[6][:, 384:448], [(Hm("Id"), T.aa[:, c, :]), (Hm("nId"), z), (Hm("L64"), selc)], n),
-               HB + ["aa" + s, zn, "sel" + s], ["Pz1"], 6)
-            act(T.zt[:, c, :], ps[6][:, 384:448], AF.Relu, ["Pz1", "zb"], ["zt" + s], n, 6, bias=C("zb"))
-            pe(grp(ps[6][:, 448:512], [(Hm("Id"), T.zt[:, c, :]), (Hm("Id"), z), (Hm("Ln16"), selc)], n),
-               HB + ["zt" + s, zn, "sel" + s], ["Pz2"], 6)
-            if not last:
-                act(T.send[:, t, c, 0:n], ps[6][:, 448:512], AF.Copy, ["Pz2"], ["sz%d_%d" % (t, c)], n, 6)
-                pe(grp(ps[5][:, 384:448], vals, n), HB + ["val" + s], ["Pnv"], 5)
-                act(T.send[:, t, c, n:2 * n], ps[5][:, 384:448], AF.Copy, ["Pnv"], ["sv%d_%d" % (t, c)], n, 5)
-                add("G", 700, lambda t=t, c=c: g.remote_dma(T.land[:, t + 1, c, :], T.send[:, t, c, :], T.sem["arr%d" % (t * NC + c)],
-                                                           T.sem["sent"], pid, rid, mask),
-                    ["sz%d_%d" % (t, c), "sv%d_%d" % (t, c)], ["sent%d_%d" % (t, c)], kind="s")
-            else:
-                act(T.oz[:, n * c:n * c + n], ps[6][:, 448:512], AF.Identity, ["Pz2", "zo"], ["oz" + s], n, 6, bias=C("zo"))
-                pe(grp(ps[5][:, 0:64], [(Hm("Id"), T.db[:])] + vals, n), HB + DB + ["val" + s], ["Pvs"], 5)
-                vop(n, lambda c=c: V.tensor_tensor_scan(T.tsc[:, c, :], T.keep[:], ps[5][:, 0:64], 0.0, OP.mult, OP.max),
-                    ["Pvs", "keep"], ["tsc" + s], 5)
-                cp(T.ov[:, lc], T.tsc[:, c, 15:n:16], ["tsc" + s], ["ov" + s])
-        gens = [chunk(c) for c in range(NC)]
-        for c in (2, 1, 0, 2, 1, 0, 2, 1, 2, 0, 1, 0):
-            next(gens[c], None)
-        for c in reversed(range(NC)):
-            s = str(c)
-            lc = slice(NB * c, NB * c + NB)
-            tt(T.nbf[:, 0:WX].indirect(T.nu[:, lc]), T.tt[:, c, :], T.pre[:, c, :], OP.add, ["nu" + s, "tt" + s, "pre" + s], NBF,
-               int(SC * n))
-            if not last:
-                cp(T.xw[:, 0:WX].indirect(T.du[:, lc]), T.ndw[:, c, :], ["du" + s, "ndw" + s], XW, int(SC * n))
+                    act(gm, ps[bk][:, 0:n * kb], AF.Relu, ["P%d" % bk], [names[-1]], kb * n, bk, bias=-4096.0)
+            pe(grp(Cp[:, n * h:n * h + n], [(T.t1[:, 16 - k:144 - k], wide(T.gm, 16, 8 * h + k, 8 * h + k + 1)) for k in range(8)], n),
+               ["t1"] + names, [PC + "c%d" % h] + ([PC] if t == 0 and h == 0 else []), cbk)
+            cp(wide(T.cu, 2, h, h + 1), Cp[:, n * h:n * h + n], [PC + "c%d" % h], ["cu" + hn], n, cbk)
+            w = n // MXS
+            mine = []
+            for j in range(MXS):
+                a = 32 * c0 + 16 * n * h + 16 * w * j
+                o, src = T.mx[:, a:a + 16 * w], win_x.indirect(T.cu[:, 2 * c0 + n * h + w * j:2 * c0 + n * h + w * j + w])
+                zr, mn = T.zrep[:, 16 * (c0 + w * j):16 * (c0 + w * j + w)], "mx%d" % j + hn
+                if (h, j) not in G2S.get(c, ()):
+                    tt(o, src, zr, OP.min, XW + ZR + ["cu" + hn], [mn], int(GA * 16 * w) + 20)
+                    mine.append(j)
+                    continue
+                bk = turn[0] % 2
+                turn[0] += 1
+                act(o, src, AF.Copy, XW + ["cu" + hn], [mn], int(GA * 16 * w) + 20)
+                pe(grp(ps[bk][:, 0:16 * w], [(Hm("nId"), zr), (Hm("Linv"), o)], 16 * w), HA + ZR + [mn], ["P%d" % bk], bk)
+                act(o, ps[bk][:, 0:16 * w], AF.Abs, ["P%d" % bk, "dabs"], [mn], 16 * w, bk, bias=C("dabs"))
+                pe(grp(Cp[:, (4 + h) * n + w * j:(4 + h) * n + w * j + w], [(T.K32[:], T.anti[:, 0:w], 4)]
+                       + [(T.ts1[:, 16 - k:144 - k], T.mx[:, a + k:a + 16 * w:16]) for k in range(16)], w),
+                   ["K32", "anti", "ts1", mn], [PR + "r%d%d" % (h, j)], rbk)
+            if mine:
+                i0, m = w * mine[0], w * len(mine)
+                a = 32 * c0 + 16 * n * h + 16 * i0
+                pe(grp(Cp[:, (4 + h) * n + i0:(4 + h) * n + i0 + m], [(Hm("Zc"), T.zq[:, 4 * (c0 + i0):4 * (c0 + i0 + m):4])]
+                       + [(T.td[:, 16 - k:144 - k], T.mx[:, a + k:a + 16 * m:16]) for k in range(16)], m),
+                   HB + ["td", zz] + ["mx%d" % j + hn for j in mine], [PR + "r%d%d" % (h, j) for j in mine], rbk)
+        pe(grp(Cp[:, 2 * n:3 * n], [(Hm("Id"), con)], n) + grp(Cp[:, 3 * n:4 * n], [(Hm("Id"), aa), (Hm("nId"), z), (Hm("K15"), oh)], n)
+           + grp(Rp(2, 3), [(Hm("WA"), oh)], n) + grp(Rp(3, 4), [(Hm("WB"), oh)], n),
+           HB + ["con" + s, "aa" + s, zz, "oh" + s, PC], [PC + "c2"], cbk)
+        yield
+        dl, ad, ww, sel, val = wide(T.dl, 2), wide(T.ad, 2), wide(T.ww, 2), wide(T.sel, 4), wide(T.val, 4)
+        RR = [PR + "r%d%d" % (h, j) for h in range(2) for j in range(MXS)]
+        act(dl, Rp(0, 2), AF.Identity, RR, ["dl" + s], 2 * n, rbk, scale=1 / 256, bias=1536 + (522225 - 120) / 256)
+        act(wide(T.r32, 2), Rp(0, 2), AF.Identity, RR, ["r32" + s], 2 * n, rbk, bias=522225.0)
+        act(ad, dl, AF.Abs, ["dl" + s], ["ad" + s], 2 * n, bias=-1536.0)
+        pe([(Rp(0, 2), Hm("n256"), dl, True, False, 2 * n), (Rp(0, 1), Hm("n256"), sh, False, False, n),
+            (Rp(1, 2), Hm("n256"), sh, False, False, n), (Rp(0, 2), T.Id32[:], wide(T.r32, 2), False, False, 8 * n)],
+           HB + ["Id32", "sh" + s, "dl" + s, PC + "c2", "r32" + s], RR, rbk)
+        pe([(Rp(0, 2), Hm("Id"), ad, False, True, 2 * n)], RR + ["ad" + s], RR, rbk)
+        act(wide(T.hh, 2), Rp(0, 2), AF.Relu, RR + ["hB"], ["hh" + s], 2 * n, rbk, scale=-256.0, bias=C("hB"))
+        tt(ww, Rp(2, 4), wide(T.hh, 2), OP.min, [PC + "c2", "hh" + s], ["ww" + s], 2 * n, rbk)
+        w0, w1 = wide(T.ww, 2, 0, 1), wide(T.ww, 2, 1, 2)
+        both = [(Hm("nOne"), w0), (Hm("nOne"), w1)]
+        f6 = lambda a, b: ps[6][:, a * n:b * n]
+        pe(grp(f6(2, 3), [(Hm("A3"), oh), (Hm("B3"), sh)] + both, n) + grp(f6(3, 4), [(Hm("eId"), sh)] + both, n)
+           + grp(f6(0, 1), [(Hm("G"), w0), (Hm("nOne"), w1)], n) + grp(f6(1, 2), [(Hm("na1"), w0), (Hm("G"), w1)], n),
+           HB + ["oh" + s, "sh" + s, "ww" + s], ["F0"], 6)
+        act(sel, f6(0, 4), AF.Sigmoid, ["F0"], ["sel" + s], 4 * n, 6, scale=2.0 ** 22, bias=-200.0)
+        tt(val, Cp[:, 0:4 * n], sel, OP.mult, [PC + "c0", PC + "c1", PC + "c2", "sel" + s], ["val" + s], 4 * n, cbk)
+        pe(grp(f6(4, 5), first(c) + [(Hm("n8192"), wide(T.sel, 4, 2, 3))], n), HB + ["cd", "eq" + s, "vsc" + s, "sel" + s], ["F2"], 6)
+        scan(T.nsc[:, sl], f6(4, 5), n, ["F2"], ["nsc" + s], 6)
+        ts(T.nu[:, l2], T.nsc[:, c0 + 15:c0 + n:16], C("hi"), C("p16"), OP.min, OP.max, ["nsc" + s, "hi", "p16"], ["nu" + s])
+        vals = [(Hm("One"), wide(T.val, 4, a, a + 1)) for a in range(3)]
+        pe(grp(Rp(0, 1), [(Hm("OHm"), oh)] + vals, n) + grp(Rp(1, 2), [(Hm("Id"), z), (Hm("Id"), wide(T.val, 4, 3, 4))], n),
+           HB + ["oh" + s, zz, "val" + s], RR, rbk)
+        out = T.send[:, t, 2 * c0:2 * c0 + 2 * n]
+        act(out, Rp(0, 2), AF.Relu, RR, ["out%d" % t + s], 2 * n, rbk)
         if not last:
-            pe(grp(ps[5][:, 448:449], [(T.o32[:], T.acc[:, c:c + 1]) for c in range(NC)], 256),
-               ["o32"] + ["acc%d" % c for c in range(NC)], ["Pa"], 5)
-            ts(T.ai[:, 0:1], ps[5][:, 448:449], 768.0, None, OP.add, None, ["Pa"], ["ai0"], 64, 5)
+            add("G", 700, lambda: g.remote_dma(T.land[:, t + 1, 2 * c0:2 * c0 + 2 * n], out, T.sem["arr%d" % (t * NC + c)],
+                                               T.sem["sent"], pid, rid, mask), ["out%d" % t + s], ["sent%d_%d" % (t, c)], kind="s")
+        else:
+            ts(T.oz[:, sl], T.send[:, t, 2 * c0 + n:2 * c0 + 2 * n].indirect(T.crev[:, 0:nb]), C("zoff"), None, OP.subtract, None,
+               ["out%d" % t + s, "crev", "zoff"], ["oz" + s], gn)
+            pe(grp(r7(0), [(Hm("Id"), T.dbr[:, 0:n])] + vals, n), HA + ["dbr", "val" + s], ["Q0"], 7)
+            scan(T.tsc[:, sl], r7(0), n, ["Q0"], ["tsc" + s], 7)
+            cp(T.ov[:, lc], T.tsc[:, c0 + 15:c0 + n:16], ["tsc" + s], ["ov" + s])
+
+    def first(c):
+        c0, n = CH[c]
+        return [(Hm("Id"), T.cd[:, 0:n]), (Hm("I8192"), T.eq[:, c0:c0 + n]), (Hm("Id"), T.vsc[:, c0:c0 + n])]
+
+    def span(cs):
+        c0, n = CH[cs[-1]][0], sum(CH[c][1] for c in cs)
+        return c0, n, slice(c0, c0 + n), T.zq[:, 4 * c0:4 * (c0 + n):4], lambda *m: [x + str(c) for x in m for c in cs]
+
+    def side(t, cs):
+        c0, n, sl, z, N = span(cs)
+        lc = slice(c0 // 16, (c0 + n) // 16)
+        con, oh, u0, u1 = T.con[:, sl], T.oh[:, sl], ps[5][:, 0:n], ps[5][:, n:2 * n]
+        pe(grp(u0, [(Hm("Id"), con), (Hm("OHm"), oh)], n) + grp(u1, [(Hm("Id"), con), (Hm("nOH"), oh)], n), HA + N("con", "oh"), ["U0", "U1"], 5)
+        act(T.yp[:, 2 * c0:2 * c0 + 2 * n], ps[5][:, 0:2 * n], AF.Relu, ["U0", "U1"], N("yp"), 2 * n, 5)
+        mm = []
+        for c in cs:
+            a, m = CH[c][0] - c0, CH[c][1]
+            PRE[c] = 2 * c0 + n + a
+            mm += grp(ps[5][:, a:a + m], [(Hm("Id"), T.db[:, 0:m]), (T.One32[:], T.yp[:, 2 * c0 + a:2 * c0 + a + m], 4)], m)
+        pe(mm, HA + ["db", "One32"] + N("yp"), ["U0"], 5)
+        scan(T.tsc[:, sl], u0, n, ["U0"], N("tsc"), 5)
+        cp(T.tu[:, lc], T.tsc[:, c0 + 15:c0 + n:16], N("tsc"), N("tu"))
+        act(T.xt[:, sl], win_x.indirect(T.tu[:, lc]), AF.Copy, XW + N("tu"), N("xt"), int(GA * n) + 20)
+        pe(grp(u1, [(Hm("Linv"), T.xt[:, sl]), (Hm("nId"), z)], n), HA + N("zq0", "xt"), ["U1"], 5)
+        act(T.at[:, sl], u1, AF.Abs, ["U1", "dabs"], N("at"), n, 5, bias=C("dabs"))
+        pe(grp(u0, [(Hm("One"), T.at[:, sl])], n), HA + N("at"), ["U0"], 5)
+        hb = "hb%d" % t
+        if t == R - 1:
+            act(T.sh[:, sl], u0, AF.Sign, ["U0", hb], N("sh"), n, 5, bias=C(hb))
+        else:
+            act(T.sh[:, sl], u0, AF.Sign, ["U0", hb], N("sh", "acc"), n + 150, 5, bias=C(hb), accum_out=T.acc[:, cs[0]:cs[0] + 1])
+
+    def digits(cs):
+        c0, n, sl, z, N = span(cs)
+        u = ps[7][:, 256:256 + n]
+        mm = []
+        for c in cs:
+            a, m = CH[c][0] - c0, CH[c][1]
+            mm += grp(ps[7][:, 256 + a:256 + a + m], first(c), m)
+        pe(mm, HA + ["cd"] + N("vsc", "eq"), ["Q4"], 7)
+        scan(T.dsc[:, sl], u, n, ["Q4"], N("dsc"), 7)
+        ts(T.du[:, c0 // 8:(c0 + n) // 8:2], T.dsc[:, c0 + 15:c0 + n:16], C("hi"), C("p16"), OP.min, OP.max, ["hi", "p16"] + N("dsc"), N("du"))
+        pe(grp(u, [(Hm("Linv"), T.xv[:, sl]), (Hm("Id"), z)], n), HA + N("zq0", "xv"), ["Q4"], 7)
+        act(T.nd[:, sl], u, AF.Identity, ["Q4", "ndb"], N("nd"), n, 7, bias=C("ndb"), scale=0.5)
+        pe(grp(u, [(T.Lb[:], T.nd[:, sl])], n), ["Lb"] + N("nd"), ["Q4"], 7)
+        act(T.ndw[:, sl], u, AF.Identity, ["Q4", "lnb"], N("ndw"), n, 7, bias=C("lnb"))
+
+    PRE = {}
+
+    def writes(t, c, digits):
+        c0, n = CH[c]
+        s = str(c)
+        for b in reversed(range(n // 16)):
+            k, a = c0 // 8 + 2 * b, 16 * b
+            if digits:
+                cp(T.xw[:].indirect(T.du[:, k:k + 1]), T.ndw[:, c0 + a:c0 + a + 16], ["du" + s, "ndw" + s], XW, 20 + int(SC * 16), kind="w")
+            else:
+                tt(T.nbf[:].indirect(T.nu[:, k:k + 1]), T.send[:, t, 2 * c0 + a:2 * c0 + a + 16],
+                   T.yp[:, PRE[c] + a:PRE[c] + a + 16], OP.add, ["nu" + s, "out%d" % t + s, "yp" + s], NBF, 20 + int(SC * 16), kind="w")
+
+    gens = [chunk(0, c) for c in range(NC)]
+    for c in range(NC):
+        next(gens[c])
+    for t in range(R):
+        for c in range(NC):
+            next(gens[c])
+        for q in range(4 if t == 0 else 0):
+            gop(512, lambda q=q: g.affine_select(T.nbf[:, SP + 512 * q:SP + 512 * q + 512], T.nbi[:, 512 * q:512 * q + 512], [[0, 512]],
+                                                 OP.is_ge, 0.0, 0, 0), ["nbi%d" % q], ["nbf%d" % q])
+        for cs in SIDE:
+            side(t, cs)
+        for c in range(NC - 1):
+            next(gens[c], None)
+        if t < R - 1:
+            for cs in DIG:
+                digits(cs)
+            for c in range(NC):
+                writes(t, c, True)
+            pe(grp(ps[7][:, 500:501], [(T.o32[:], T.acc[:, cs[0]:cs[0] + 1]) for cs in SIDE], 64),
+               ["o32"] + ["acc%d" % c for c in range(NC)], ["Pa"], 7)
+            ts(T.ai[:, 0:1], ps[7][:, 500:501], 1 / 32, 768.0, OP.mult, OP.add, ["Pa"], ["ai0"], 64, 7)
             ts(T.ai[:, 1:2], T.ai[:, 0:1], 15, None, OP.bitwise_and, None, ["ai0"], ["ai1"])
             ts(C("hb%d" % (t + 1)), T.ai[:, 1:2], -1.0, C("hb0"), OP.mult, OP.add, ["ai1", "hb0"], ["hb%d" % (t + 1)])
-    dma("Y", T.ynb[0:64, :], T.nbf[0:64, SP:WX], NBF, ["o0"], 6000)
-    dma("S", T.ynb[64:128, :], T.nbf[64:128, SP:WX], NBF, ["o1"], 6000)
+        for c in range(NC - 1):
+            writes(t, c, False)
+        nxt = [chunk(t + 1, c) for c in range(NC)] if t < R - 1 else []
+        for c in range(len(nxt) - 1):
+            next(nxt[c])
+        next(gens[NC - 1], None)
+        writes(t, NC - 1, False)
+        if nxt:
+            next(nxt[NC - 1])
+        gens = nxt
+    dma("Y", T.ynb[0:64, :], T.nbf[0:64, SP:SP + W], NBF, ["o0"], 5000)
+    dma("S", T.ynb[64:128, :], T.nbf[64:128, SP:SP + W], NBF, ["o1"], 5000)
     dma("Y", T.yz[:], T.oz[:], ["oz%d" % c for c in range(NC)], ["o2"], 3000)
     dma("Y", T.yv[:], T.ov[:], ["ov%d" % c for c in range(NC)], ["o3"], 3000)
     return ops, len(eng)
@@ -446,7 +479,7 @@ def key(o):
     return o["wr"][0] + "<" + (o["rd"][-1] if o["rd"] else "")
 
 
-def plan(ops):
+def graph(ops):
     N = len(ops)
     deps = [set() for _ in range(N)]
     wr, rd = {}, {}
@@ -468,19 +501,36 @@ def plan(ops):
     for i in range(N):
         for d in deps[i]:
             succ[d].append(i)
-    prio = [0] * N
+    return deps, succ
+
+
+def free(ops, d, i):
+    a, b = ops[d], ops[i]
+    return a["eng"] == b["eng"] and (a["eng"] == "P" or (NOWAW and a["kind"] == "w" and b["kind"] == "w"))
+
+
+def plan(ops, gr=None):
+    N = len(ops)
+    deps0, succ = gr or graph(ops)
+    deps = [set(d) for d in deps0]
+    prio, big = [0] * N, {}
     for i in reversed(range(N)):
-        prio[i] = ops[i]["cost"] + max([prio[j] + HOP for j in succ[i]], default=0)
-    prio = [p + BONUS.get(key(o), 0) for p, o in zip(prio, ops)]
+        o = ops[i]
+        prio[i] = o["cost"] + max([prio[j] + HOP for j in succ[i]], default=0)
+        row = ROW.get(o["eng"] + o["wr"][0][:2])
+        if row:
+            prio[i] = max(prio[i], int(o["cost"] * row) + big.get(o["eng"], 0))
+            big[o["eng"]] = prio[i]
+    prio = [p + BONUS.get(key(o), 0) + (SHORT if o["cost"] < 500 else 0) for p, o in zip(prio, ops)]
     left = [len(d) for d in deps]
     ready = [i for i in range(N) if not left[i]]
-    end, free, bank, order = [0] * N, {}, {}, []
+    end, busy, bank, order, at = [0] * N, {}, {}, [], [0] * N
     while ready:
         def start(i):
             o = ops[i]
-            s = max([end[d] + HOP for d in deps[i]], default=0)
+            s = at[i]
             if o["kind"] != "r":
-                s = max(s, free.get(o["eng"], 0))
+                s = max(s, busy.get(o["eng"], 0))
             b = bank.get(o["bank"])
             if b is not None:
                 s = max(s, end[b] + (HOP if ops[b]["eng"] != o["eng"] else 0))
@@ -488,11 +538,11 @@ def plan(ops):
         st = {i: start(i) for i in ready}
         t0 = min(st.values())
         e0 = ops[min(ready, key=lambda i: (st[i], -prio[i]))]["eng"]
-        i = max([j for j in ready if ops[j]["eng"] == e0 and st[j] <= t0 + SLACK], key=lambda j: (prio[j], -j))
+        i = max([j for j in ready if ops[j]["eng"] == e0 and st[j] <= t0 + SLACK], key=lambda j: (prio[j] - IDLE * (st[j] - t0), -j))
         o = ops[i]
         end[i] = st[i] + o["cost"]
         if o["kind"] != "r":
-            free[o["eng"]] = st[i] + 60 if o["kind"] == "d" else end[i]
+            busy[o["eng"]] = st[i] + 60 if o["kind"] == "d" else end[i]
         if o["bank"] is not None:
             b = bank.get(o["bank"])
             if b is not None and ops[b]["eng"] != o["eng"]:
@@ -501,13 +551,15 @@ def plan(ops):
         order.append(i)
         ready.remove(i)
         for j in succ[i]:
+            at[j] = max(at[j], end[i] + (0 if free(ops, i, j) else HOP))
             left[j] -= 1
             if not left[j]:
                 ready.append(j)
     return order, deps, end
 
 
-SLACK = 60
+SLACK, IDLE, ROW, SHORT = 60, 0, {"Vmx": 1.0}, 2000
+NOWAW = False
 BONUS = {}
 TUNED = []
 
@@ -515,7 +567,8 @@ TUNED = []
 def tune(ops, rounds):
     keys = sorted({key(o) for o in ops})
     steps = (-3000, -1500, -600, -200, 200, 600, 1500, 3000)
-    best, x = max(plan(ops)[2]), 12345
+    gr = graph(ops)
+    best, x = max(plan(ops, gr)[2]), 12345
     for _ in range(rounds):
         old = dict(BONUS)
         x = (x * 1103515245 + 12345) % 2147483648
@@ -524,7 +577,7 @@ def tune(ops, rounds):
             k = keys[(x >> 8) % len(keys)]
             x = (x * 1103515245 + 12345) % 2147483648
             BONUS[k] = BONUS.get(k, 0) + steps[(x >> 16) % 8]
-        e = max(plan(ops)[2])
+        e = max(plan(ops, gr)[2])
         if e <= best:
             best = e
         else:
@@ -542,11 +595,12 @@ def rank_program(g, core, T, topo):
     if not TUNED:
         TUNED.append(tune(ops, ROUNDS))
     order, deps, _end = plan(ops)
+    place = {i: k for k, i in enumerate(order)}
     Q = {"V": g.vector, "S": g.scalar, "P": g.tensor, "G": g, "Y": g.sync}
     need = set()
     for i in order:
         for d in deps[i]:
-            if not (ops[d]["eng"] == "P" and ops[i]["eng"] == "P") and ops[i]["kind"] != "r":
+            if not free(ops, d, i) and ops[i]["kind"] != "r":
                 need.add(d)
     count, tick, know, clock = {}, {}, {q: {} for q in Q}, {}
     for i in order:
@@ -558,11 +612,11 @@ def rank_program(g, core, T, topo):
         q, kn = o["eng"], know[o["eng"]]
         want = {}
         for d in deps[i]:
-            if d in tick and not (ops[d]["eng"] == "P" and q == "P"):
+            if d in tick and not free(ops, d, i):
                 sem, v = tick[d]
                 if v > want.get(sem, (0, 0))[0]:
                     want[sem] = (v, d)
-        for sem, (v, d) in sorted(want.items(), key=lambda kv: -order.index(kv[1][1])):
+        for sem, (v, d) in sorted(want.items(), key=lambda kv: -place[kv[1][1]]):
             if kn.get(sem, 0) < v:
                 Q[q].wait_ge(T.sem[sem], v)
                 kn[sem] = v

@@ -1,17 +1,19 @@
 from concourse.mybir import AluOpType as OP, ActivationFunctionType as AF
 
 W, P, R, STEP = 2048, 192, 3, 3
-CH = [(128, 64), (64, 64), (0, 64)]
+CH = [(0, 64), (64, 64), (128, 64)]
+SEG = (0, 64, 112, 144, 160)
+SG = SEG[4]
 NC = len(CH)
 NM = max(n for _c, n in CH)
-SP = 16
+SP = 192
 WX = W + 2 * SP
-H16 = ["Id", "One", "L", "nId", "Linv", "Tri", "M", "OHm", "nOH", "I8192",
-       "Zc", "n256", "WA", "WB", "G", "nOne", "na1", "n8192", "A3", "B3", "eId", "K15"]
-HE = 10
+H16 = ["Id", "One", "nId", "Linv", "Tri", "M", "OHm", "nOH", "I8192",
+       "Zc", "n256", "WA", "WB", "G", "nOne", "na1", "n8192", "A3", "B3", "eId", "K15", "K0", "K1"]
+HE = 9
 F16, BF, F32, U16 = "float16", "bfloat16", "float32", "uint16"
-CN = ["p16", "odd", "p8", "p15", "bdb", "t1c", "tdw", "zc", "zoff", "dabs", "ndb", "lnb", "xwb", "ohb", "lin", "l15", "b3", "hi",
-      "th0", "th1", "hB", "hb0", "hb1", "hb2", "pm"]
+CN = ["p16", "odd", "p8", "p4", "p15", "bdb", "t1c", "tdw", "zc", "zoff", "dabs", "ndb", "lnb", "xwb", "ohb", "lin", "l15", "b3", "lo",
+      "x1", "x2", "x3", "x4", "x5", "x6", "hB", "hb0", "hb1", "hb2", "pm", "hbc", "hbt"]
 
 
 def _s(cols, dt):
@@ -29,40 +31,54 @@ SCRATCH = {
     "tmp": ("sbuf", [128, 8, 16], F32), "wt": ("sbuf", [128, 3, 2, 16], F32), "li": _s(24, "int32"),
     "cb": _s(12, U16), "crev": _s(12, U16),
     "jj": _s(NM, F32), "j2": _s(NM, F32), "j3": _s(NM, F32), "db": _s(NM, F16), "dbr": _s(NM, F16), "anti": _s(NM, F32),
-    "cd": _s(NM, F16), "keep": _s(P, F32), "r32": _s(2 * P, F32),
+    "cd": _s(SG, F16), "ne": _s(NC * SG, F16), "keepx": _s(640, F32), "hi": _s(16, F32), "xl": _s(10, U16), "keep": _s(P, F32), "r32": _s(2 * P, F32),
     "land": ("sbuf", [128, R, 2 * P], F32), "send": ("sbuf", [128, R, 2 * P], F32),
-    "zrep": _s(16 * P, F16), "zq": _s(4 * P, F16),
-    "vsc": _s(P, F16), "vu": _s(12, U16), "eq": _s(P, F16), "xv": _s(P, F16), "conu": _s(P, U16), "con": _s(P, F16),
+    "zrep": _s(16 * P, F16), "zq": _s(4 * P, F16), "z0": _s(P, F16), "an": _s(P, F16), "ah": _s(2, F16),
+    "vsc": _s(P, F32), "vt": _s(P, F16), "yy": _s(P, F16), "fr": _s(2 * P, F16), "vu": _s(12, U16), "eq": _s(P, F16), "xv": _s(P, F16), "conu": _s(P, U16), "con": _s(P, F16),
     "aa": _s(P, F16), "bad": _s(P, F16), "oh": _s(P, F16), "nd": _s(P, BF), "ndw": _s(P, F32), "yp": _s(2 * P, F32),
     "gg": _s(16 * P, F16), "gm": _s(16 * P, F16), "cu": _s(2 * P, U16), "mx": _s(32 * P, F16),
     "tsc": _s(P, F32), "tu": _s(12, U16), "xt": _s(P, F16), "at": _s(P, F16), "sh": _s(P, F16),
-    "acc": _s(4, F32), "ai": _s(2, "int32"), "dsc": _s(P, F32), "nsc": _s(P, F32), "du": _s(24, U16), "nu": _s(24, U16),
+    "acc": _s(4, F32), "ai": _s(2, "int32"), "dsc": _s(NC * SG, F32), "nsc": _s(NC * SG, F32), "du": _s(16, U16), "nu": _s(16 * NC, U16),
     "dl": _s(2 * P, F16), "ad": _s(2 * P, F16), "hh": _s(2 * P, F16), "ww": _s(2 * P, F16),
     "sel": _s(4 * P, F16), "val": _s(4 * P, F16),
-    "oz": _s(P, BF), "ov": _s(12, F32),
+    "oz": _s(P, BF), "ov": _s(16, F32),
 }
 for _b in range(8):
     SCRATCH["ps%d" % _b] = ("psum", [128, 512], F32)
-NDMA = 16
+NDMA = 24
 SEMAPHORES = (["eV", "eS", "eP", "eG", "sent"] + ["d%d" % k for k in range(NDMA)]
               + ["arr%d" % k for k in range((R - 1) * NC)])
 
-ROUNDS = 4000
+ROUNDS = 2500
 MXS = 2
 G1V = {0: (1,), 1: (0,)}
 RLV = {0: (1,)}
-G2S = {2: ((0, 1),)}
+G2S = {}
 SIDE = [[0], [1, 2]]
 DIG = [[0, 1, 2]]
-HOP, GA, SC = 110, 1.56, 3.8
+FRV, RSP, CUS = (0, 1, 2), 2, ("12",)
+XWV, NEV, NE, ZQS, S16, NS = (3,), (), 4500, (0, 1), False, 17100
+G16 = ("vu2", "conu2", "tu")
+HOP, GA, SC, PEC = 110, 1.56, 3.8, 0.55
 
 
 def build(g, T, topo, core, dst):
-    ops = []
+    ops, tail = [], [0]
     V, S, PE = g.vector, g.scalar, g.tensor
+    due = [None, 0]
+
+    def at(t, x, step=250):
+        due[0], due[1] = t * LEN + x, step
+
+    def nxt_due():
+        d = due[0]
+        if d is not None:
+            due[0] += due[1]
+        return d
 
     def add(eng, cost, fn, rd, wr, bank=None, kind="c", sem=None):
-        ops.append({"eng": eng, "cost": cost, "fn": fn, "rd": rd, "wr": wr, "bank": bank, "kind": kind, "sem": sem})
+        ops.append({"eng": eng, "cost": cost, "fn": fn, "rd": rd, "wr": wr, "bank": bank, "kind": kind, "sem": sem, "tail": tail[0], "due": nxt_due(),
+                    "ind": kind == "w" or wr[0][:2] in ("mx", "gg", "xv", "xt", "co") and bank is None})
 
     def vop(cols, fn, rd, wr, bank=None, kind="c"):
         add("V", 40 + max(64, cols), fn, rd, wr, bank, kind)
@@ -79,7 +95,7 @@ def build(g, T, topo, core, dst):
             for o, l, r, st, sp, _n in mms:
                 last = PE.matmul(o, l, r, st, sp)
             return last
-        add("P", 30 + sum(max(64, m[5]) for m in mms) // 2, fn, rd, wr, bank)
+        add("P", 30 + int(PEC * sum(max(64, m[5]) for m in mms)), fn, rd, wr, bank)
 
     def grp(out, terms, cols, start=True, stop=None):
         stop = start if stop is None else stop
@@ -106,11 +122,20 @@ def build(g, T, topo, core, dst):
     def cp(out, a, rd, wr, cols=64, bank=None, kind="c"):
         vop(cols, lambda: V.tensor_copy(out, a), rd, wr, bank, kind)
 
+    def gcp(out, a, rd, wr, cols):
+        if S16:
+            act(out, a, AF.Copy, rd, wr, cols)
+        else:
+            gop(cols, lambda: g.affine_select(out, a, [[0, cols]], OP.is_ge, 0.0, 0, 0), rd, wr)
+
     def ms(out, c, wr, cols=64, rd=()):
         vop(cols, lambda: V.memset(out, c), list(rd), wr)
 
     def scan(out, src, n, rd, wr, bank):
         vop(n, lambda: V.tensor_tensor_scan(out, T.keep[:, 0:n], src, 0.0, OP.min, OP.max), rd + ["keep"], wr, bank)
+
+    def scanx(out, src, n, rd, wr, bank):
+        vop(n, lambda: V.tensor_tensor_scan(out, T.keepx[:, 0:n], src, 30000.0, OP.min, OP.max), rd + ["keepx"], wr, bank)
 
     def act(out, a, f, rd, wr, cols=64, bank=None, **kw):
         sop(cols, lambda: S.activation(out, a, f, **kw), rd, wr, bank)
@@ -127,12 +152,12 @@ def build(g, T, topo, core, dst):
     C = lambda m: T.col[:, CN.index(m):CN.index(m) + 1]
     tm = lambda k: T.tmp[:, k, :]
 
-    dma("Y", T.xdb[:], T.xd[:], [], ["xdb"], 4200)
+    dma("Y", T.xdb[:], T.xd[:], [], ["xdb"], 3200)
     dma("S", T.pvi[:], T.pv[:], [], ["pvi"], 2600)
     dma("S", T.pzb[:], T.pz[:], [], ["pzb"], 2700)
     dma("S", T.thi[:], T.th[:], [], ["thi"], 2700)
     for q in range(4):
-        dma("Y", T.nbi[:, 512 * q:512 * q + 512], T.nb[:, 512 * q:512 * q + 512], [], ["nbi%d" % q], 5000 + 900 * q)
+        dma("Y", T.nbi[:, 512 * q:512 * q + 512], T.nb[:, 512 * q:512 * q + 512], [], ["nbi%d" % q], 3900 + 700 * q)
     NBI = ["nbi%d" % q for q in range(4)]
     NBF = ["nbf%d" % q for q in range(4)]
     XW = ["xw%d" % q for q in range(4)]
@@ -142,8 +167,8 @@ def build(g, T, topo, core, dst):
     iota(T.jj[:], [[0, NM // 16], [1, 16]], 0, 0, ["jj"], NM)
     iota(T.wt[:, 0, :, :], [[8, 2], [0, 2], [1, 8]], 0, 0, ["w0"], 32)
     iota(T.wt[:, 1, :, :], [[0, 2], [1, 2], [0, 8]], 0, 0, ["w1"], 32)
-    iota(T.li[:, 0:12], [[1, 12]], 0, 0, ["li0"], 12, False)
-    iota(T.j3[:, 0:12], [[16, 12]], 15, 0, ["j3"], 12)
+    iota(T.cb[:], [[-1, 12]], 11, 0, ["cb"], 12)
+    iota(T.j3[:, 0:12], [[-16, 12]], P - 1, 0, ["j3"], 12)
     iota(T.keep[:], [[0, P // 16], [8192, 16]], 0, 0, ["keep"], P)
     c15 = lambda m, k=15: T.h16[:, H16.index(m), k:k + 1]
     im = H16.index("nOne")
@@ -151,17 +176,20 @@ def build(g, T, topo, core, dst):
     iota(hs("n8192"), [[0, 16]], -8192, 0, ["hn8192"], 16)
     iota(hs("K15"), [[0, 16]], 0, 0, ["hK15"], 16)
     iota(c15("K15"), [[0, 1]], 2032, 0, ["hK15"], 1)
+    iota(hs("K0"), [[0, 16]], 3576, 0, ["hK0"], 16)
+    iota(hs("K1"), [[0, 16]], 1536, 0, ["hK1"], 16)
+    RS = 1 / 256
     iota(T.o32[:], [[0, 128]], 1, 0, ["o32"], 128)
-    for k, m in enumerate((15, 1, 7)):
+    for k, m in enumerate((15, 1, 7, 3)):
         ts(T.coli[:, k + 1:k + 2], T.coli[:, 0:1], m, None, OP.bitwise_and, None, ["ci0"], ["ci%d" % (k + 1)])
-    cp(T.col[:, 0:3], T.coli[:, 1:4], ["ci1", "ci2", "ci3"], ["p16", "odd", "p8"])
+    cp(T.col[:, 0:4], T.coli[:, 1:5], ["ci1", "ci2", "ci3", "ci4"], ["p16", "odd", "p8", "p4"])
     ts(C("p15"), C("p16"), 15.0, None, OP.is_equal, None, ["p16"], ["p15"])
-    ts(C("bdb"), C("p16"), 14.0, 100.0, OP.is_equal, OP.mult, ["p16"], ["bdb"])
-    for name, src, a, b in (("t1c", "odd", 8, 16), ("tdw", "p15", 3, -2), ("zc", "p15", -257, 1), ("zoff", "p15", 2032, 0),
-                            ("dabs", "p15", 2032 + 2033 / 256, 0), ("ndb", "p15", -1016 + 2033 / 512, 191.75),
-                            ("lnb", "p15", -53873, -192), ("xwb", "p15", -2033, 0), ("lin", "p15", 2 / 256, -1 / 256),
-                            ("l15", "p15", 255, 1), ("b3", "p15", 0.5 + 2.0 ** -12, -0.5), ("hi", "p16", 1, W + SP),
-                            ("pm", "p16", -1, 15), ("ohb", "p16", -1, 0.5), ("bdb", "bdb", 1, -1.5)):
+    ts(C("bdb"), C("p16"), 13.0, 13 + 1.5 / 64, OP.max, OP.subtract, ["p16"], ["bdb"])
+    for name, src, a, b in (("t1c", "odd", 8, 16), ("tdw", "p15", 3 * RS, -2 * RS), ("zc", "p15", -257 * RS, RS), ("zoff", "p15", 2032, 0),
+                            ("dabs", "p15", 2040, 0), ("ndb", "p15", -1012, 191.75),
+                            ("lnb", "p15", -53888, -192), ("xwb", "p15", -2048, 0), ("lin", "p15", 2 / 256, -1 / 256),
+                            ("l15", "p15", 255, 1), ("b3", "p15", 0.5 + 2.0 ** -12, -0.5), ("lo", "p16", 1, SP - 16),
+                            ("pm", "p16", -8192, 15 * 8192), ("ohb", "p16", -1, 0.5)):
         act(C(name), C(src), AF.Identity, [src], [name], scale=float(a), bias=float(b))
     ts(T.dw[:], T.dw[:], C("p16"), None, OP.add, None, ["dw", "p16"], ["dw"], 144)
     ts(T.td[:], T.dw[:], 16.0, C("tdw"), OP.is_equal, OP.mult, ["dw", "tdw"], ["td"], 144)
@@ -169,10 +197,13 @@ def build(g, T, topo, core, dst):
     ts(T.blk[:], T.dw[:, 0:128:16], 0.0, None, OP.is_equal, None, ["dw"], ["blk"])
     ts(T.j2[:], T.jj[:], C("p16"), None, OP.subtract, None, ["jj", "p16"], ["j2"], NM)
     D16 = T.j2[:, 0:16]
-    for name in ("Id", "L", "Linv"):
+    for name in ("Id", "Linv"):
         ts(hs(name), D16, 0.0, None, OP.is_equal, None, ["j2"], ["h" + name])
-    act(hs("One"), D16, AF.Sigmoid, ["j2"], ["hOne"], 1600, scale=0.0, bias=1000.0)
-    for name, src, a, b in (("nId", "Id", -1.0, 0), ("nOH", "Id", -4096.0, 0), ("I8192", "Id", 8192.0, 0), ("OHm", "Id", 4096.0, -4096.0),
+    ms(tm(0), 1000.0, ["m0"])
+    act(hs("One"), tm(0), AF.Sigmoid, ["m0"], ["hOne"], 1600)
+    gop(128, lambda: g.affine_select(T.Lb[:], T.o32[:], [[-1, 128]], OP.is_equal, 0.0, 0, 1), ["o32"], ["Lb"])
+    ts(T.Lb[:, 15:128:16], T.blk[:], C("l15"), None, OP.mult, None, ["blk", "l15"], ["Lb"])
+    for name, src, a, b in (("nId", "Id", -1.0, 0), ("nOH", "Id", -4096.0, 0), ("I8192", "Id", -8192.0, 0), ("OHm", "Id", 4096.0, -4096.0),
                             ("n256", "Id", -256.0, 0), ("eId", "Id", 2.0 ** -12, 0), ("B3", "Id", "b3", 0), ("A3", "Id", 1.0, -1.0),
                             ("Zc", "One", "zc", 0)):
         if a in CN:
@@ -180,7 +211,6 @@ def build(g, T, topo, core, dst):
         else:
             act(hs(name), hs(src), AF.Identity, ["h" + src], ["h" + name], scale=a, bias=float(b))
     iota(c15("A3"), [[0, 1]], 0, 0, ["hA3"], 1)
-    cp(c15("L"), C("l15"), ["l15"], ["hL"])
     cp(c15("Linv"), C("lin"), ["lin"], ["hLinv"])
     ts(hs("Tri"), D16, 0.0, -2.0, OP.is_gt, OP.mult, ["j2"], ["hTri"])
     act(tm(2), D16, AF.Abs, ["j2"], ["m2"], bias=-0.5)
@@ -200,36 +230,48 @@ def build(g, T, topo, core, dst):
                ["blk"] + ["h" + m for m in H16[m0:m1]], ["hb%d_%d" % (part, gq)], (m1 - m0) * 8)
     HA = ["hb0_%d" % q for q in range(8)]
     HB = HA + ["hb1_%d" % q for q in range(8)]
-    cp(T.Lb[:], Hm("L"), HA, ["Lb"])
-    act(T.One32[:], Hm("One"), AF.Copy, HA, ["One32"], 128)
-    act(T.Id32[:], Hm("Id"), AF.Copy, HA, ["Id32"], 128)
+    if len(FRV) < NC:
+        act(T.Id32[:], Hm("Id"), AF.Copy, HA, ["Id32"], 128)
     if G2S:
-        act(T.K32[:], Hm("One"), AF.Identity, HA, ["K32"], 128, scale=-522225.0)
-        ts(T.ts1[:], T.dw[:], 16.0, None, OP.is_equal, None, ["dw"], ["ts1"], 144)
+        ts(T.ts1[:], T.dw[:], 16.0, RS, OP.is_equal, OP.mult, ["dw"], ["ts1"], 144)
     ts(T.db[:], T.j2[:], 0.0, -8192.0, OP.not_equal, OP.mult, ["j2"], ["db"], NM)
-    ts(T.anti[:], T.jj[:], C("pm"), None, OP.is_equal, None, ["jj", "pm"], ["anti"], NM)
-    act(T.dbr[:], T.anti[:], AF.Identity, ["anti"], ["dbr"], NM, scale=8192.0, bias=-8192.0)
+    ts(T.an[:], T.keep[:], C("pm"), None, OP.is_equal, None, ["keep", "pm"], ["anti"], P)
+    act(T.dbr[:], T.an[:, 0:NM], AF.Identity, ["anti"], ["dbr"], NM, scale=8192.0, bias=-8192.0)
     ts(T.crev[:], T.j3[:, 0:12], C("p16"), None, OP.subtract, None, ["j3", "p16"], ["crev"])
-    cp(T.cb[:], T.li[:, 0:12], ["li0"], ["cb"])
-    ts(T.j3[:], T.j2[:], 1.0, 2560.0, OP.min, OP.mult, ["j2", "crev"], ["j3"], NM)
-    act(T.cd[:], T.j3[:], AF.Identity, ["j3"], ["cd"], NM, bias=SP - 8192.0)
-    cp(T.col[:, CN.index("th0"):CN.index("th0") + 2], T.thi[:], ["thi"], ["th"])
-    ts(C("hB"), C("th1"), -256.0 * 1537, 256.0, OP.add, OP.mult, ["th"], ["hB"])
-    ts(C("hb0"), C("th0"), -1.0, 0.5, OP.mult, OP.add, ["th"], ["hb0"])
+    iota(T.cd[:], [[0, SG]], 4096, 0, ["cd"], SG)
+    ts(tm(5), D16, 1.0, 4096.0 - SP, OP.min, OP.mult, ["j2"], ["m5"])
+    for b in range(4):
+        act(T.cd[:, SEG[b]:SEG[b] + 16], tm(5), AF.Identity, ["m5"], ["cd"], bias=float(SP))
+    iota(tm(6), [[16, 16]], 0, 0, ["m6"], 16)
+    ts(T.hi[:], tm(6), C("p16"), float(W + SP), OP.add, OP.add, ["m6", "p16"], ["hi"])
+    act(tm(7), tm(6), AF.Identity, ["m6", "lo"], ["m7"], scale=-1.0, bias=C("lo"))
+    for name, src, a, b in (("x1", "p4", -8.0, -8.0), ("x2", "x1", "p4", 63.0), ("x3", "p4", 64.0, "x2"), ("x4", "p4", -40.0, "x3"),
+                            ("x5", "p16", 40.0, "x4"), ("x6", "p4", 16.0, "x5")):
+        act(C(name), C(src), AF.Identity, [src] + [x for x in (a, b) if x in CN], [name], scale=C(a) if a in CN else a, bias=C(b) if b in CN else b)
+    act(T.xl[:, 0:1], C("x3"), AF.Identity, ["x3"], ["xl0"])
+    ts(T.xl[:, 2:3], C("x5"), NC * SG - 1.0, None, OP.min, None, ["x5"], ["xl2"])
+    ts(T.xl[:, 8:9], C("x5"), 2 * SG - 1.0, None, OP.min, None, ["x5"], ["xl8"])
+    act(T.xl[:, 4:5], C("x6"), AF.Identity, ["x6"], ["xl4"], bias=-63.0)
+    ts(T.xl[:, 6:7], C("p16"), -16.0, P - 1.0, OP.mult, OP.add, ["p16"], ["xl6"])
+    iota(T.keepx[:], [[0, 640]], 30000, 0, ["keepx"], 640)
+    cp(T.keepx[:].indirect(T.xl[:, 4:5]), tm(7), ["xl4", "m7"], ["keepx"], 80)
+    act(C("hB"), T.thi[:, 1:2], AF.Identity, ["thi"], ["hB"], scale=256.0, bias=-65536.0)
+    act(C("hb0"), T.thi[:, 0:1], AF.Identity, ["thi"], ["hb0"], scale=-1.0, bias=0.5)
+    act(C("hbc"), T.thi[:, 0:1], AF.Identity, ["thi"], ["hbc"], scale=-1.0, bias=0.5 - 768 - 16 * 1536)
 
     for q in range(4):
         sl = slice(512 * q, 512 * q + 512)
         pe(grp(ps[q][:, 0:512], [(T.Lb[:], T.xdb[:, sl])], 512), ["Lb", "xdb"], ["P%d" % q], q)
-        act(T.xw[:, SP + 512 * q:SP + 512 * q + 512], ps[q][:, 0:512], AF.Identity, ["P%d" % q, "xwb"], ["xw%d" % q], 512, q, bias=C("xwb"))
+        o = T.xw[:, SP + 512 * q:SP + 512 * q + 512]
+        if q in XWV:
+            ts(o, ps[q][:, 0:512], C("xwb"), None, OP.add, None, ["P%d" % q, "xwb"], ["xw%d" % q], 512, q)
+        else:
+            act(o, ps[q][:, 0:512], AF.Identity, ["P%d" % q, "xwb"], ["xw%d" % q], 512, q, bias=C("xwb"))
 
     cp(T.pvf[:, 0:12], T.pvi[:], ["pvi"], ["pvf"])
-    for c, (c0, n) in enumerate(CH):
-        lc = slice(c0 // 16, (c0 + n) // 16)
-        gn = int(GA * n) + 20
-        tt(T.land[:, 0, 2 * c0:2 * c0 + n], T.pvf[:, 0:12].indirect(T.cb[:, lc]), T.anti[:, 0:n], OP.mult, ["pvf", "cb", "anti"],
-           ["v0_%d" % c], gn)
-        ts(T.land[:, 0, 2 * c0 + n:2 * c0 + 2 * n], T.pzb[:].indirect(T.crev[:, lc]), C("zoff"), None, OP.add, None,
-           ["pzb", "crev", "zoff"], ["z0_%d" % c], gn)
+    tt(T.vt[:], T.pvf[:, 0:12].indirect(T.cb[:]), T.an[:], OP.mult, ["pvf", "cb", "anti"], ["vt%d" % c for c in range(NC)], int(GA * P) + 20)
+    ts(T.z0[:], T.pzb[:].indirect(T.crev[:]), C("zoff"), None, OP.add, None, ["pzb", "crev", "zoff"], ["z0_%d" % c for c in range(NC)],
+       int(GA * P) + 20)
 
     rid, pid, _se = topo.addr(dst)
     eng = topo.engines(core, dst)
@@ -246,40 +288,49 @@ def build(g, T, topo, core, dst):
         wide = lambda buf, m, a=0, b=None: buf[:, m * c0 + a * n:m * c0 + (m if b is None else b) * n]
         r7 = lambda k, w=1: ps[7][:, NM * k:NM * k + w * n]
         r5 = lambda k, w=1: ps[5][:, NM * k:NM * k + w * n]
-        vt, z32 = T.land[:, t, 2 * c0:2 * c0 + n], T.land[:, t, 2 * c0 + n:2 * c0 + 2 * n]
+        vt, z32 = T.land[:, t, 2 * c0:2 * c0 + n], T.land[:, t, 2 * c0 + n:2 * c0 + 2 * n] if t else T.z0[:, sl]
         zn, vn = "z%d_%d" % (t, c), "v%d_%d" % (t, c)
         lc = slice(c0 // 16, (c0 + n) // 16)
         l2 = slice(c0 // 8, (c0 + n) // 8, 2)
         gn = int(GA * n) + 20
+        at(t, HEAD[c])
         if t > 0:
             add("X", 3000, None, ["sent%d_%d" % (t - 1, c)], [zn, vn], kind="r", sem="arr%d" % ((t - 1) * NC + c))
 
         def zcopy(o, a, cols, rd, wr):
             gop(cols, lambda: g.affine_select(o, a, [[0, cols]], OP.is_ge, 0.0, 0, 0), rd, wr)
-        for j in range(4):
-            zcopy(T.zq[:, 4 * c0 + j:4 * (c0 + n):4], z32, n, [zn], ["zq%d" % j + s])
-        for j in range(4):
-            zcopy(T.zrep[:, 16 * c0 + j:16 * (c0 + n):4], wide(T.zq, 4), 4 * n, ["zq%d" % i + s for i in range(4)], ["zr%d" % j + s])
+        scp = lambda o, a, cols, rd, wr: act(o, a, AF.Copy, rd, wr, cols)
         ZR = ["zr%d" % j + s for j in range(4)]
         z, zz = T.zq[:, 4 * c0:4 * (c0 + n):4], "zq0" + s
-        pe(grp(r7(0), [(T.One32[:], vt, 4)], n) + grp(r7(1), [(Hm("Id"), T.db[:, 0:n]), (T.One32[:], vt, 4)], n),
-           HA + ["One32", "db", vn], ["Q0", "Q1"], 7)
+        for j in range(4):
+            (scp if c in ZQS and t else zcopy)(T.zq[:, 4 * c0 + j:4 * (c0 + n):4], z32, n, [zn], ["zq%d" % j + s])
+            at(t, A0[c] - 4200 + 300 * j, 700)
+        for j in range(4):
+            zcopy(T.zrep[:, 16 * c0 + j:16 * (c0 + n):4], wide(T.zq, 4), 4 * n, ["zq%d" % i + s for i in range(4)], ["zr%d" % j + s])
+        at(t, HEAD[c] - 300)
+        if t:
+            (scp if c in ZQS else zcopy)(T.vt[:, sl], vt, n, [vn], ["vt" + s])
+        pe(grp(r7(1), [(Hm("Id"), T.db[:, 0:n]), (Hm("One"), T.vt[:, sl])], n), HA + ["db", "vt" + s], ["Q1"], 7)
         scan(T.vsc[:, sl], r7(1), n, ["Q1"], ["vsc" + s], 7)
-        cp(T.vu[:, lc], T.vsc[:, c0 + 15:c0 + n:16], ["vsc" + s], ["vu" + s])
-        tt(T.eq[:, sl], r7(0), T.vsc[:, sl], OP.is_equal, ["Q0", "vsc" + s], ["eq" + s], n, 7)
+        (gcp if "vu" + s in G16 else cp)(T.vu[:, lc], T.vsc[:, c0 + 15:c0 + n:16], ["vsc" + s], ["vu" + s], nb)
         vl_ = T.vu[:, lc]
         xv, oh, con, aa, sh = T.xv[:, sl], T.oh[:, sl], T.con[:, sl], T.aa[:, sl], T.sh[:, sl]
         act(xv, win_x.indirect(vl_), AF.Copy, XW + ["vu" + s], ["xv" + s], gn)
         pe(grp(r7(2), [(Hm("Linv"), xv), (Hm("nId"), z)], n), HA + ["xv" + s, zz], ["Q2"], 7)
         act(aa, r7(2), AF.Abs, ["Q2", "dabs"], ["aa" + s], n, 7, bias=C("dabs"))
-        act(T.bad[:, sl], aa, AF.Sign, ["bdb", "aa" + s], ["bad" + s], n, bias=C("bdb"))
+        act(T.bad[:, sl], aa, AF.Sign, ["bdb", "aa" + s], ["bad" + s], n, bias=C("bdb"), scale=1 / 64)
         pe(grp(r7(3), [(Hm("Tri"), T.bad[:, sl]), (Hm("Id"), T.bad[:, sl])], n), HA + ["bad" + s], ["Q3"], 7)
         act(oh, r7(3), AF.Relu, ["Q3", "ohb"], ["oh" + s], n, 7, bias=C("ohb"), scale=0.5)
         yield
         win_n, NBF = (T.nbf[:, SP:SP + W], NBG) if t else (T.nbi[:], NBI)
-        cp(T.conu[:, sl], win_n.indirect(vl_), NBF + ["vu" + s], ["conu" + s], gn)
+        at(t, GG[c] + 900, -1200)
         act(con, win_n.indirect(vl_), AF.Copy, NBF + ["vu" + s], ["con" + s], gn)
+        if "conu" + s in G16:
+            gcp(T.conu[:, sl], con, ["con" + s], ["conu" + s], n)
+        else:
+            cp(T.conu[:, sl], win_n.indirect(vl_), NBF + ["vu" + s], ["conu" + s], gn)
         h2 = n // 2
+        at(t, GG[c], 900 * (c > 0))
         for j in range(2):
             o = T.gg[:, 16 * (c0 + h2 * j):16 * (c0 + h2 * j + h2)]
             src = win_n.indirect(T.conu[:, c0 + h2 * j:c0 + h2 * j + h2])
@@ -291,26 +342,34 @@ def build(g, T, topo, core, dst):
         Cp, PC, PR = ps[cbk], "P%d" % cbk, "R%d" % cbk
         Rp = lambda a, b: Cp[:, (4 + a) * n:(4 + b) * n]
         kb = 4 if (n > 64 or c in RLV) else 8
+        sums, late = [], []
         for h in range(2):
             hn = "%d" % h + s
             names = []
+            at(t, A0[c] - 1800 + 1200 * h, 200)
             for k0 in range(8 * h, 8 * h + 8, kb):
                 bk = turn[0] % 2
                 turn[0] += 1
-                mm = []
-                for k in range(kb):
-                    mm += grp(ps[bk][:, n * k:n * k + n], [(Hm("Id"), T.gg[:, 16 * c0 + k0 + k:16 * (c0 + n):16]), (Hm("M"), oh)], n)
-                pe(mm, HA + ["gg0" + s, "gg1" + s, "oh" + s], ["P%d" % bk], bk)
+                pn = ["P%d" % bk, "P%db" % bk]
+                for q in range(kb // 4):
+                    mm = []
+                    for k in range(4 * q, 4 * q + 4):
+                        mm += grp(ps[bk][:, n * k:n * k + n], [(Hm("M"), oh), (Hm("Id"), T.gg[:, 16 * c0 + k0 + k:16 * (c0 + n):16])], n)
+                    pe(mm, HA + ["gg0" + s, "gg1" + s, "oh" + s], [pn[q]], bk)
                 gm = wide(T.gm, 16, k0, k0 + kb)
                 names.append("gm%d_" % k0 + s)
                 if k0 // kb in RLV.get(c, ()):
-                    ts(gm, ps[bk][:, 0:n * kb], -4096.0, 0.0, OP.add, OP.max, ["P%d" % bk], [names[-1]], kb * n, bk)
+                    ts(gm, ps[bk][:, 0:n * kb], -4096.0, 0.0, OP.add, OP.max, pn, [names[-1]], kb * n, bk)
                 else:
-                    act(gm, ps[bk][:, 0:n * kb], AF.Relu, ["P%d" % bk], [names[-1]], kb * n, bk, bias=-4096.0)
+                    act(gm, ps[bk][:, 0:n * kb], AF.Relu, pn, [names[-1]], kb * n, bk, bias=-4096.0)
             pe(grp(Cp[:, n * h:n * h + n], [(T.t1[:, 16 - k:144 - k], wide(T.gm, 16, 8 * h + k, 8 * h + k + 1)) for k in range(8)], n),
-               ["t1"] + names, [PC + "c%d" % h] + ([PC] if t == 0 and h == 0 else []), cbk)
-            cp(wide(T.cu, 2, h, h + 1), Cp[:, n * h:n * h + n], [PC + "c%d" % h], ["cu" + hn], n, cbk)
+               ["t1", PC + "open"] + names, [PC + "c%d" % h] + ([PC] if t == 0 and h == 0 else []), cbk)
+            if hn in CUS:
+                act(wide(T.cu, 2, h, h + 1), Cp[:, n * h:n * h + n], AF.Copy, [PC + "c%d" % h], ["cu" + hn], n, cbk)
+            else:
+                cp(wide(T.cu, 2, h, h + 1), Cp[:, n * h:n * h + n], [PC + "c%d" % h], ["cu" + hn], n, cbk)
             w = n // MXS
+            at(t, A0[c] + 1800 * h, 900)
             mine = []
             for j in range(MXS):
                 a = 32 * c0 + 16 * n * h + 16 * w * j
@@ -322,31 +381,51 @@ def build(g, T, topo, core, dst):
                     continue
                 bk = turn[0] % 2
                 turn[0] += 1
+                at(t, A0[c] + 1800 * h, 600)
                 act(o, src, AF.Copy, XW + ["cu" + hn], [mn], int(GA * 16 * w) + 20)
-                pe(grp(ps[bk][:, 0:16 * w], [(Hm("nId"), zr), (Hm("Linv"), o)], 16 * w), HA + ZR + [mn], ["P%d" % bk], bk)
-                act(o, ps[bk][:, 0:16 * w], AF.Abs, ["P%d" % bk, "dabs"], [mn], 16 * w, bk, bias=C("dabs"))
-                pe(grp(Cp[:, (4 + h) * n + w * j:(4 + h) * n + w * j + w], [(T.K32[:], T.anti[:, 0:w], 4)]
-                       + [(T.ts1[:, 16 - k:144 - k], T.mx[:, a + k:a + 16 * w:16]) for k in range(16)], w),
-                   ["K32", "anti", "ts1", mn], [PR + "r%d%d" % (h, j)], rbk)
+                pe(grp(ps[bk][:, 0:16 * w], [(Hm("nId"), zr), (Hm("Linv"), o)], 16 * w), HA + ZR + [mn], ["P%d" % bk, "P%db" % bk], bk)
+                act(o, ps[bk][:, 0:16 * w], AF.Abs, ["P%d" % bk, "P%db" % bk, "dabs"], [mn], 16 * w, bk, bias=C("dabs"))
+                late.append((grp(Cp[:, (4 + h) * n + w * j:(4 + h) * n + w * j + w], [(Hm("K1"), T.oh[:, c0 + w * j:c0 + w * j + w])]
+                                 + [(T.ts1[:, 16 - k:144 - k], T.mx[:, a + k:a + 16 * w:16]) for k in range(16)], w),
+                             HB + ["oh" + s, "ts1", mn], [PR + "r%d%d" % (h, j), PC + "open"], rbk))
+                at(t, A0[c] + 1800 * h + 900, 900)
             if mine:
                 i0, m = w * mine[0], w * len(mine)
                 a = 32 * c0 + 16 * n * h + 16 * i0
-                pe(grp(Cp[:, (4 + h) * n + i0:(4 + h) * n + i0 + m], [(Hm("Zc"), T.zq[:, 4 * (c0 + i0):4 * (c0 + i0 + m):4])]
-                       + [(T.td[:, 16 - k:144 - k], T.mx[:, a + k:a + 16 * m:16]) for k in range(16)], m),
-                   HB + ["td", zz] + ["mx%d" % j + hn for j in mine], [PR + "r%d%d" % (h, j) for j in mine], rbk)
+                mm = grp(Cp[:, (4 + h) * n + i0:(4 + h) * n + i0 + m], [(Hm("Zc"), T.zq[:, 4 * (c0 + i0):4 * (c0 + i0 + m):4])]
+                         + [(Hm("K0"), T.oh[:, c0 + i0:c0 + i0 + m])]
+                         + [(T.td[:, 16 - k:144 - k], T.mx[:, a + k:a + 16 * m:16]) for k in range(16)], m)
+                cut = [len(mm) * q // RSP for q in range(RSP + 1)]
+                for q in range(RSP):
+                    sums.append((mm[cut[q]:cut[q + 1]], HB + ["td", zz, "oh" + s] + ["mx%d" % j + hn for j in mine],
+                                 [PR + "r%d%d" % (h, j) for j in mine] + [PC + "open"], rbk))
+        sums[RSP:RSP] = late
+        at(t, A0[c] + 1000, 0)
         pe(grp(Cp[:, 2 * n:3 * n], [(Hm("Id"), con)], n) + grp(Cp[:, 3 * n:4 * n], [(Hm("Id"), aa), (Hm("nId"), z), (Hm("K15"), oh)], n)
            + grp(Rp(2, 3), [(Hm("WA"), oh)], n) + grp(Rp(3, 4), [(Hm("WB"), oh)], n),
-           HB + ["con" + s, "aa" + s, zz, "oh" + s, PC], [PC + "c2"], cbk)
+           HB + ["con" + s, "aa" + s, zz, "oh" + s, PC, PC + "open"], [PC + "c2"], cbk)
+        for q, x in enumerate(sums):
+            at(t, A0[c] + 1900 + (q >= RSP) * 1700 + q)
+            pe(*x)
         yield
         dl, ad, ww, sel, val = wide(T.dl, 2), wide(T.ad, 2), wide(T.ww, 2), wide(T.sel, 4), wide(T.val, 4)
         RR = [PR + "r%d%d" % (h, j) for h in range(2) for j in range(MXS)]
-        act(dl, Rp(0, 2), AF.Identity, RR, ["dl" + s], 2 * n, rbk, scale=1 / 256, bias=1536 + (522225 - 120) / 256)
-        act(wide(T.r32, 2), Rp(0, 2), AF.Identity, RR, ["r32" + s], 2 * n, rbk, bias=522225.0)
-        act(ad, dl, AF.Abs, ["dl" + s], ["ad" + s], 2 * n, bias=-1536.0)
-        pe([(Rp(0, 2), Hm("n256"), dl, True, False, 2 * n), (Rp(0, 1), Hm("n256"), sh, False, False, n),
-            (Rp(1, 2), Hm("n256"), sh, False, False, n), (Rp(0, 2), T.Id32[:], wide(T.r32, 2), False, False, 8 * n)],
-           HB + ["Id32", "sh" + s, "dl" + s, PC + "c2", "r32" + s], RR, rbk)
-        pe([(Rp(0, 2), Hm("Id"), ad, False, True, 2 * n)], RR + ["ad" + s], RR, rbk)
+        tail[0] = 1
+        at(t, A0[c] + TL, 200)
+        act(dl, Rp(0, 2), AF.Identity, RR, ["dl" + s], 2 * n, rbk, bias=-120 / 256)
+        if c in FRV:
+            tt(wide(T.fr, 2), dl, Rp(0, 2), OP.subtract, RR + ["dl" + s], ["fr" + s], 2 * n, rbk)
+            act(ad, dl, AF.Abs, ["dl" + s], ["ad" + s], 2 * n, bias=-1536.0)
+            pe([(Rp(0, 2), Hm("Id"), ad, True, False, 2 * n), (Rp(0, 1), Hm("n256"), sh, False, False, n),
+                (Rp(1, 2), Hm("n256"), sh, False, False, n), (Rp(0, 2), Hm("n256"), wide(T.fr, 2), False, True, 2 * n)],
+               HB + ["sh" + s, "ad" + s, "fr" + s], RR, rbk)
+        else:
+            act(wide(T.r32, 2), Rp(0, 2), AF.Identity, RR, ["r32" + s], 2 * n, rbk, scale=256.0)
+            act(ad, dl, AF.Abs, ["dl" + s], ["ad" + s], 2 * n, bias=-1536.0)
+            pe([(Rp(0, 2), Hm("n256"), dl, True, False, 2 * n), (Rp(0, 1), Hm("n256"), sh, False, False, n),
+                (Rp(1, 2), Hm("n256"), sh, False, False, n), (Rp(0, 2), T.Id32[:], wide(T.r32, 2), False, False, 8 * n)],
+               HB + ["Id32", "sh" + s, "dl" + s, PC + "c2", "r32" + s], RR, rbk)
+            pe([(Rp(0, 2), Hm("Id"), ad, False, True, 2 * n)], RR + ["ad" + s], RR, rbk)
         act(wide(T.hh, 2), Rp(0, 2), AF.Relu, RR + ["hB"], ["hh" + s], 2 * n, rbk, scale=-256.0, bias=C("hB"))
         tt(ww, Rp(2, 4), wide(T.hh, 2), OP.min, [PC + "c2", "hh" + s], ["ww" + s], 2 * n, rbk)
         w0, w1 = wide(T.ww, 2, 0, 1), wide(T.ww, 2, 1, 2)
@@ -357,9 +436,12 @@ def build(g, T, topo, core, dst):
            HB + ["oh" + s, "sh" + s, "ww" + s], ["F0"], 6)
         act(sel, f6(0, 4), AF.Sigmoid, ["F0"], ["sel" + s], 4 * n, 6, scale=2.0 ** 22, bias=-200.0)
         tt(val, Cp[:, 0:4 * n], sel, OP.mult, [PC + "c0", PC + "c1", PC + "c2", "sel" + s], ["val" + s], 4 * n, cbk)
-        pe(grp(f6(4, 5), first(c) + [(Hm("n8192"), wide(T.sel, 4, 2, 3))], n), HB + ["cd", "eq" + s, "vsc" + s, "sel" + s], ["F2"], 6)
-        scan(T.nsc[:, sl], f6(4, 5), n, ["F2"], ["nsc" + s], 6)
-        ts(T.nu[:, l2], T.nsc[:, c0 + 15:c0 + n:16], C("hi"), C("p16"), OP.min, OP.max, ["nsc" + s, "hi", "p16"], ["nu" + s])
+        if c == NC - 1:
+            mm, UU = first(c, 5, 0, True), ["U0", "U1", "U2"]
+            pe(mm[:6], HB + ["cd", "vt" + s] + ["ne%d" % b + s for b in range(4)] + ["hh" + s], UU, 5)
+            pe(mm[6:], ["sel" + s], UU, 5)
+            scanx(T.nsc[:, SG * c:SG * c + SG], ps[5][:, 0:SG], SG, UU, ["nsc" + s], 5)
+            tt(T.nu[:, 16:32], T.nsc[:, SG * c:SG * c + SG].indirect(T.xl[:, 0:1]), T.hi[:], OP.min, ["nsc" + s, "hi", "xl0"], ["nu" + s], 64)
         vals = [(Hm("One"), wide(T.val, 4, a, a + 1)) for a in range(3)]
         pe(grp(Rp(0, 1), [(Hm("OHm"), oh)] + vals, n) + grp(Rp(1, 2), [(Hm("Id"), z), (Hm("Id"), wide(T.val, 4, 3, 4))], n),
            HB + ["oh" + s, zz, "val" + s], RR, rbk)
@@ -369,34 +451,54 @@ def build(g, T, topo, core, dst):
             add("G", 700, lambda: g.remote_dma(T.land[:, t + 1, 2 * c0:2 * c0 + 2 * n], out, T.sem["arr%d" % (t * NC + c)],
                                                T.sem["sent"], pid, rid, mask), ["out%d" % t + s], ["sent%d_%d" % (t, c)], kind="s")
         else:
-            ts(T.oz[:, sl], T.send[:, t, 2 * c0 + n:2 * c0 + 2 * n].indirect(T.crev[:, 0:nb]), C("zoff"), None, OP.subtract, None,
-               ["out%d" % t + s, "crev", "zoff"], ["oz" + s], gn)
+            ts(T.oz[:, P - c0 - n:P - c0], T.send[:, t, 2 * c0 + n:2 * c0 + 2 * n].indirect(T.crev[:, 12 - nb:12]), C("zoff"), None,
+               OP.subtract, None, ["out%d" % t + s, "crev", "zoff"], ["oz" + s], gn)
             pe(grp(r7(0), [(Hm("Id"), T.dbr[:, 0:n])] + vals, n), HA + ["dbr", "val" + s], ["Q0"], 7)
             scan(T.tsc[:, sl], r7(0), n, ["Q0"], ["tsc" + s], 7)
-            cp(T.ov[:, lc], T.tsc[:, c0 + 15:c0 + n:16], ["tsc" + s], ["ov" + s])
+        tail[0] = 0
 
-    def first(c):
+    def same(c):
         c0, n = CH[c]
-        return [(Hm("Id"), T.cd[:, 0:n]), (Hm("I8192"), T.eq[:, c0:c0 + n]), (Hm("Id"), T.vsc[:, c0:c0 + n])]
+        s, a = str(c), 256 + 64 * c
+        pe(grp(ps[7][:, a:a + n], [(Hm("One"), T.vt[:, c0:c0 + n])], n), HA + ["vt" + s], ["Q4" + s], 7)
+        for b in range(4):
+            o, src = T.ne[:, SG * c + SEG[b]:SG * c + SEG[b + 1]], ps[7][:, a + 16 * b:a + n]
+            me = T.vsc[:, c0 + 16 * b + 15:c0 + 16 * b + 16]
+            if c in NEV:
+                ts(o, src, me, None, OP.not_equal, None, ["Q4" + s, "vsc" + s], ["ne%d" % b + s], 64, 7)
+            else:
+                act(o, src, AF.Abs, ["Q4" + s, "vsc" + s], ["ne%d" % b + s], 64, 7, scale=-1.0, bias=me)
+
+    def first(c, bank, a, repaired):
+        c0, n = CH[c]
+        mm = [(ps[bank][:, a:a + SG], Hm("Id"), T.cd[:], True, False, SG)]
+        for b in range(4):
+            mm.append((ps[bank][:, a + SEG[b]:a + SEG[b] + 16], Hm("One"), T.vt[:, c0 + 16 * b:c0 + 16 * b + 16], False, False, 16))
+        mm.append((ps[bank][:, a:a + SG], Hm("I8192"), T.ne[:, SG * c:SG * c + SG], False, not repaired, SG))
+        for b in range(4 if repaired else 0):
+            mm.append((ps[bank][:, a + SEG[b]:a + SEG[b + 1]], Hm("n8192"), T.sel[:, 4 * c0 + 2 * n + 16 * b:4 * c0 + 3 * n], False, b == 3, 64))
+        return mm
 
     def span(cs):
-        c0, n = CH[cs[-1]][0], sum(CH[c][1] for c in cs)
+        c0, n = CH[cs[0]][0], sum(CH[c][1] for c in cs)
         return c0, n, slice(c0, c0 + n), T.zq[:, 4 * c0:4 * (c0 + n):4], lambda *m: [x + str(c) for x in m for c in cs]
 
     def side(t, cs):
         c0, n, sl, z, N = span(cs)
+        at(t, A0[cs[0]] + SD, 400)
         lc = slice(c0 // 16, (c0 + n) // 16)
         con, oh, u0, u1 = T.con[:, sl], T.oh[:, sl], ps[5][:, 0:n], ps[5][:, n:2 * n]
         pe(grp(u0, [(Hm("Id"), con), (Hm("OHm"), oh)], n) + grp(u1, [(Hm("Id"), con), (Hm("nOH"), oh)], n), HA + N("con", "oh"), ["U0", "U1"], 5)
-        act(T.yp[:, 2 * c0:2 * c0 + 2 * n], ps[5][:, 0:2 * n], AF.Relu, ["U0", "U1"], N("yp"), 2 * n, 5)
+        act(T.yy[:, sl], u0, AF.Relu, ["U0"], N("yy"), n, 5)
+        act(T.yp[:, sl], u1, AF.Relu, ["U1"], N("yp"), n, 5)
         mm = []
         for c in cs:
             a, m = CH[c][0] - c0, CH[c][1]
-            PRE[c] = 2 * c0 + n + a
-            mm += grp(ps[5][:, a:a + m], [(Hm("Id"), T.db[:, 0:m]), (T.One32[:], T.yp[:, 2 * c0 + a:2 * c0 + a + m], 4)], m)
-        pe(mm, HA + ["db", "One32"] + N("yp"), ["U0"], 5)
+            PRE[c] = c0 + a
+            mm += grp(ps[5][:, a:a + m], [(Hm("Id"), T.db[:, 0:m]), (Hm("One"), T.yy[:, c0 + a:c0 + a + m])], m)
+        pe(mm, HA + ["db"] + N("yy"), ["U0"], 5)
         scan(T.tsc[:, sl], u0, n, ["U0"], N("tsc"), 5)
-        cp(T.tu[:, lc], T.tsc[:, c0 + 15:c0 + n:16], N("tsc"), N("tu"))
+        (gcp if "tu" in G16 else cp)(T.tu[:, lc], T.tsc[:, c0 + 15:c0 + n:16], N("tsc"), N("tu"), n // 16)
         act(T.xt[:, sl], win_x.indirect(T.tu[:, lc]), AF.Copy, XW + N("tu"), N("xt"), int(GA * n) + 20)
         pe(grp(u1, [(Hm("Linv"), T.xt[:, sl]), (Hm("nId"), z)], n), HA + N("zq0", "xt"), ["U1"], 5)
         act(T.at[:, sl], u1, AF.Abs, ["U1", "dabs"], N("at"), n, 5, bias=C("dabs"))
@@ -410,30 +512,25 @@ def build(g, T, topo, core, dst):
     def digits(cs):
         c0, n, sl, z, N = span(cs)
         u = ps[7][:, 256:256 + n]
-        mm = []
         for c in cs:
-            a, m = CH[c][0] - c0, CH[c][1]
-            mm += grp(ps[7][:, 256 + a:256 + a + m], first(c), m)
-        pe(mm, HA + ["cd"] + N("vsc", "eq"), ["Q4"], 7)
-        scan(T.dsc[:, sl], u, n, ["Q4"], N("dsc"), 7)
-        ts(T.du[:, c0 // 8:(c0 + n) // 8:2], T.dsc[:, c0 + 15:c0 + n:16], C("hi"), C("p16"), OP.min, OP.max, ["hi", "p16"] + N("dsc"), N("du"))
-        pe(grp(u, [(Hm("Linv"), T.xv[:, sl]), (Hm("Id"), z)], n), HA + N("zq0", "xv"), ["Q4"], 7)
-        act(T.nd[:, sl], u, AF.Identity, ["Q4", "ndb"], N("nd"), n, 7, bias=C("ndb"), scale=0.5)
-        pe(grp(u, [(T.Lb[:], T.nd[:, sl])], n), ["Lb"] + N("nd"), ["Q4"], 7)
-        act(T.ndw[:, sl], u, AF.Identity, ["Q4", "lnb"], N("ndw"), n, 7, bias=C("lnb"))
+            pe(first(c, 5, SG * c, False), HA + ["cd", "vt%d" % c] + ["ne%d%d" % (b, c) for b in range(4)], ["U0", "U1", "U%d" % (c + 2)], 5)
+        scanx(T.dsc[:], ps[5][:, 0:NC * SG], NC * SG, ["U0", "U1", "U2", "U3", "U4"], N("dsc"), 5)
+        tt(T.du[:, 0:16], T.dsc[:].indirect(T.xl[:, 2:3]), T.hi[:], OP.min, ["hi", "xl2"] + N("dsc"), N("du"), 64)
+        pe(grp(u, [(Hm("Linv"), T.xv[:, sl]), (Hm("Id"), z)], n), HA + N("zq0", "xv"), N("Q4"), 7)
+        act(T.nd[:, sl], u, AF.Identity, N("Q4") + ["ndb"], N("nd"), n, 7, bias=C("ndb"), scale=0.5)
+        pe(grp(u, [(T.Lb[:], T.nd[:, sl])], n), ["Lb"] + N("nd"), N("Q4"), 7)
+        act(T.ndw[:, sl], u, AF.Identity, N("Q4") + ["lnb"], N("ndw"), n, 7, bias=C("lnb"))
 
     PRE = {}
 
     def writes(t, c, digits):
         c0, n = CH[c]
         s = str(c)
-        for b in reversed(range(n // 16)):
-            k, a = c0 // 8 + 2 * b, 16 * b
-            if digits:
-                cp(T.xw[:].indirect(T.du[:, k:k + 1]), T.ndw[:, c0 + a:c0 + a + 16], ["du" + s, "ndw" + s], XW, 20 + int(SC * 16), kind="w")
-            else:
-                tt(T.nbf[:].indirect(T.nu[:, k:k + 1]), T.send[:, t, 2 * c0 + a:2 * c0 + a + 16],
-                   T.yp[:, PRE[c] + a:PRE[c] + a + 16], OP.add, ["nu" + s, "out%d" % t + s, "yp" + s], NBF, 20 + int(SC * 16), kind="w")
+        if digits:
+            cp(T.xw[:].indirect(T.du[:, 4 * c:4 * c + 4]), T.ndw[:, c0:c0 + n], ["du" + s, "ndw" + s], XW, 20 + int(SC * n), kind="w")
+        else:
+            tt(T.nbf[:].indirect(T.nu[:, (0, 4, 16)[c]:(0, 4, 16)[c] + 4]), T.send[:, t, 2 * c0:2 * c0 + n], T.yp[:, c0:c0 + n], OP.add,
+               ["nu" + s, "out%d" % t + s, "yp" + s], NBF, 20 + int(SC * n), kind="w")
 
     gens = [chunk(0, c) for c in range(NC)]
     for c in range(NC):
@@ -441,37 +538,52 @@ def build(g, T, topo, core, dst):
     for t in range(R):
         for c in range(NC):
             next(gens[c])
+        at(t, 9000)
         for q in range(4 if t == 0 else 0):
             gop(512, lambda q=q: g.affine_select(T.nbf[:, SP + 512 * q:SP + 512 * q + 512], T.nbi[:, 512 * q:512 * q + 512], [[0, 512]],
                                                  OP.is_ge, 0.0, 0, 0), ["nbi%d" % q], ["nbf%d" % q])
         for cs in SIDE:
             side(t, cs)
+        for c in range(NC):
+            at(t, A0[2] + NE, 150)
+            same(c)
         for c in range(NC - 1):
             next(gens[c], None)
         if t < R - 1:
+            at(t, A0[2] - 500, 500)
             for cs in DIG:
                 digits(cs)
+            at(t, A0[2] + WR, 120)
             for c in range(NC):
                 writes(t, c, True)
             pe(grp(ps[7][:, 500:501], [(T.o32[:], T.acc[:, cs[0]:cs[0] + 1]) for cs in SIDE], 64),
                ["o32"] + ["acc%d" % c for c in range(NC)], ["Pa"], 7)
-            ts(T.ai[:, 0:1], ps[7][:, 500:501], 1 / 32, 768.0, OP.mult, OP.add, ["Pa"], ["ai0"], 64, 7)
-            ts(T.ai[:, 1:2], T.ai[:, 0:1], 15, None, OP.bitwise_and, None, ["ai0"], ["ai1"])
-            ts(C("hb%d" % (t + 1)), T.ai[:, 1:2], -1.0, C("hb0"), OP.mult, OP.add, ["ai1", "hb0"], ["hb%d" % (t + 1)])
+            act(T.ah[:, 0:1], ps[7][:, 500:501], AF.Identity, ["Pa"], ["ai0"], 64, 7, scale=1 / 512, bias=1536 + 48 - 15 / 32)
+            act(C("hbt"), ps[7][:, 500:501], AF.Identity, ["Pa", "hbc"], ["ai1"], 64, 7, scale=-1 / 32, bias=C("hbc"))
+            act(C("hb%d" % (t + 1)), T.ah[:, 0:1], AF.Identity, ["ai0", "ai1"], ["hb%d" % (t + 1)], scale=16.0, bias=C("hbt"))
+        at(t, A0[2] + NS, 120)
+        for c in range(NC - 1):
+            pe(first(c, 5, SG * c, True), HB + ["cd", "vt%d" % c] + ["ne%d%d" % (b, c) for b in range(4)] + ["sel%d" % c],
+               ["U0", "U1", "U%d" % (c + 2)], 5)
+        scanx(T.nsc[:, 0:2 * SG], ps[5][:, 0:2 * SG], 2 * SG, ["U0", "U1", "U2", "U3"], ["nsc0", "nsc1"], 5)
+        tt(T.nu[:, 0:16], T.nsc[:, 0:2 * SG].indirect(T.xl[:, 8:9]), T.hi[:], OP.min, ["nsc0", "nsc1", "hi", "xl8"], ["nu0", "nu1"], 64)
         for c in range(NC - 1):
             writes(t, c, False)
         nxt = [chunk(t + 1, c) for c in range(NC)] if t < R - 1 else []
         for c in range(len(nxt) - 1):
             next(nxt[c])
         next(gens[NC - 1], None)
+        at(t, LEN - 1000, 200)
         writes(t, NC - 1, False)
         if nxt:
             next(nxt[NC - 1])
         gens = nxt
+    cp(T.ov[:], T.tsc[:].indirect(T.xl[:, 6:7]), ["xl6"] + ["tsc%d" % c for c in range(NC)], ["ov"])
+    at(R, 0)
     dma("Y", T.ynb[0:64, :], T.nbf[0:64, SP:SP + W], NBF, ["o0"], 5000)
     dma("S", T.ynb[64:128, :], T.nbf[64:128, SP:SP + W], NBF, ["o1"], 5000)
     dma("Y", T.yz[:], T.oz[:], ["oz%d" % c for c in range(NC)], ["o2"], 3000)
-    dma("Y", T.yv[:], T.ov[:], ["ov%d" % c for c in range(NC)], ["o3"], 3000)
+    dma("Y", T.yv[:], T.ov[:, 0:12], ["ov"], ["o3"], 3000)
     return ops, len(eng)
 
 
@@ -501,7 +613,28 @@ def graph(ops):
     for i in range(N):
         for d in deps[i]:
             succ[d].append(i)
-    return deps, succ
+    prio, least = [0] * N, {}
+    for _pass in range(R + 1):
+        big = {}
+        for i in reversed(range(N)):
+            o = ops[i]
+            prio[i] = max(least.get(i, 0), o["cost"] + max([prio[j] + HOP for j in succ[i]], default=0))
+            row = ROW.get(o["eng"] + o["wr"][0][:2])
+            if row:
+                prio[i] = max(prio[i], int(o["cost"] * row) + big.get(o["eng"], 0))
+                big[o["eng"]] = prio[i]
+        seen = {}
+        for i, o in enumerate(ops):
+            seen[o["wr"][0]] = i
+            if o["wr"][0][:3] == "out" and o["wr"][0][4:] in DUE:
+                least[i] = prio[seen[DUE[o["wr"][0][4:]]]]
+    if LEN:
+        zero = max(prio[i] for i in range(N) if ops[i]["wr"][0] == "conu0")
+        for i in reversed(range(N)):
+            d = zero - prio[i] if ops[i]["due"] is None else ops[i]["due"]
+            least[i] = min([d] + [least[j] - ops[i]["cost"] - HOP for j in succ[i]])
+        prio = [-least[i] for i in range(N)]
+    return deps, succ, prio
 
 
 def free(ops, d, i):
@@ -511,17 +644,9 @@ def free(ops, d, i):
 
 def plan(ops, gr=None):
     N = len(ops)
-    deps0, succ = gr or graph(ops)
+    deps0, succ, base = gr or graph(ops)
     deps = [set(d) for d in deps0]
-    prio, big = [0] * N, {}
-    for i in reversed(range(N)):
-        o = ops[i]
-        prio[i] = o["cost"] + max([prio[j] + HOP for j in succ[i]], default=0)
-        row = ROW.get(o["eng"] + o["wr"][0][:2])
-        if row:
-            prio[i] = max(prio[i], int(o["cost"] * row) + big.get(o["eng"], 0))
-            big[o["eng"]] = prio[i]
-    prio = [p + BONUS.get(key(o), 0) + (SHORT if o["cost"] < 500 else 0) for p, o in zip(prio, ops)]
+    prio = [p + BONUS.get(key(o), 0) + (SHORT if o["cost"] < 500 else 0) + TAIL * o["tail"] for p, o in zip(base, ops)]
     left = [len(d) for d in deps]
     ready = [i for i in range(N) if not left[i]]
     end, busy, bank, order, at = [0] * N, {}, {}, [], [0] * N
@@ -558,17 +683,43 @@ def plan(ops, gr=None):
     return order, deps, end
 
 
-SLACK, IDLE, ROW, SHORT = 60, 0, {"Vmx": 1.0}, 2000
+SLACK, IDLE, ROW, SHORT = 60, 0, {"Vmx": 1.0}, 1800
 NOWAW = False
+DUE = {}
+TAIL = 100
 BONUS = {}
 TUNED = []
+
+
+LEN, A0, HEAD, GG, TL, SD, WR = 16300, (4600, 25600, 11800), (-4400, -2400, 300), (6370, 4100, 3200), 12600, 6700, 700
+SEED = 12345
+OTHER = [(200, 0.75, 1.1, 2000), (80, 1.3, 0.9, 4000)]
+
+
+def replay(ops, order, deps, hop, ind, pe, way):
+    end, busy = [0] * len(ops), {}
+    for i in order:
+        o = ops[i]
+        q, c = o["eng"], o["cost"]
+        s = max([end[d] + (0 if free(ops, d, i) else hop) for d in deps[i]], default=0)
+        if o["kind"] == "r":
+            end[i] = s + way
+            continue
+        s = max(s, busy.get(q, 0))
+        end[i] = s + (c * pe if q == "P" else 60 + (c - 60) * ind if o["ind"] else c)
+        busy[q] = s + 60 if o["kind"] == "d" else end[i]
+    return max(end)
 
 
 def tune(ops, rounds):
     keys = sorted({key(o) for o in ops})
     steps = (-3000, -1500, -600, -200, 200, 600, 1500, 3000)
     gr = graph(ops)
-    best, x = max(plan(ops, gr)[2]), 12345
+
+    def length():
+        order, deps, end = plan(ops, gr)
+        return max(end) + sum(replay(ops, order, deps, *m) for m in OTHER)
+    best, x = length(), SEED
     for _ in range(rounds):
         old = dict(BONUS)
         x = (x * 1103515245 + 12345) % 2147483648
@@ -577,13 +728,100 @@ def tune(ops, rounds):
             k = keys[(x >> 8) % len(keys)]
             x = (x * 1103515245 + 12345) % 2147483648
             BONUS[k] = BONUS.get(k, 0) + steps[(x >> 16) % 8]
-        e = max(plan(ops, gr)[2])
+        e = length()
         if e <= best:
             best = e
         else:
             BONUS.clear()
             BONUS.update(old)
     return best
+
+
+def lay(ops, gr, when, models):
+    deps0, succ = gr[0], gr[1]
+    N = len(ops)
+    order = sorted(range(N), key=lambda i: (when[i], i))
+    total, swaps, deps = 0, [], None
+    for hop, ind, pe, way in models:
+        end, by, busy, bank, extra = [0] * N, [None] * N, {}, {}, {}
+        for i in order:
+            o = ops[i]
+            q, c, s, w = o["eng"], o["cost"], 0, None
+            for d in deps0[i]:
+                e = end[d] + (0 if q == "P" == ops[d]["eng"] else hop)
+                if e > s:
+                    s, w = e, (d, 0)
+            if o["kind"] == "r":
+                end[i], by[i] = s + way, w
+                continue
+            b = bank.get(o["bank"])
+            if b is not None and ops[b]["eng"] != q:
+                extra[i] = b
+                if end[b] + hop > s:
+                    s, w = end[b] + hop, (b, 1)
+            if q in busy and busy[q][0] >= s:
+                s, w = busy[q][0], (busy[q][1], 1)
+            end[i], by[i] = s + (c * pe if q == "P" else 60 + (c - 60) * ind if o["ind"] else c), w
+            busy[q] = (s + 60 if o["kind"] == "d" else end[i], i)
+            if o["bank"] is not None:
+                bank[o["bank"]] = i
+        i = end.index(max(end))
+        total += end[i]
+        while by[i]:
+            if by[i][1] and by[i][0] not in deps0[i]:
+                swaps.append((by[i][0], i))
+            i = by[i][0]
+    return total, swaps, order, extra
+
+
+def polish(ops, rounds):
+    gr = graph(ops)
+    order, _deps, end = plan(ops, gr)
+    when = [0] * len(ops)
+    for k, i in enumerate(sorted(order, key=lambda i: end[i] - ops[i]["cost"])):
+        when[i] = float(k)
+    models = [(HOP, 1.0, 1.0, 3000)] + OTHER
+    best, swaps, order, extra = lay(ops, gr, when, models)
+    now, keep, x = best, (best, list(when)), SEED
+    for r in range(rounds):
+        x = (x * 1103515245 + 12345) % 2147483648
+        a, b = swaps[(x >> 8) % len(swaps)]
+        x = (x * 1103515245 + 12345) % 2147483648
+        new = list(when)
+        if (x >> 16) % 2:
+            new[b] = when[a] - 0.001 * (1 + (x >> 8) % 7)
+            todo = [b]
+            while todo:
+                j = todo.pop()
+                for d in gr[0][j]:
+                    if new[d] >= new[j]:
+                        new[d] = new[j] - 0.0001
+                        todo.append(d)
+        else:
+            new[a] = when[b] + 0.001 * (1 + (x >> 8) % 7)
+            todo = [a]
+            while todo:
+                j = todo.pop()
+                for d in gr[1][j]:
+                    if new[d] <= new[j]:
+                        new[d] = new[j] + 0.0001
+                        todo.append(d)
+        e, sw, order, extra = lay(ops, gr, new, models)
+        if e <= now + WARM * (1 - r / rounds):
+            now, swaps = e, sw
+            when = [0] * len(ops)
+            for k, i in enumerate(order):
+                when[i] = float(k)
+            if e < keep[0]:
+                keep = (e, list(when))
+    e, _sw, order, extra = lay(ops, gr, keep[1], models)
+    deps = [set(d) for d in gr[0]]
+    for i, b in extra.items():
+        deps[i].add(b)
+    return order, deps, e
+
+
+WARM = 150
 
 
 def rank_program(g, core, T, topo):
@@ -593,8 +831,9 @@ def rank_program(g, core, T, topo):
     dst = T.cores[(rank + STEP) % len(T.cores)]
     ops, ne = build(g, T, topo, core, dst)
     if not TUNED:
-        TUNED.append(tune(ops, ROUNDS))
-    order, deps, _end = plan(ops)
+        tune(ops, ROUNDS)
+        TUNED.append(polish(ops, 5 * ROUNDS))
+    order, deps, _end = TUNED[0]
     place = {i: k for k, i in enumerate(order)}
     Q = {"V": g.vector, "S": g.scalar, "P": g.tensor, "G": g, "Y": g.sync}
     need = set()

from concourse.mybir import AluOpType as OP, ActivationFunctionType as AF

W, P, R, STEP = 2048, 192, 3, 3
CH = [(0, 64), (64, 64), (128, 64)]
SEG = (0, 64, 112, 144, 160)
SG = SEG[4]
NC = len(CH)
NM = max(n for _c, n in CH)
SP = 192
WX = W + 2 * SP
H16 = ["Id", "One", "nId", "Linv", "Tri", "M", "OHm", "nOH", "I8192",
       "Zc", "n256", "WA", "WB", "G", "nOne", "na1", "n8192", "A3", "B3", "eId", "K15", "K0", "K1"]
HE = 9
F16, BF, F32, U16 = "float16", "bfloat16", "float32", "uint16"
CN = ["p16", "odd", "p8", "p4", "p15", "bdb", "t1c", "tdw", "zc", "zoff", "dabs", "ndb", "lnb", "xwb", "ohb", "lin", "l15", "b3", "lo",
      "x1", "x2", "x3", "x4", "x5", "x6", "hB", "hb0", "hb1", "hb2", "pm", "hbc", "hbt"]


def _s(cols, dt):
    return ("sbuf", [128, cols], dt)


SCRATCH = {
    "nbi": _s(W, "int32"), "nbf": _s(WX, F32), "xdb": _s(W, BF), "xw": _s(WX, F32),
    "pvi": _s(12, "int32"), "pvf": _s(16, F32), "pzb": _s(P, BF), "thi": _s(2, "int32"),
    "h16": ("sbuf", [128, len(H16), 16], F16), "hbig": ("sbuf", [128, len(H16), 128], F16),
    "Lb": _s(128, BF), "One32": _s(128, F32), "Id32": _s(128, F32), "o32": _s(128, F32), "K32": _s(128, F32),
    "ts1": _s(144, F16),
    "dw": _s(144, F32), "t1": _s(144, F16), "td": _s(144, F16),
    "col": _s(32, F32), "coli": _s(8, "int32"), "blk": _s(8, F32),
    "tmp": ("sbuf", [128, 8, 16], F32), "wt": ("sbuf", [128, 3, 2, 16], F32), "li": _s(24, "int32"),
    "cb": _s(12, U16), "crev": _s(12, U16),
    "jj": _s(NM, F32), "j2": _s(NM, F32), "j3": _s(NM, F32), "db": _s(NM, F16), "dbr": _s(NM, F16), "anti": _s(NM, F32),
    "cd": _s(SG, F16), "ne": _s(NC * SG, F16), "keepx": _s(640, F32), "hi": _s(16, F32), "xl": _s(10, U16), "keep": _s(P, F32), "r32": _s(2 * P, F32),
    "land": ("sbuf", [128, R, 2 * P], F32), "send": ("sbuf", [128, R, 2 * P], F32),
    "zrep": _s(16 * P, F16), "zq": _s(4 * P, F16), "z0": _s(P, F16), "an": _s(P, F16), "ah": _s(2, F16),
    "vsc": _s(P, F32), "vt": _s(P, F16), "yy": _s(P, F16), "fr": _s(2 * P, F16), "vu": _s(12, U16), "eq": _s(P, F16), "xv": _s(P, F16), "conu": _s(P, U16), "con": _s(P, F16),
    "aa": _s(P, F16), "bad": _s(P, F16), "oh": _s(P, F16), "nd": _s(P, BF), "ndw": _s(P, F32), "yp": _s(2 * P, F32),
    "gg": _s(16 * P, F16), "gm": _s(16 * P, F16), "cu": _s(2 * P, U16), "mx": _s(32 * P, F16),
    "tsc": _s(P, F32), "tu": _s(12, U16), "xt": _s(P, F16), "at": _s(P, F16), "sh": _s(P, F16),
    "acc": _s(4, F32), "ai": _s(2, "int32"), "dsc": _s(NC * SG, F32), "nsc": _s(NC * SG, F32), "du": _s(16, U16), "nu": _s(16 * NC, U16),
    "dl": _s(2 * P, F16), "ad": _s(2 * P, F16), "hh": _s(2 * P, F16), "ww": _s(2 * P, F16),
    "sel": _s(4 * P, F16), "val": _s(4 * P, F16),
    "oz": _s(P, BF), "ov": _s(16, F32),
}
for _b in range(8):
    SCRATCH["ps%d" % _b] = ("psum", [128, 512], F32)
NDMA = 24
SEMAPHORES = (["eV", "eS", "eP", "eG", "sent"] + ["d%d" % k for k in range(NDMA)]
              + ["arr%d" % k for k in range((R - 1) * NC)])

ROUNDS = 2500
MXS = 2
G1V = {0: (1,), 1: (0,)}
RLV = {0: (1,)}
G2S = {}
SIDE = [[0], [1, 2]]
DIG = [[0, 1, 2]]
FRV, RSP, CUS = (0, 1, 2), 2, ("12",)
XWV, NEV, NE, ZQS, S16, NS = (3,), (), 4500, (0, 1), False, 17100
G16 = ("vu2", "conu2", "tu")
HOP, GA, SC, PEC = 110, 1.56, 3.8, 0.55


def build(g, T, topo, core, dst):
    ops, tail = [], [0]
    V, S, PE = g.vector, g.scalar, g.tensor
    due = [None, 0]

    def at(t, x, step=250):
        due[0], due[1] = t * LEN + x, step

    def nxt_due():
        d = due[0]
        if d is not None:
            due[0] += due[1]
        return d

    def add(eng, cost, fn, rd, wr, bank=None, kind="c", sem=None):
        ops.append({"eng": eng, "cost": cost, "fn": fn, "rd": rd, "wr": wr, "bank": bank, "kind": kind, "sem": sem, "tail": tail[0], "due": nxt_due(),
                    "ind": kind == "w" or wr[0][:2] in ("mx", "gg", "xv", "xt", "co") and bank is None})

    def vop(cols, fn, rd, wr, bank=None, kind="c"):
        add("V", 40 + max(64, cols), fn, rd, wr, bank, kind)

    def sop(cols, fn, rd, wr, bank=None):
        add("S", 60 + max(64, cols), fn, rd, wr, bank)

    def gop(cols, fn, rd, wr):
        add("G", 200 + 2 * cols, fn, rd, wr)

    def pe(mms, rd, wr, bank):
        def fn():
            last = None
            for o, l, r, st, sp, _n in mms:
                last = PE.matmul(o, l, r, st, sp)
            return last
        add("P", 30 + int(PEC * sum(max(64, m[5]) for m in mms)), fn, rd, wr, bank)

    def grp(out, terms, cols, start=True, stop=None):
        stop = start if stop is None else stop
        return [(out, x[0], x[1], start and j == 0, stop and j == len(terms) - 1, cols * (x[2] if len(x) > 2 else 1))
                for j, x in enumerate(terms)]

    nd_ = [0]

    def dma(q, out, in_, rd, wr, cost):
        s = "d%d" % nd_[0]
        nd_[0] += 1
        Q = {"Y": g.sync, "S": g.scalar}[q]
        add(q, cost, lambda: Q.dma_start(out, in_), rd, wr, kind="d", sem=s)

    def ts(out, in0, s1, s2, o0, o1, rd, wr, cols=64, bank=None):
        if o1 is None:
            vop(cols, lambda: V.tensor_scalar(out, in0, s1, None, o0), rd, wr, bank)
        else:
            vop(cols, lambda: V.tensor_scalar(out, in0, s1, s2, o0, o1), rd, wr, bank)

    def tt(out, a, b, o, rd, wr, cols=64, bank=None, kind="c"):
        vop(cols, lambda: V.tensor_tensor(out, a, b, o), rd, wr, bank, kind)

    def cp(out, a, rd, wr, cols=64, bank=None, kind="c"):
        vop(cols, lambda: V.tensor_copy(out, a), rd, wr, bank, kind)

    def gcp(out, a, rd, wr, cols):
        if S16:
            act(out, a, AF.Copy, rd, wr, cols)
        else:
            gop(cols, lambda: g.affine_select(out, a, [[0, cols]], OP.is_ge, 0.0, 0, 0), rd, wr)

    def ms(out, c, wr, cols=64, rd=()):
        vop(cols, lambda: V.memset(out, c), list(rd), wr)

    def scan(out, src, n, rd, wr, bank):
        vop(n, lambda: V.tensor_tensor_scan(out, T.keep[:, 0:n], src, 0.0, OP.min, OP.max), rd + ["keep"], wr, bank)

    def scanx(out, src, n, rd, wr, bank):
        vop(n, lambda: V.tensor_tensor_scan(out, T.keepx[:, 0:n], src, 30000.0, OP.min, OP.max), rd + ["keepx"], wr, bank)

    def act(out, a, f, rd, wr, cols=64, bank=None, **kw):
        sop(cols, lambda: S.activation(out, a, f, **kw), rd, wr, bank)

    def iota(out, pat, base, cm, wr, cols, flt=True):
        if flt:
            gop(cols, lambda: g.iota(out, pat, base, cm, allow_small_or_imprecise_dtypes=True), [], wr)
        else:
            gop(cols, lambda: g.iota(out, pat, base, cm), [], wr)

    ps = [T["ps%d" % b] for b in range(8)]
    hs = lambda m: T.h16[:, H16.index(m), :]
    Hm = lambda m: T.hbig[:, H16.index(m), :]
    C = lambda m: T.col[:, CN.index(m):CN.index(m) + 1]
    tm = lambda k: T.tmp[:, k, :]

    dma("Y", T.xdb[:], T.xd[:], [], ["xdb"], 3200)
    dma("S", T.pvi[:], T.pv[:], [], ["pvi"], 2600)
    dma("S", T.pzb[:], T.pz[:], [], ["pzb"], 2700)
    dma("S", T.thi[:], T.th[:], [], ["thi"], 2700)
    for q in range(4):
        dma("Y", T.nbi[:, 512 * q:512 * q + 512], T.nb[:, 512 * q:512 * q + 512], [], ["nbi%d" % q], 3900 + 700 * q)
    NBI = ["nbi%d" % q for q in range(4)]
    NBF = ["nbf%d" % q for q in range(4)]
    XW = ["xw%d" % q for q in range(4)]

    iota(T.coli[:, 0:1], [[0, 1]], 0, 1, ["ci0"], 1, False)
    iota(T.dw[:], [[1, 144]], 0, -1, ["dw"], 144)
    iota(T.jj[:], [[0, NM // 16], [1, 16]], 0, 0, ["jj"], NM)
    iota(T.wt[:, 0, :, :], [[8, 2], [0, 2], [1, 8]], 0, 0, ["w0"], 32)
    iota(T.wt[:, 1, :, :], [[0, 2], [1, 2], [0, 8]], 0, 0, ["w1"], 32)
    iota(T.cb[:], [[-1, 12]], 11, 0, ["cb"], 12)
    iota(T.j3[:, 0:12], [[-16, 12]], P - 1, 0, ["j3"], 12)
    iota(T.keep[:], [[0, P // 16], [8192, 16]], 0, 0, ["keep"], P)
    c15 = lambda m, k=15: T.h16[:, H16.index(m), k:k + 1]
    im = H16.index("nOne")
    iota(T.h16[:, im:im + 3, :], [[-39, 3], [0, 16]], -1, 0, ["hnOne", "hna1", "hn8192"], 48)
    iota(hs("n8192"), [[0, 16]], -8192, 0, ["hn8192"], 16)
    iota(hs("K15"), [[0, 16]], 0, 0, ["hK15"], 16)
    iota(c15("K15"), [[0, 1]], 2032, 0, ["hK15"], 1)
    iota(hs("K0"), [[0, 16]], 3576, 0, ["hK0"], 16)
    iota(hs("K1"), [[0, 16]], 1536, 0, ["hK1"], 16)
    RS = 1 / 256
    iota(T.o32[:], [[0, 128]], 1, 0, ["o32"], 128)
    for k, m in enumerate((15, 1, 7, 3)):
        ts(T.coli[:, k + 1:k + 2], T.coli[:, 0:1], m, None, OP.bitwise_and, None, ["ci0"], ["ci%d" % (k + 1)])
    cp(T.col[:, 0:4], T.coli[:, 1:5], ["ci1", "ci2", "ci3", "ci4"], ["p16", "odd", "p8", "p4"])
    ts(C("p15"), C("p16"), 15.0, None, OP.is_equal, None, ["p16"], ["p15"])
    ts(C("bdb"), C("p16"), 13.0, 13 + 1.5 / 64, OP.max, OP.subtract, ["p16"], ["bdb"])
    for name, src, a, b in (("t1c", "odd", 8, 16), ("tdw", "p15", 3 * RS, -2 * RS), ("zc", "p15", -257 * RS, RS), ("zoff", "p15", 2032, 0),
                            ("dabs", "p15", 2040, 0), ("ndb", "p15", -1012, 191.75),
                            ("lnb", "p15", -53888, -192), ("xwb", "p15", -2048, 0), ("lin", "p15", 2 / 256, -1 / 256),
                            ("l15", "p15", 255, 1), ("b3", "p15", 0.5 + 2.0 ** -12, -0.5), ("lo", "p16", 1, SP - 16),
                            ("pm", "p16", -8192, 15 * 8192), ("ohb", "p16", -1, 0.5)):
        act(C(name), C(src), AF.Identity, [src], [name], scale=float(a), bias=float(b))
    ts(T.dw[:], T.dw[:], C("p16"), None, OP.add, None, ["dw", "p16"], ["dw"], 144)
    ts(T.td[:], T.dw[:], 16.0, C("tdw"), OP.is_equal, OP.mult, ["dw", "tdw"], ["td"], 144)
    ts(T.t1[:], T.dw[:], C("t1c"), None, OP.is_equal, None, ["dw", "t1c"], ["t1"], 144)
    ts(T.blk[:], T.dw[:, 0:128:16], 0.0, None, OP.is_equal, None, ["dw"], ["blk"])
    ts(T.j2[:], T.jj[:], C("p16"), None, OP.subtract, None, ["jj", "p16"], ["j2"], NM)
    D16 = T.j2[:, 0:16]
    for name in ("Id", "Linv"):
        ts(hs(name), D16, 0.0, None, OP.is_equal, None, ["j2"], ["h" + name])
    ms(tm(0), 1000.0, ["m0"])
    act(hs("One"), tm(0), AF.Sigmoid, ["m0"], ["hOne"], 1600)
    gop(128, lambda: g.affine_select(T.Lb[:], T.o32[:], [[-1, 128]], OP.is_equal, 0.0, 0, 1), ["o32"], ["Lb"])
    ts(T.Lb[:, 15:128:16], T.blk[:], C("l15"), None, OP.mult, None, ["blk", "l15"], ["Lb"])
    for name, src, a, b in (("nId", "Id", -1.0, 0), ("nOH", "Id", -4096.0, 0), ("I8192", "Id", -8192.0, 0), ("OHm", "Id", 4096.0, -4096.0),
                            ("n256", "Id", -256.0, 0), ("eId", "Id", 2.0 ** -12, 0), ("B3", "Id", "b3", 0), ("A3", "Id", 1.0, -1.0),
                            ("Zc", "One", "zc", 0)):
        if a in CN:
            act(hs(name), hs(src), AF.Identity, ["h" + src, a], ["h" + name], scale=C(a))
        else:
            act(hs(name), hs(src), AF.Identity, ["h" + src], ["h" + name], scale=a, bias=float(b))
    iota(c15("A3"), [[0, 1]], 0, 0, ["hA3"], 1)
    cp(c15("Linv"), C("lin"), ["lin"], ["hLinv"])
    ts(hs("Tri"), D16, 0.0, -2.0, OP.is_gt, OP.mult, ["j2"], ["hTri"])
    act(tm(2), D16, AF.Abs, ["j2"], ["m2"], bias=-0.5)
    ts(hs("M"), tm(2), 1.0, 4096.0, OP.is_lt, OP.mult, ["m2"], ["hM"])
    ts(tm(3), T.wt[:, 0, 0, :], C("p8"), -39.0, OP.is_ge, OP.mult, ["w0", "p8"], ["m3"])
    act(tm(4), hs("Id"), AF.Identity, ["hId"], ["m4"], scale=72.0, bias=-1.0)
    tt(hs("G"), tm(3), tm(4), OP.add, ["m3", "m4"], ["hG"])
    ts(T.wt[:, 1, :, :], T.wt[:, 1, :, :], C("odd"), 2.0 ** -4 - 256, OP.not_equal, OP.mult, ["w1", "odd"], ["w1"])
    act(T.wt[:, 1, :, :], T.wt[:, 1, :, :], AF.Identity, ["w1"], ["w1"], bias=256.0)
    ts(T.wt[:, 2, :, :], T.wt[:, 0, :, :], C("p16"), 2.0 ** -6 - 1, OP.is_lt, OP.mult, ["w0", "p16"], ["w2"])
    act(T.wt[:, 2, :, :], T.wt[:, 2, :, :], AF.Identity, ["w2"], ["w2"], bias=1.0)
    iw = H16.index("WA")
    tt(T.h16[:, iw:iw + 2, :], T.wt[:, 1, :, :], T.wt[:, 2, :, :], OP.mult, ["w1", "w2"], ["hWA", "hWB"])
    for part, (m0, m1) in enumerate(((0, HE), (HE, len(H16)))):
        for gq in range(8):
            ts(T.hbig[:, m0:m1, 16 * gq:16 * gq + 16], T.h16[:, m0:m1, :], T.blk[:, gq:gq + 1], None, OP.mult, None,
               ["blk"] + ["h" + m for m in H16[m0:m1]], ["hb%d_%d" % (part, gq)], (m1 - m0) * 8)
    HA = ["hb0_%d" % q for q in range(8)]
    HB = HA + ["hb1_%d" % q for q in range(8)]
    if len(FRV) < NC:
        act(T.Id32[:], Hm("Id"), AF.Copy, HA, ["Id32"], 128)
    if G2S:
        ts(T.ts1[:], T.dw[:], 16.0, RS, OP.is_equal, OP.mult, ["dw"], ["ts1"], 144)
    ts(T.db[:], T.j2[:], 0.0, -8192.0, OP.not_equal, OP.mult, ["j2"], ["db"], NM)
    ts(T.an[:], T.keep[:], C("pm"), None, OP.is_equal, None, ["keep", "pm"], ["anti"], P)
    act(T.dbr[:], T.an[:, 0:NM], AF.Identity, ["anti"], ["dbr"], NM, scale=8192.0, bias=-8192.0)
    ts(T.crev[:], T.j3[:, 0:12], C("p16"), None, OP.subtract, None, ["j3", "p16"], ["crev"])
    iota(T.cd[:], [[0, SG]], 4096, 0, ["cd"], SG)
    ts(tm(5), D16, 1.0, 4096.0 - SP, OP.min, OP.mult, ["j2"], ["m5"])
    for b in range(4):
        act(T.cd[:, SEG[b]:SEG[b] + 16], tm(5), AF.Identity, ["m5"], ["cd"], bias=float(SP))
    iota(tm(6), [[16, 16]], 0, 0, ["m6"], 16)
    ts(T.hi[:], tm(6), C("p16"), float(W + SP), OP.add, OP.add, ["m6", "p16"], ["hi"])
    act(tm(7), tm(6), AF.Identity, ["m6", "lo"], ["m7"], scale=-1.0, bias=C("lo"))
    for name, src, a, b in (("x1", "p4", -8.0, -8.0), ("x2", "x1", "p4", 63.0), ("x3", "p4", 64.0, "x2"), ("x4", "p4", -40.0, "x3"),
                            ("x5", "p16", 40.0, "x4"), ("x6", "p4", 16.0, "x5")):
        act(C(name), C(src), AF.Identity, [src] + [x for x in (a, b) if x in CN], [name], scale=C(a) if a in CN else a, bias=C(b) if b in CN else b)
    act(T.xl[:, 0:1], C("x3"), AF.Identity, ["x3"], ["xl0"])
    ts(T.xl[:, 2:3], C("x5"), NC * SG - 1.0, None, OP.min, None, ["x5"], ["xl2"])
    ts(T.xl[:, 8:9], C("x5"), 2 * SG - 1.0, None, OP.min, None, ["x5"], ["xl8"])
    act(T.xl[:, 4:5], C("x6"), AF.Identity, ["x6"], ["xl4"], bias=-63.0)
    ts(T.xl[:, 6:7], C("p16"), -16.0, P - 1.0, OP.mult, OP.add, ["p16"], ["xl6"])
    iota(T.keepx[:], [[0, 640]], 30000, 0, ["keepx"], 640)
    cp(T.keepx[:].indirect(T.xl[:, 4:5]), tm(7), ["xl4", "m7"], ["keepx"], 80)
    act(C("hB"), T.thi[:, 1:2], AF.Identity, ["thi"], ["hB"], scale=256.0, bias=-65536.0)
    act(C("hb0"), T.thi[:, 0:1], AF.Identity, ["thi"], ["hb0"], scale=-1.0, bias=0.5)
    act(C("hbc"), T.thi[:, 0:1], AF.Identity, ["thi"], ["hbc"], scale=-1.0, bias=0.5 - 768 - 16 * 1536)

    for q in range(4):
        sl = slice(512 * q, 512 * q + 512)
        pe(grp(ps[q][:, 0:512], [(T.Lb[:], T.xdb[:, sl])], 512), ["Lb", "xdb"], ["P%d" % q], q)
        o = T.xw[:, SP + 512 * q:SP + 512 * q + 512]
        if q in XWV:
            ts(o, ps[q][:, 0:512], C("xwb"), None, OP.add, None, ["P%d" % q, "xwb"], ["xw%d" % q], 512, q)
        else:
            act(o, ps[q][:, 0:512], AF.Identity, ["P%d" % q, "xwb"], ["xw%d" % q], 512, q, bias=C("xwb"))

    cp(T.pvf[:, 0:12], T.pvi[:], ["pvi"], ["pvf"])
    tt(T.vt[:], T.pvf[:, 0:12].indirect(T.cb[:]), T.an[:], OP.mult, ["pvf", "cb", "anti"], ["vt%d" % c for c in range(NC)], int(GA * P) + 20)
    ts(T.z0[:], T.pzb[:].indirect(T.crev[:]), C("zoff"), None, OP.add, None, ["pzb", "crev", "zoff"], ["z0_%d" % c for c in range(NC)],
       int(GA * P) + 20)

    rid, pid, _se = topo.addr(dst)
    eng = topo.engines(core, dst)
    mask = topo.mask(core, dst)
    win_x, NBG = T.xw[:, SP:SP + W], NBF
    turn = [0]

    def chunk(t, c):
        last = t == R - 1
        c0, n = CH[c]
        s = str(c)
        nb = n // 16
        sl = slice(c0, c0 + n)
        wide = lambda buf, m, a=0, b=None: buf[:, m * c0 + a * n:m * c0 + (m if b is None else b) * n]
        r7 = lambda k, w=1: ps[7][:, NM * k:NM * k + w * n]
        r5 = lambda k, w=1: ps[5][:, NM * k:NM * k + w * n]
        vt, z32 = T.land[:, t, 2 * c0:2 * c0 + n], T.land[:, t, 2 * c0 + n:2 * c0 + 2 * n] if t else T.z0[:, sl]
        zn, vn = "z%d_%d" % (t, c), "v%d_%d" % (t, c)
        lc = slice(c0 // 16, (c0 + n) // 16)
        l2 = slice(c0 // 8, (c0 + n) // 8, 2)
        gn = int(GA * n) + 20
        at(t, HEAD[c])
        if t > 0:
            add("X", 3000, None, ["sent%d_%d" % (t - 1, c)], [zn, vn], kind="r", sem="arr%d" % ((t - 1) * NC + c))

        def zcopy(o, a, cols, rd, wr):
            gop(cols, lambda: g.affine_select(o, a, [[0, cols]], OP.is_ge, 0.0, 0, 0), rd, wr)
        scp = lambda o, a, cols, rd, wr: act(o, a, AF.Copy, rd, wr, cols)
        ZR = ["zr%d" % j + s for j in range(4)]
        z, zz = T.zq[:, 4 * c0:4 * (c0 + n):4], "zq0" + s
        for j in range(4):
            (scp if c in ZQS and t else zcopy)(T.zq[:, 4 * c0 + j:4 * (c0 + n):4], z32, n, [zn], ["zq%d" % j + s])
            at(t, A0[c] - 4200 + 300 * j, 700)
        for j in range(4):
            zcopy(T.zrep[:, 16 * c0 + j:16 * (c0 + n):4], wide(T.zq, 4), 4 * n, ["zq%d" % i + s for i in range(4)], ["zr%d" % j + s])
        at(t, HEAD[c] - 300)
        if t:
            (scp if c in ZQS else zcopy)(T.vt[:, sl], vt, n, [vn], ["vt" + s])
        pe(grp(r7(1), [(Hm("Id"), T.db[:, 0:n]), (Hm("One"), T.vt[:, sl])], n), HA + ["db", "vt" + s], ["Q1"], 7)
        scan(T.vsc[:, sl], r7(1), n, ["Q1"], ["vsc" + s], 7)
        (gcp if "vu" + s in G16 else cp)(T.vu[:, lc], T.vsc[:, c0 + 15:c0 + n:16], ["vsc" + s], ["vu" + s], nb)
        vl_ = T.vu[:, lc]
        xv, oh, con, aa, sh = T.xv[:, sl], T.oh[:, sl], T.con[:, sl], T.aa[:, sl], T.sh[:, sl]
        act(xv, win_x.indirect(vl_), AF.Copy, XW + ["vu" + s], ["xv" + s], gn)
        pe(grp(r7(2), [(Hm("Linv"), xv), (Hm("nId"), z)], n), HA + ["xv" + s, zz], ["Q2"], 7)
        act(aa, r7(2), AF.Abs, ["Q2", "dabs"], ["aa" + s], n, 7, bias=C("dabs"))
        act(T.bad[:, sl], aa, AF.Sign, ["bdb", "aa" + s], ["bad" + s], n, bias=C("bdb"), scale=1 / 64)
        pe(grp(r7(3), [(Hm("Tri"), T.bad[:, sl]), (Hm("Id"), T.bad[:, sl])], n), HA + ["bad" + s], ["Q3"], 7)
        act(oh, r7(3), AF.Relu, ["Q3", "ohb"], ["oh" + s], n, 7, bias=C("ohb"), scale=0.5)
        yield
        win_n, NBF = (T.nbf[:, SP:SP + W], NBG) if t else (T.nbi[:], NBI)
        at(t, GG[c] + 900, -1200)
        act(con, win_n.indirect(vl_), AF.Copy, NBF + ["vu" + s], ["con" + s], gn)
        if "conu" + s in G16:
            gcp(T.conu[:, sl], con, ["con" + s], ["conu" + s], n)
        else:
            cp(T.conu[:, sl], win_n.indirect(vl_), NBF + ["vu" + s], ["conu" + s], gn)
        h2 = n // 2
        at(t, GG[c], 900 * (c > 0))
        for j in range(2):
            o = T.gg[:, 16 * (c0 + h2 * j):16 * (c0 + h2 * j + h2)]
            src = win_n.indirect(T.conu[:, c0 + h2 * j:c0 + h2 * j + h2])
            if j in G1V.get(c, ()):
                cp(o, src, NBF + ["conu" + s], ["gg%d" % j + s], int(GA * 16 * h2) + 20)
            else:
                act(o, src, AF.Copy, NBF + ["conu" + s], ["gg%d" % j + s], int(GA * 16 * h2) + 20)
        cbk = rbk = 2 + c
        Cp, PC, PR = ps[cbk], "P%d" % cbk, "R%d" % cbk
        Rp = lambda a, b: Cp[:, (4 + a) * n:(4 + b) * n]
        kb = 4 if (n > 64 or c in RLV) else 8
        sums, late = [], []
        for h in range(2):
            hn = "%d" % h + s
            names = []
            at(t, A0[c] - 1800 + 1200 * h, 200)
            for k0 in range(8 * h, 8 * h + 8, kb):
                bk = turn[0] % 2
                turn[0] += 1
                pn = ["P%d" % bk, "P%db" % bk]
                for q in range(kb // 4):
                    mm = []
                    for k in range(4 * q, 4 * q + 4):
                        mm += grp(ps[bk][:, n * k:n * k + n], [(Hm("M"), oh), (Hm("Id"), T.gg[:, 16 * c0 + k0 + k:16 * (c0 + n):16])], n)
                    pe(mm, HA + ["gg0" + s, "gg1" + s, "oh" + s], [pn[q]], bk)
                gm = wide(T.gm, 16, k0, k0 + kb)
                names.append("gm%d_" % k0 + s)
                if k0 // kb in RLV.get(c, ()):
                    ts(gm, ps[bk][:, 0:n * kb], -4096.0, 0.0, OP.add, OP.max, pn, [names[-1]], kb * n, bk)
                else:
                    act(gm, ps[bk][:, 0:n * kb], AF.Relu, pn, [names[-1]], kb * n, bk, bias=-4096.0)
            pe(grp(Cp[:, n * h:n * h + n], [(T.t1[:, 16 - k:144 - k], wide(T.gm, 16, 8 * h + k, 8 * h + k + 1)) for k in range(8)], n),
               ["t1", PC + "open"] + names, [PC + "c%d" % h] + ([PC] if t == 0 and h == 0 else []), cbk)
            if hn in CUS:
                act(wide(T.cu, 2, h, h + 1), Cp[:, n * h:n * h + n], AF.Copy, [PC + "c%d" % h], ["cu" + hn], n, cbk)
            else:
                cp(wide(T.cu, 2, h, h + 1), Cp[:, n * h:n * h + n], [PC + "c%d" % h], ["cu" + hn], n, cbk)
            w = n // MXS
            at(t, A0[c] + 1800 * h, 900)
            mine = []
            for j in range(MXS):
                a = 32 * c0 + 16 * n * h + 16 * w * j
                o, src = T.mx[:, a:a + 16 * w], win_x.indirect(T.cu[:, 2 * c0 + n * h + w * j:2 * c0 + n * h + w * j + w])
                zr, mn = T.zrep[:, 16 * (c0 + w * j):16 * (c0 + w * j + w)], "mx%d" % j + hn
                if (h, j) not in G2S.get(c, ()):
                    tt(o, src, zr, OP.min, XW + ZR + ["cu" + hn], [mn], int(GA * 16 * w) + 20)
                    mine.append(j)
                    continue
                bk = turn[0] % 2
                turn[0] += 1
                at(t, A0[c] + 1800 * h, 600)
                act(o, src, AF.Copy, XW + ["cu" + hn], [mn], int(GA * 16 * w) + 20)
                pe(grp(ps[bk][:, 0:16 * w], [(Hm("nId"), zr), (Hm("Linv"), o)], 16 * w), HA + ZR + [mn], ["P%d" % bk, "P%db" % bk], bk)
                act(o, ps[bk][:, 0:16 * w], AF.Abs, ["P%d" % bk, "P%db" % bk, "dabs"], [mn], 16 * w, bk, bias=C("dabs"))
                late.append((grp(Cp[:, (4 + h) * n + w * j:(4 + h) * n + w * j + w], [(Hm("K1"), T.oh[:, c0 + w * j:c0 + w * j + w])]
                                 + [(T.ts1[:, 16 - k:144 - k], T.mx[:, a + k:a + 16 * w:16]) for k in range(16)], w),
                             HB + ["oh" + s, "ts1", mn], [PR + "r%d%d" % (h, j), PC + "open"], rbk))
                at(t, A0[c] + 1800 * h + 900, 900)
            if mine:
                i0, m = w * mine[0], w * len(mine)
                a = 32 * c0 + 16 * n * h + 16 * i0
                mm = grp(Cp[:, (4 + h) * n + i0:(4 + h) * n + i0 + m], [(Hm("Zc"), T.zq[:, 4 * (c0 + i0):4 * (c0 + i0 + m):4])]
                         + [(Hm("K0"), T.oh[:, c0 + i0:c0 + i0 + m])]
                         + [(T.td[:, 16 - k:144 - k], T.mx[:, a + k:a + 16 * m:16]) for k in range(16)], m)
                cut = [len(mm) * q // RSP for q in range(RSP + 1)]
                for q in range(RSP):
                    sums.append((mm[cut[q]:cut[q + 1]], HB + ["td", zz, "oh" + s] + ["mx%d" % j + hn for j in mine],
                                 [PR + "r%d%d" % (h, j) for j in mine] + [PC + "open"], rbk))
        sums[RSP:RSP] = late
        at(t, A0[c] + 1000, 0)
        pe(grp(Cp[:, 2 * n:3 * n], [(Hm("Id"), con)], n) + grp(Cp[:, 3 * n:4 * n], [(Hm("Id"), aa), (Hm("nId"), z), (Hm("K15"), oh)], n)
           + grp(Rp(2, 3), [(Hm("WA"), oh)], n) + grp(Rp(3, 4), [(Hm("WB"), oh)], n),
           HB + ["con" + s, "aa" + s, zz, "oh" + s, PC, PC + "open"], [PC + "c2"], cbk)
        for q, x in enumerate(sums):
            at(t, A0[c] + 1900 + (q >= RSP) * 1700 + q)
            pe(*x)
        yield
        dl, ad, ww, sel, val = wide(T.dl, 2), wide(T.ad, 2), wide(T.ww, 2), wide(T.sel, 4), wide(T.val, 4)
        RR = [PR + "r%d%d" % (h, j) for h in range(2) for j in range(MXS)]
        tail[0] = 1
        at(t, A0[c] + TL, 200)
        act(dl, Rp(0, 2), AF.Identity, RR, ["dl" + s], 2 * n, rbk, bias=-120 / 256)
        if c in FRV:
            tt(wide(T.fr, 2), dl, Rp(0, 2), OP.subtract, RR + ["dl" + s], ["fr" + s], 2 * n, rbk)
            act(ad, dl, AF.Abs, ["dl" + s], ["ad" + s], 2 * n, bias=-1536.0)
            pe([(Rp(0, 2), Hm("Id"), ad, True, False, 2 * n), (Rp(0, 1), Hm("n256"), sh, False, False, n),
                (Rp(1, 2), Hm("n256"), sh, False, False, n), (Rp(0, 2), Hm("n256"), wide(T.fr, 2), False, True, 2 * n)],
               HB + ["sh" + s, "ad" + s, "fr" + s], RR, rbk)
        else:
            act(wide(T.r32, 2), Rp(0, 2), AF.Identity, RR, ["r32" + s], 2 * n, rbk, scale=256.0)
            act(ad, dl, AF.Abs, ["dl" + s], ["ad" + s], 2 * n, bias=-1536.0)
            pe([(Rp(0, 2), Hm("n256"), dl, True, False, 2 * n), (Rp(0, 1), Hm("n256"), sh, False, False, n),
                (Rp(1, 2), Hm("n256"), sh, False, False, n), (Rp(0, 2), T.Id32[:], wide(T.r32, 2), False, False, 8 * n)],
               HB + ["Id32", "sh" + s, "dl" + s, PC + "c2", "r32" + s], RR, rbk)
            pe([(Rp(0, 2), Hm("Id"), ad, False, True, 2 * n)], RR + ["ad" + s], RR, rbk)
        act(wide(T.hh, 2), Rp(0, 2), AF.Relu, RR + ["hB"], ["hh" + s], 2 * n, rbk, scale=-256.0, bias=C("hB"))
        tt(ww, Rp(2, 4), wide(T.hh, 2), OP.min, [PC + "c2", "hh" + s], ["ww" + s], 2 * n, rbk)
        w0, w1 = wide(T.ww, 2, 0, 1), wide(T.ww, 2, 1, 2)
        both = [(Hm("nOne"), w0), (Hm("nOne"), w1)]
        f6 = lambda a, b: ps[6][:, a * n:b * n]
        pe(grp(f6(2, 3), [(Hm("A3"), oh), (Hm("B3"), sh)] + both, n) + grp(f6(3, 4), [(Hm("eId"), sh)] + both, n)
           + grp(f6(0, 1), [(Hm("G"), w0), (Hm("nOne"), w1)], n) + grp(f6(1, 2), [(Hm("na1"), w0), (Hm("G"), w1)], n),
           HB + ["oh" + s, "sh" + s, "ww" + s], ["F0"], 6)
        act(sel, f6(0, 4), AF.Sigmoid, ["F0"], ["sel" + s], 4 * n, 6, scale=2.0 ** 22, bias=-200.0)
        tt(val, Cp[:, 0:4 * n], sel, OP.mult, [PC + "c0", PC + "c1", PC + "c2", "sel" + s], ["val" + s], 4 * n, cbk)
        if c == NC - 1:
            mm, UU = first(c, 5, 0, True), ["U0", "U1", "U2"]
            pe(mm[:6], HB + ["cd", "vt" + s] + ["ne%d" % b + s for b in range(4)] + ["hh" + s], UU, 5)
            pe(mm[6:], ["sel" + s], UU, 5)
            scanx(T.nsc[:, SG * c:SG * c + SG], ps[5][:, 0:SG], SG, UU, ["nsc" + s], 5)
            tt(T.nu[:, 16:32], T.nsc[:, SG * c:SG * c + SG].indirect(T.xl[:, 0:1]), T.hi[:], OP.min, ["nsc" + s, "hi", "xl0"], ["nu" + s], 64)
        vals = [(Hm("One"), wide(T.val, 4, a, a + 1)) for a in range(3)]
        pe(grp(Rp(0, 1), [(Hm("OHm"), oh)] + vals, n) + grp(Rp(1, 2), [(Hm("Id"), z), (Hm("Id"), wide(T.val, 4, 3, 4))], n),
           HB + ["oh" + s, zz, "val" + s], RR, rbk)
        out = T.send[:, t, 2 * c0:2 * c0 + 2 * n]
        act(out, Rp(0, 2), AF.Relu, RR, ["out%d" % t + s], 2 * n, rbk)
        if not last:
            add("G", 700, lambda: g.remote_dma(T.land[:, t + 1, 2 * c0:2 * c0 + 2 * n], out, T.sem["arr%d" % (t * NC + c)],
                                               T.sem["sent"], pid, rid, mask), ["out%d" % t + s], ["sent%d_%d" % (t, c)], kind="s")
        else:
            ts(T.oz[:, P - c0 - n:P - c0], T.send[:, t, 2 * c0 + n:2 * c0 + 2 * n].indirect(T.crev[:, 12 - nb:12]), C("zoff"), None,
               OP.subtract, None, ["out%d" % t + s, "crev", "zoff"], ["oz" + s], gn)
            pe(grp(r7(0), [(Hm("Id"), T.dbr[:, 0:n])] + vals, n), HA + ["dbr", "val" + s], ["Q0"], 7)
            scan(T.tsc[:, sl], r7(0), n, ["Q0"], ["tsc" + s], 7)
        tail[0] = 0

    def same(c):
        c0, n = CH[c]
        s, a = str(c), 256 + 64 * c
        pe(grp(ps[7][:, a:a + n], [(Hm("One"), T.vt[:, c0:c0 + n])], n), HA + ["vt" + s], ["Q4" + s], 7)
        for b in range(4):
            o, src = T.ne[:, SG * c + SEG[b]:SG * c + SEG[b + 1]], ps[7][:, a + 16 * b:a + n]
            me = T.vsc[:, c0 + 16 * b + 15:c0 + 16 * b + 16]
            if c in NEV:
                ts(o, src, me, None, OP.not_equal, None, ["Q4" + s, "vsc" + s], ["ne%d" % b + s], 64, 7)
            else:
                act(o, src, AF.Abs, ["Q4" + s, "vsc" + s], ["ne%d" % b + s], 64, 7, scale=-1.0, bias=me)

    def first(c, bank, a, repaired):
        c0, n = CH[c]
        mm = [(ps[bank][:, a:a + SG], Hm("Id"), T.cd[:], True, False, SG)]
        for b in range(4):
            mm.append((ps[bank][:, a + SEG[b]:a + SEG[b] + 16], Hm("One"), T.vt[:, c0 + 16 * b:c0 + 16 * b + 16], False, False, 16))
        mm.append((ps[bank][:, a:a + SG], Hm("I8192"), T.ne[:, SG * c:SG * c + SG], False, not repaired, SG))
        for b in range(4 if repaired else 0):
            mm.append((ps[bank][:, a + SEG[b]:a + SEG[b + 1]], Hm("n8192"), T.sel[:, 4 * c0 + 2 * n + 16 * b:4 * c0 + 3 * n], False, b == 3, 64))
        return mm

    def span(cs):
        c0, n = CH[cs[0]][0], sum(CH[c][1] for c in cs)
        return c0, n, slice(c0, c0 + n), T.zq[:, 4 * c0:4 * (c0 + n):4], lambda *m: [x + str(c) for x in m for c in cs]

    def side(t, cs):
        c0, n, sl, z, N = span(cs)
        at(t, A0[cs[0]] + SD, 400)
        lc = slice(c0 // 16, (c0 + n) // 16)
        con, oh, u0, u1 = T.con[:, sl], T.oh[:, sl], ps[5][:, 0:n], ps[5][:, n:2 * n]
        pe(grp(u0, [(Hm("Id"), con), (Hm("OHm"), oh)], n) + grp(u1, [(Hm("Id"), con), (Hm("nOH"), oh)], n), HA + N("con", "oh"), ["U0", "U1"], 5)
        act(T.yy[:, sl], u0, AF.Relu, ["U0"], N("yy"), n, 5)
        act(T.yp[:, sl], u1, AF.Relu, ["U1"], N("yp"), n, 5)
        mm = []
        for c in cs:
            a, m = CH[c][0] - c0, CH[c][1]
            PRE[c] = c0 + a
            mm += grp(ps[5][:, a:a + m], [(Hm("Id"), T.db[:, 0:m]), (Hm("One"), T.yy[:, c0 + a:c0 + a + m])], m)
        pe(mm, HA + ["db"] + N("yy"), ["U0"], 5)
        scan(T.tsc[:, sl], u0, n, ["U0"], N("tsc"), 5)
        (gcp if "tu" in G16 else cp)(T.tu[:, lc], T.tsc[:, c0 + 15:c0 + n:16], N("tsc"), N("tu"), n // 16)
        act(T.xt[:, sl], win_x.indirect(T.tu[:, lc]), AF.Copy, XW + N("tu"), N("xt"), int(GA * n) + 20)
        pe(grp(u1, [(Hm("Linv"), T.xt[:, sl]), (Hm("nId"), z)], n), HA + N("zq0", "xt"), ["U1"], 5)
        act(T.at[:, sl], u1, AF.Abs, ["U1", "dabs"], N("at"), n, 5, bias=C("dabs"))
        pe(grp(u0, [(Hm("One"), T.at[:, sl])], n), HA + N("at"), ["U0"], 5)
        hb = "hb%d" % t
        if t == R - 1:
            act(T.sh[:, sl], u0, AF.Sign, ["U0", hb], N("sh"), n, 5, bias=C(hb))
        else:
            act(T.sh[:, sl], u0, AF.Sign, ["U0", hb], N("sh", "acc"), n + 150, 5, bias=C(hb), accum_out=T.acc[:, cs[0]:cs[0] + 1])

    def digits(cs):
        c0, n, sl, z, N = span(cs)
        u = ps[7][:, 256:256 + n]
        for c in cs:
            pe(first(c, 5, SG * c, False), HA + ["cd", "vt%d" % c] + ["ne%d%d" % (b, c) for b in range(4)], ["U0", "U1", "U%d" % (c + 2)], 5)
        scanx(T.dsc[:], ps[5][:, 0:NC * SG], NC * SG, ["U0", "U1", "U2", "U3", "U4"], N("dsc"), 5)
        tt(T.du[:, 0:16], T.dsc[:].indirect(T.xl[:, 2:3]), T.hi[:], OP.min, ["hi", "xl2"] + N("dsc"), N("du"), 64)
        pe(grp(u, [(Hm("Linv"), T.xv[:, sl]), (Hm("Id"), z)], n), HA + N("zq0", "xv"), N("Q4"), 7)
        act(T.nd[:, sl], u, AF.Identity, N("Q4") + ["ndb"], N("nd"), n, 7, bias=C("ndb"), scale=0.5)
        pe(grp(u, [(T.Lb[:], T.nd[:, sl])], n), ["Lb"] + N("nd"), N("Q4"), 7)
        act(T.ndw[:, sl], u, AF.Identity, N("Q4") + ["lnb"], N("ndw"), n, 7, bias=C("lnb"))

    PRE = {}

    def writes(t, c, digits):
        c0, n = CH[c]
        s = str(c)
        if digits:
            cp(T.xw[:].indirect(T.du[:, 4 * c:4 * c + 4]), T.ndw[:, c0:c0 + n], ["du" + s, "ndw" + s], XW, 20 + int(SC * n), kind="w")
        else:
            tt(T.nbf[:].indirect(T.nu[:, (0, 4, 16)[c]:(0, 4, 16)[c] + 4]), T.send[:, t, 2 * c0:2 * c0 + n], T.yp[:, c0:c0 + n], OP.add,
               ["nu" + s, "out%d" % t + s, "yp" + s], NBF, 20 + int(SC * n), kind="w")

    gens = [chunk(0, c) for c in range(NC)]
    for c in range(NC):
        next(gens[c])
    for t in range(R):
        for c in range(NC):
            next(gens[c])
        at(t, 9000)
        for q in range(4 if t == 0 else 0):
            gop(512, lambda q=q: g.affine_select(T.nbf[:, SP + 512 * q:SP + 512 * q + 512], T.nbi[:, 512 * q:512 * q + 512], [[0, 512]],
                                                 OP.is_ge, 0.0, 0, 0), ["nbi%d" % q], ["nbf%d" % q])
        for cs in SIDE:
            side(t, cs)
        for c in range(NC):
            at(t, A0[2] + NE, 150)
            same(c)
        for c in range(NC - 1):
            next(gens[c], None)
        if t < R - 1:
            at(t, A0[2] - 500, 500)
            for cs in DIG:
                digits(cs)
            at(t, A0[2] + WR, 120)
            for c in range(NC):
                writes(t, c, True)
            pe(grp(ps[7][:, 500:501], [(T.o32[:], T.acc[:, cs[0]:cs[0] + 1]) for cs in SIDE], 64),
               ["o32"] + ["acc%d" % c for c in range(NC)], ["Pa"], 7)
            act(T.ah[:, 0:1], ps[7][:, 500:501], AF.Identity, ["Pa"], ["ai0"], 64, 7, scale=1 / 512, bias=1536 + 48 - 15 / 32)
            act(C("hbt"), ps[7][:, 500:501], AF.Identity, ["Pa", "hbc"], ["ai1"], 64, 7, scale=-1 / 32, bias=C("hbc"))
            act(C("hb%d" % (t + 1)), T.ah[:, 0:1], AF.Identity, ["ai0", "ai1"], ["hb%d" % (t + 1)], scale=16.0, bias=C("hbt"))
        at(t, A0[2] + NS, 120)
        for c in range(NC - 1):
            pe(first(c, 5, SG * c, True), HB + ["cd", "vt%d" % c] + ["ne%d%d" % (b, c) for b in range(4)] + ["sel%d" % c],
               ["U0", "U1", "U%d" % (c + 2)], 5)
        scanx(T.nsc[:, 0:2 * SG], ps[5][:, 0:2 * SG], 2 * SG, ["U0", "U1", "U2", "U3"], ["nsc0", "nsc1"], 5)
        tt(T.nu[:, 0:16], T.nsc[:, 0:2 * SG].indirect(T.xl[:, 8:9]), T.hi[:], OP.min, ["nsc0", "nsc1", "hi", "xl8"], ["nu0", "nu1"], 64)
        for c in range(NC - 1):
            writes(t, c, False)
        nxt = [chunk(t + 1, c) for c in range(NC)] if t < R - 1 else []
        for c in range(len(nxt) - 1):
            next(nxt[c])
        next(gens[NC - 1], None)
        at(t, LEN - 1000, 200)
        writes(t, NC - 1, False)
        if nxt:
            next(nxt[NC - 1])
        gens = nxt
    cp(T.ov[:], T.tsc[:].indirect(T.xl[:, 6:7]), ["xl6"] + ["tsc%d" % c for c in range(NC)], ["ov"])
    at(R, 0)
    dma("Y", T.ynb[0:64, :], T.nbf[0:64, SP:SP + W], NBF, ["o0"], 5000)
    dma("S", T.ynb[64:128, :], T.nbf[64:128, SP:SP + W], NBF, ["o1"], 5000)
    dma("Y", T.yz[:], T.oz[:], ["oz%d" % c for c in range(NC)], ["o2"], 3000)
    dma("Y", T.yv[:], T.ov[:, 0:12], ["ov"], ["o3"], 3000)
    return ops, len(eng)


def key(o):
    return o["wr"][0] + "<" + (o["rd"][-1] if o["rd"] else "")


def graph(ops):
    N = len(ops)
    deps = [set() for _ in range(N)]
    wr, rd = {}, {}
    for i, o in enumerate(ops):
        for a in o["rd"]:
            if a in wr:
                deps[i].add(wr[a])
        for a in o["wr"]:
            if a in wr:
                deps[i].add(wr[a])
            deps[i].update(rd.get(a, ()))
        for a in o["rd"]:
            rd.setdefault(a, []).append(i)
        for a in o["wr"]:
            wr[a] = i
            rd[a] = []
        deps[i].discard(i)
    succ = [[] for _ in range(N)]
    for i in range(N):
        for d in deps[i]:
            succ[d].append(i)
    prio, least = [0] * N, {}
    for _pass in range(R + 1):
        big = {}
        for i in reversed(range(N)):
            o = ops[i]
            prio[i] = max(least.get(i, 0), o["cost"] + max([prio[j] + HOP for j in succ[i]], default=0))
            row = ROW.get(o["eng"] + o["wr"][0][:2])
            if row:
                prio[i] = max(prio[i], int(o["cost"] * row) + big.get(o["eng"], 0))
                big[o["eng"]] = prio[i]
        seen = {}
        for i, o in enumerate(ops):
            seen[o["wr"][0]] = i
            if o["wr"][0][:3] == "out" and o["wr"][0][4:] in DUE:
                least[i] = prio[seen[DUE[o["wr"][0][4:]]]]
    if LEN:
        zero = max(prio[i] for i in range(N) if ops[i]["wr"][0] == "conu0")
        for i in reversed(range(N)):
            d = zero - prio[i] if ops[i]["due"] is None else ops[i]["due"]
            least[i] = min([d] + [least[j] - ops[i]["cost"] - HOP for j in succ[i]])
        prio = [-least[i] for i in range(N)]
    return deps, succ, prio


def free(ops, d, i):
    a, b = ops[d], ops[i]
    return a["eng"] == b["eng"] and (a["eng"] == "P" or (NOWAW and a["kind"] == "w" and b["kind"] == "w"))


def plan(ops, gr=None):
    N = len(ops)
    deps0, succ, base = gr or graph(ops)
    deps = [set(d) for d in deps0]
    prio = [p + BONUS.get(key(o), 0) + (SHORT if o["cost"] < 500 else 0) + TAIL * o["tail"] for p, o in zip(base, ops)]
    left = [len(d) for d in deps]
    ready = [i for i in range(N) if not left[i]]
    end, busy, bank, order, at = [0] * N, {}, {}, [], [0] * N
    while ready:
        def start(i):
            o = ops[i]
            s = at[i]
            if o["kind"] != "r":
                s = max(s, busy.get(o["eng"], 0))
            b = bank.get(o["bank"])
            if b is not None:
                s = max(s, end[b] + (HOP if ops[b]["eng"] != o["eng"] else 0))
            return s
        st = {i: start(i) for i in ready}
        t0 = min(st.values())
        e0 = ops[min(ready, key=lambda i: (st[i], -prio[i]))]["eng"]
        i = max([j for j in ready if ops[j]["eng"] == e0 and st[j] <= t0 + SLACK], key=lambda j: (prio[j] - IDLE * (st[j] - t0), -j))
        o = ops[i]
        end[i] = st[i] + o["cost"]
        if o["kind"] != "r":
            busy[o["eng"]] = st[i] + 60 if o["kind"] == "d" else end[i]
        if o["bank"] is not None:
            b = bank.get(o["bank"])
            if b is not None and ops[b]["eng"] != o["eng"]:
                deps[i].add(b)
            bank[o["bank"]] = i
        order.append(i)
        ready.remove(i)
        for j in succ[i]:
            at[j] = max(at[j], end[i] + (0 if free(ops, i, j) else HOP))
            left[j] -= 1
            if not left[j]:
                ready.append(j)
    return order, deps, end


SLACK, IDLE, ROW, SHORT = 60, 0, {"Vmx": 1.0}, 1800
NOWAW = False
DUE = {}
TAIL = 100
BONUS = {}
TUNED = []


LEN, A0, HEAD, GG, TL, SD, WR = 16300, (4600, 25600, 11800), (-4400, -2400, 300), (6370, 4100, 3200), 12600, 6700, 700
SEED = 12345
OTHER = [(200, 0.75, 1.1, 2000), (80, 1.3, 0.9, 4000)]


def replay(ops, order, deps, hop, ind, pe, way):
    end, busy = [0] * len(ops), {}
    for i in order:
        o = ops[i]
        q, c = o["eng"], o["cost"]
        s = max([end[d] + (0 if free(ops, d, i) else hop) for d in deps[i]], default=0)
        if o["kind"] == "r":
            end[i] = s + way
            continue
        s = max(s, busy.get(q, 0))
        end[i] = s + (c * pe if q == "P" else 60 + (c - 60) * ind if o["ind"] else c)
        busy[q] = s + 60 if o["kind"] == "d" else end[i]
    return max(end)


def tune(ops, rounds):
    keys = sorted({key(o) for o in ops})
    steps = (-3000, -1500, -600, -200, 200, 600, 1500, 3000)
    gr = graph(ops)

    def length():
        order, deps, end = plan(ops, gr)
        return max(end) + sum(replay(ops, order, deps, *m) for m in OTHER)
    best, x = length(), SEED
    for _ in range(rounds):
        old = dict(BONUS)
        x = (x * 1103515245 + 12345) % 2147483648
        for _j in range(1 + (x >> 16) % 3):
            x = (x * 1103515245 + 12345) % 2147483648
            k = keys[(x >> 8) % len(keys)]
            x = (x * 1103515245 + 12345) % 2147483648
            BONUS[k] = BONUS.get(k, 0) + steps[(x >> 16) % 8]
        e = length()
        if e <= best:
            best = e
        else:
            BONUS.clear()
            BONUS.update(old)
    return best


def lay(ops, gr, when, models):
    deps0, succ = gr[0], gr[1]
    N = len(ops)
    order = sorted(range(N), key=lambda i: (when[i], i))
    total, swaps, deps = 0, [], None
    for hop, ind, pe, way in models:
        end, by, busy, bank, extra = [0] * N, [None] * N, {}, {}, {}
        for i in order:
            o = ops[i]
            q, c, s, w = o["eng"], o["cost"], 0, None
            for d in deps0[i]:
                e = end[d] + (0 if q == "P" == ops[d]["eng"] else hop)
                if e > s:
                    s, w = e, (d, 0)
            if o["kind"] == "r":
                end[i], by[i] = s + way, w
                continue
            b = bank.get(o["bank"])
            if b is not None and ops[b]["eng"] != q:
                extra[i] = b
                if end[b] + hop > s:
                    s, w = end[b] + hop, (b, 1)
            if q in busy and busy[q][0] >= s:
                s, w = busy[q][0], (busy[q][1], 1)
            end[i], by[i] = s + (c * pe if q == "P" else 60 + (c - 60) * ind if o["ind"] else c), w
            busy[q] = (s + 60 if o["kind"] == "d" else end[i], i)
            if o["bank"] is not None:
                bank[o["bank"]] = i
        i = end.index(max(end))
        total += end[i]
        while by[i]:
            if by[i][1] and by[i][0] not in deps0[i]:
                swaps.append((by[i][0], i))
            i = by[i][0]
    return total, swaps, order, extra


def polish(ops, rounds):
    gr = graph(ops)
    order, _deps, end = plan(ops, gr)
    when = [0] * len(ops)
    for k, i in enumerate(sorted(order, key=lambda i: end[i] - ops[i]["cost"])):
        when[i] = float(k)
    models = [(HOP, 1.0, 1.0, 3000)] + OTHER
    best, swaps, order, extra = lay(ops, gr, when, models)
    now, keep, x = best, (best, list(when)), SEED
    for r in range(rounds):
        x = (x * 1103515245 + 12345) % 2147483648
        a, b = swaps[(x >> 8) % len(swaps)]
        x = (x * 1103515245 + 12345) % 2147483648
        new = list(when)
        if (x >> 16) % 2:
            new[b] = when[a] - 0.001 * (1 + (x >> 8) % 7)
            todo = [b]
            while todo:
                j = todo.pop()
                for d in gr[0][j]:
                    if new[d] >= new[j]:
                        new[d] = new[j] - 0.0001
                        todo.append(d)
        else:
            new[a] = when[b] + 0.001 * (1 + (x >> 8) % 7)
            todo = [a]
            while todo:
                j = todo.pop()
                for d in gr[1][j]:
                    if new[d] <= new[j]:
                        new[d] = new[j] + 0.0001
                        todo.append(d)
        e, sw, order, extra = lay(ops, gr, new, models)
        if e <= now + WARM * (1 - r / rounds):
            now, swaps = e, sw
            when = [0] * len(ops)
            for k, i in enumerate(order):
                when[i] = float(k)
            if e < keep[0]:
                keep = (e, list(when))
    e, _sw, order, extra = lay(ops, gr, keep[1], models)
    deps = [set(d) for d in gr[0]]
    for i, b in extra.items():
        deps[i].add(b)
    return order, deps, e


WARM = 150


def rank_program(g, core, T, topo):
    rank = T.rank_of(core)
    if rank is None:
        return
    dst = T.cores[(rank + STEP) % len(T.cores)]
    ops, ne = build(g, T, topo, core, dst)
    if not TUNED:
        tune(ops, ROUNDS)
        TUNED.append(polish(ops, 5 * ROUNDS))
    order, deps, _end = TUNED[0]
    place = {i: k for k, i in enumerate(order)}
    Q = {"V": g.vector, "S": g.scalar, "P": g.tensor, "G": g, "Y": g.sync}
    need = set()
    for i in order:
        for d in deps[i]:
            if not free(ops, d, i) and ops[i]["kind"] != "r":
                need.add(d)
    count, tick, know, clock = {}, {}, {q: {} for q in Q}, {}
    for i in order:
        o = ops[i]
        if o["kind"] == "r":
            tick[i], clock[i] = (o["sem"], ne), {}
            count[o["sem"]] = ne
            continue
        q, kn = o["eng"], know[o["eng"]]
        want = {}
        for d in deps[i]:
            if d in tick and not free(ops, d, i):
                sem, v = tick[d]
                if v > want.get(sem, (0, 0))[0]:
                    want[sem] = (v, d)
        for sem, (v, d) in sorted(want.items(), key=lambda kv: -place[kv[1][1]]):
            if kn.get(sem, 0) < v:
                Q[q].wait_ge(T.sem[sem], v)
                kn[sem] = v
                for s2, v2 in clock[d].items():
                    kn[s2] = max(kn.get(s2, 0), v2)
        ins = o["fn"]()
        clock[i] = dict(kn)
        if o["kind"] == "d":
            ins.then_inc(T.sem[o["sem"]], 16)
            tick[i] = (o["sem"], 16)
            count[o["sem"]] = 16
        elif o["kind"] == "s":
            count["sent"] = count.get("sent", 0) + ne
        elif i in need:
            sem = "e" + q
            count[sem] = count.get(sem, 0) + 1
            ins.then_inc(T.sem[sem], 1)
            tick[i] = (sem, count[sem])
    for sem, v in count.items():
        if max(know[q].get(sem, 0) for q in Q) < v or sem == "sent":
            g.sync.wait_ge(T.sem[sem], v)
